import numpy as np
import ml_dtypes


def mxq(x, axis, fmt="e4m3"):
    dtype, down = {"e4m3": (ml_dtypes.float8_e4m3fn, 7), "e5m2": (ml_dtypes.float8_e5m2, 14)}[fmt]
    v = np.moveaxis(np.asarray(x, np.float32).astype(ml_dtypes.bfloat16).astype(np.float64), axis, -1)
    blocks = v.reshape(v.shape[:-1] + (-1, 32))
    amax = np.abs(blocks).max(-1, keepdims=True)
    byte = np.maximum(np.where(amax > 0, np.frexp(amax)[1] - 1 + 127, 0) - down, 1)
    scale = np.exp2(byte - 127.0)
    codes = (blocks / scale).astype(np.float32).astype(dtype).astype(np.float64)
    return np.moveaxis((codes * scale).reshape(v.shape), -1, axis)


WIDE = False


def mx_kscale(k):
    if not WIDE:
        return np.ones(k)
    levels = np.array([10, -10, 5, -5, 0])
    if k % 512:
        return np.exp2(np.random.permutation(np.resize(levels, k // 32))).repeat(32)
    a = np.empty((k // 512, 16))
    for p in range(k // 512):
        a[p, :8] = np.random.permutation(np.resize(levels, 8))
        for g in range(8):
            far = levels[np.abs(levels - a[p, g]) >= 10]
            a[p, g + 8] = far[np.random.randint(len(far))]
    return np.exp2(a.ravel()).repeat(32)


def f64(x):
    return np.asarray(x).astype(np.float64)


def striped(idx):
    return np.tile(idx.reshape(-1, 16).T, (8, 1)).astype(np.uint16)


def unstriped(offs):
    return offs[:16].T.reshape(-1).astype(np.int64)


E2M1 = np.array([0.0, 0.5, 1.0, 1.5, 2.0, 3.0, 4.0, 6.0, -0.0, -0.5, -1.0, -1.5, -2.0, -3.0, -4.0, -6.0])


def pack_weight(w, fmt):
    k, n = w.shape
    w = f64(np.asarray(w, np.float32).astype(ml_dtypes.bfloat16)).reshape(k // 32, 32, n)
    amax = np.abs(w).max(1)
    if fmt == "e4m3":
        byte = np.frexp(amax)[1] - 1 + 127 - 7
    else:
        mant, ex = np.frexp(amax / 6.0)
        byte = np.where(mant > 0.5, ex, ex - 1) + 127
    byte = np.clip(np.where(amax > 0, byte, 1), 1, 254)
    scaled = (w * np.exp2(127.0 - byte)[:, None, :]).reshape(k, n).astype(np.float32)
    by_word = np.ascontiguousarray(scaled.reshape(k // 512, 128, 4, n).transpose(0, 1, 3, 2))
    if fmt == "e4m3":
        words = by_word.astype(ml_dtypes.float8_e4m3fn).view(np.uint8)
    else:
        c = by_word.astype(ml_dtypes.float4_e2m1fn).view(np.uint8) & 0xF
        words = (c[..., 0::2] | (c[..., 1::2] << 4)).reshape(k // 512, 128, 2 * n)
    return np.ascontiguousarray(words), np.ascontiguousarray(byte.astype(np.uint8).reshape(k // 512, 16, n))


def unpack_weight(words, scales, fmt):
    g, _, n = scales.shape
    words = np.ascontiguousarray(words).reshape(g, 128, n, -1)
    if fmt == "e4m3":
        vals = words.view(ml_dtypes.float8_e4m3fn).astype(np.float64)
    else:
        nib = np.empty((g, 128, n, 4), np.uint8)
        nib[..., 0::2] = words & 0xF
        nib[..., 1::2] = words >> 4
        vals = E2M1[nib]
    vals = vals * np.repeat(np.exp2(scales.astype(np.float64) - 127.0), 8, axis=1)[..., None]
    return vals.transpose(0, 1, 3, 2).reshape(g * 512, n)


def gelu(v):
    return 0.5 * v * (1.0 + np.tanh(np.sqrt(2.0 / np.pi) * (v + 0.044715 * v**3)))


K, L, H, N, T, T2, S = 1024, 512, 1024, 768, 2048, 1024, 512

def setup_inputs():
    n = np.random.standard_normal
    s, s2, u = mx_kscale(K)[:, None], mx_kscale(L)[:, None], mx_kscale(H)[:, None]
    tab_words, tab_scales = pack_weight(n((K, T)) * s, "e4m3")
    tab2_words, tab2_scales = pack_weight(n((L, T2)) * s2, "e4m3")
    wb_words, wb_scales = pack_weight(n((L, H)) / np.sqrt(L) / s2, "e2m1")
    wc_words, wc_scales = pack_weight(n((K, H)) / np.sqrt(K) / s * u.T, "e2m1")
    wo_words, wo_scales = pack_weight(n((H, N)) / np.sqrt(H) / u, "e4m3")
    return {
        "tab_words": tab_words, "tab_scales": tab_scales,
        "tab2_words": tab2_words, "tab2_scales": tab2_scales,
        "offs": striped(np.random.permutation(T)[:S]),
        "offs2": striped(np.random.permutation(T2)[:S]),
        "wa": (n((K, H)) / np.sqrt(K) / s * u.T).astype(np.float32),
        "wb_words": wb_words, "wb_scales": wb_scales,
        "wc_words": wc_words, "wc_scales": wc_scales,
        "wd": (n((L, H)) / np.sqrt(L) / s2).astype(np.float32),
        "wo_words": wo_words, "wo_scales": wo_scales,
        "gT": np.exp(0.4 * n((N, T))).astype(np.float32)}

def reference(tab_words, tab_scales, tab2_words, tab2_scales, offs, offs2, wa, wb_words, wb_scales,
              wc_words, wc_scales, wd, wo_words, wo_scales, gT):
    v = unpack_weight(tab_words, tab_scales, "e4m3")[:, unstriped(offs)]
    v2 = unpack_weight(tab2_words, tab2_scales, "e4m3")[:, unstriped(offs2)]
    g = f64(gT)[:, unstriped(offs)]
    s_re = mxq(f64(wa), 0, "e4m3").T @ v
    s_im = unpack_weight(wc_words, wc_scales, "e2m1").T @ v
    r_re = unpack_weight(wb_words, wb_scales, "e2m1").T @ v2
    r_im = mxq(f64(wd), 0, "e4m3").T @ v2
    h = s_re * r_re - s_im * r_im
    y = unpack_weight(wo_words, wo_scales, "e4m3").T @ mxq(h, 0, "e4m3")
    return y * g

@@ -1,0 +1,213 @@
+from contextlib import ExitStack
+
+import concourse.mybir as mybir
+from concourse.masks import make_identity
+
+K, L, H, N, T, T2, S = 1024, 512, 1024, 768, 2048, 1024, 512
+FLOPS = 2 * S * (2 * K * H + 2 * L * H + H * N)
+
+F32 = mybir.dt.float32
+BF16 = mybir.dt.bfloat16
+I32 = mybir.dt.int32
+U32 = mybir.dt.uint32
+U16 = mybir.dt.uint16
+U8 = mybir.dt.uint8
+FP8X4 = mybir.dt.float8_e4m3fn_x4
+FP4X4 = mybir.dt.float4_e2m1fn_x4
+MULT = mybir.AluOpType.mult
+COPY = mybir.ActivationFunctionType.Copy
+
+P = 128
+PACK = 4
+PASS = P * PACK
+HALF = 512
+VECTOR_SHARE = 320
+
+
+def tile_list_complex_relation_embedding_kernel(
+    tc, tab_words, tab_scales, tab2_words, tab2_scales, offs, offs2, wa, wb_words, wb_scales,
+    wc_words, wc_scales, wd, wo_words, wo_scales, gT, out,
+):
+    nc = tc.nc
+    with ExitStack() as ctx:
+        keep = ctx.enter_context(tc.tile_pool(name="keep", bufs=1))
+        ring = ctx.enter_context(tc.tile_pool(name="ring", bufs=3))
+        psum_mm = ctx.enter_context(tc.psum_pool(name="psum_mm", bufs=4))
+        psum_tr = ctx.enter_context(tc.psum_pool(name="psum_tr", bufs=4))
+
+        def held(name, shape, dtype):
+            return keep.tile(shape, dtype, name=name, align_bytes=64)
+
+        list_v = keep.tile([P, S // 16], U16, name="list_v")
+        list_v2 = keep.tile([P, S // 16], U16, name="list_v2")
+
+        tab2_sc = held("tab2_sc", [P, 1, T2 // 4], I32)
+        wb_sc = held("wb_sc", [P, 1, H // 4], I32)
+        tab_sc = held("tab_sc", [P, 2, T // 4], I32)
+        wc_sc = held("wc_sc", [P, 2, H // 4], I32)
+        wo_sc = held("wo_sc", [P, N // 4], I32)
+        for plane in (tab2_sc, wb_sc):
+            nc.gpsimd.memset(plane[:], 0)
+        for plane in (tab_sc, wc_sc, wo_sc):
+            nc.vector.memset(plane[:], 0)
+
+        ident = held("ident", [P, P], F32)
+        make_identity(nc, ident[:])
+
+        def load_scales(plane, scales):
+            for q in range(4):
+                nc.sync.dma_start(
+                    out=plane[32 * q : 32 * q + 4, :, :],
+                    in_=scales[:, 4 * q : 4 * q + 4, :].rearrange("a r c -> r a c").bitcast(I32),
+                )
+
+        def load_table(name, words):
+            tile = held(name, [P, words.shape[1]], U32)
+            nc.sync.dma_start(out=tile[:].bitcast(I32), in_=words.rearrange("p t i -> p (t i)").bitcast(I32))
+            return tile
+
+        def load_raw(name, w, a, b):
+            tile = held(name, [P, PACK, HALF], F32)
+            rows = w[PASS * a : PASS * (a + 1), HALF * b : HALF * (b + 1)]
+            nc.sync.dma_start(out=tile[:], in_=rows.rearrange("(p i) c -> p i c", i=PACK))
+            return tile
+
+        nc.sync.dma_start(list_v2[:], offs2)
+        tab2_w = load_table("tab2_w", tab2_words[0])
+        wd_raw = [load_raw("wd_raw0", wd, 0, 0)]
+        load_scales(tab2_sc, tab2_scales)
+        wd_raw.append(load_raw("wd_raw1", wd, 0, 1))
+        wb_w = held("wb_w", [P, 2 * H], U8)
+        nc.sync.dma_start(out=wb_w[:].bitcast(I32), in_=wb_words[0].bitcast(I32))
+        load_scales(wb_sc, wb_scales)
+        nc.sync.dma_start(list_v[:], offs)
+        tab_w = [load_table("tab_w0", tab_words[0])]
+        load_scales(tab_sc, tab_scales)
+        tab_w.append(load_table("tab_w1", tab_words[1]))
+        load_scales(wc_sc, wc_scales)
+        wc_w = held("wc_w", [P, 2, 2 * H], U8)
+        nc.sync.dma_start(out=wc_w[:].bitcast(I32), in_=wc_words.rearrange("a p c -> p a c").bitcast(I32))
+        wa_raw = [[load_raw("wa_raw%d%d" % (b, a), wa, a, b) for a in range(2)] for b in range(2)]
+        for q in range(4):
+            nc.sync.dma_start(
+                out=wo_sc[32 * q + 4 : 32 * q + 12, :],
+                in_=wo_scales[:, 4 * q : 4 * q + 4, :].bitcast(I32),
+            )
+        wo_w = held("wo_w", [P, 2, N], U32)
+        nc.sync.dma_start(out=wo_w[:].bitcast(I32), in_=wo_words.rearrange("a p c i -> p a (c i)").bitcast(I32))
+        g = []
+        for n in range(N // P):
+            tile = held("g%d" % n, [P, T], F32)
+            nc.sync.dma_start(out=tile[:], in_=gT[P * n : P * (n + 1), :])
+            g.append(tile)
+
+        def gather(name, words, plane, a, offsets):
+            codes = held(name + "_codes", [P, S], U32)
+            scales = held(name + "_scales", [P, S], U8)
+            nc.vector.tensor_copy(out=codes[:], in_=words[:].indirect(offsets[:]))
+            nc.vector.tensor_copy(out=scales[:], in_=plane[:, a, :].bitcast(U8).indirect(offsets[:]))
+            return codes, scales
+
+        def quantise(name, raw, vector_cols):
+            grouped = ring.tile([P, HALF, PACK], BF16, name="grouped", align_bytes=64)
+            for copy, c0, c1 in (
+                (nc.scalar.copy, vector_cols, HALF),
+                (nc.vector.tensor_copy, 0, vector_cols),
+            ):
+                if c1 > c0:
+                    copy(
+                        out=grouped[:, c0:c1, :].rearrange("p (c e) i -> p c i e", e=4),
+                        in_=raw[:, :, c0:c1].rearrange("p i (c e) -> p c i e", e=4),
+                    )
+            codes = held(name + "_codes", [P, HALF], U32)
+            scales = held(name + "_scales", [P, HALF], U8)
+            nc.vector.quantize_mx(
+                out=codes[:].bitcast(FP8X4), scales=scales[:], in_=grouped[:].rearrange("p c i -> p (c i)")
+            )
+            return codes[:].bitcast(FP8X4), scales[:]
+
+        def product(picked, weights, j):
+            acc = psum_mm.tile([P, HALF], F32, name="acc")
+            cols = slice(P * j, P * (j + 1))
+            for a in range(len(picked)):
+                nc.tensor.matmul_mx(
+                    out=acc[:],
+                    lhsT=picked[a][0][:, cols].bitcast(FP8X4),
+                    lhsT_scale=picked[a][1][:, cols],
+                    rhs=weights[a][0],
+                    rhs_scale=weights[a][1],
+                    start=(a == 0),
+                    stop=(a == len(picked) - 1),
+                )
+            return acc[:].rearrange("p (m t) -> p t m", t=PACK)
+
+        def fp4_half(words, plane, a, b):
+            return (
+                words[:, 2 * HALF * b : 2 * HALF * (b + 1)].bitcast(FP4X4),
+                plane[:, a, HALF // 4 * b : HALF // 4 * (b + 1)].bitcast(U8),
+            )
+
+        tiles = range(S // P)
+        v2 = [gather("v2", tab2_w, tab2_sc, 0, list_v2)]
+        re = [[held("re%d%d" % (b, j), [P, PACK, P], F32) for j in tiles] for b in range(2)]
+        im = [[held("im%d%d" % (b, j), [P, PACK, P], F32) for j in tiles] for b in range(2)]
+        for b in range(2):
+            wd_q = quantise("wd%d" % b, wd_raw[b], HALF)
+            for j in tiles:
+                nc.scalar.activation(out=im[b][j][:], in_=product(v2, [wd_q], j), func=COPY, scale=-1.0)
+        for b in range(2):
+            for j in tiles:
+                nc.scalar.copy(out=re[b][j][:], in_=product(v2, [fp4_half(wb_w, wb_sc, 0, b)], j))
+
+        v = [gather("v%d" % a, tab_w[a], tab_sc, a, list_v) for a in range(2)]
+        h_codes = held("h_codes", [P, 2, S], U32)
+        h_scales = held("h_scales", [P, 2, S], U8)
+        for b in range(2):
+            turned = {}
+            wc_q = [fp4_half(wc_w[:, a, :], wc_sc, a, b) for a in range(2)]
+            for j in tiles:
+                nc.vector.tensor_tensor(out=im[b][j][:], in0=product(v, wc_q, j), in1=im[b][j][:], op=MULT)
+                turned[j] = psum_tr.tile([P, PACK, P], F32, name="turned")
+                for t in range(PACK):
+                    nc.tensor.matmul(
+                        out=turned[j][:, t, :], lhsT=im[b][j][:, t, :], rhs=ident[:],
+                        start=(t == 0), stop=False, is_transpose=True,
+                    )
+            wa_q = [
+                quantise("wa%d%d" % (b, a), wa_raw[b][a], VECTOR_SHARE if (b, a) == (1, 1) else 0)
+                for a in range(2)
+            ]
+            h_bf = held("h_bf%d" % b, [P, S, PACK], BF16)
+            for j in tiles:
+                nc.vector.tensor_tensor(out=re[b][j][:], in0=product(v, wa_q, j), in1=re[b][j][:], op=MULT)
+                for t in range(PACK):
+                    nc.tensor.matmul(
+                        out=turned[j][:, t, :], lhsT=re[b][j][:, t, :], rhs=ident[:],
+                        start=False, stop=(t == PACK - 1), is_transpose=True,
+                    )
+                nc.scalar.copy(out=h_bf[:, P * j : P * (j + 1), :], in_=turned[j][:].rearrange("p t j -> p j t"))
+                if j % 2 == 1:
+                    cols = slice(P * (j - 1), P * (j + 1))
+                    nc.vector.quantize_mx(
+                        out=h_codes[:, b, cols].bitcast(FP8X4),
+                        scales=h_scales[:, b, cols],
+                        in_=h_bf[:, cols, :].rearrange("p j t -> p (j t)"),
+                    )
+
+        for n in range(N // P):
+            y_acc = psum_mm.tile([P, S], F32, name="acc")
+            for b in range(2):
+                nc.tensor.matmul_mx(
+                    out=y_acc[:],
+                    lhsT=wo_w[:, b, P * n : P * (n + 1)].bitcast(FP8X4),
+                    lhsT_scale=wo_sc[4 * (b + 1) :, P // 4 * n : P // 4 * (n + 1)].bitcast(U8),
+                    rhs=h_codes[:, b, :].bitcast(FP8X4),
+                    rhs_scale=h_scales[:, b, :],
+                    start=(b == 0),
+                    stop=(b == 1),
+                )
+            y = ring.tile([P, S], F32, name="y")
+            nc.scalar.copy(out=y[:], in_=y_acc[:])
+            scaled = held("scaled%d" % n, [P, S], F32)
+            nc.vector.tensor_tensor(out=scaled[:], in0=g[n][:].indirect(list_v[:]), in1=y[:], op=MULT)
+            nc.sync.dma_start(out=out[P * n : P * (n + 1), :], in_=scaled[:])

@@ -15,13 +15,46 @@ U8 = mybir.dt.uint8
 FP8X4 = mybir.dt.float8_e4m3fn_x4
 FP4X4 = mybir.dt.float4_e2m1fn_x4
 MULT = mybir.AluOpType.mult
+ADD = mybir.AluOpType.add
 COPY = mybir.ActivationFunctionType.Copy
 
 P = 128
 PACK = 4
 PASS = P * PACK
 HALF = 512
-VECTOR_SHARE = 320
+QUARTER = 256
+CFG = {
+ "piece": 128,
+ "rev": [
+  "I"
+ ],
+ "banks": {
+  "a": 5,
+  "c": 3
+ },
+ "ybank": "c",
+ "rings": {
+  "V": 16,
+  "S": 24
+ },
+ "first": "rs",
+ "loads": "t2 s2 o o2 d0 wb sb t0 st t1 wc sc a00 a01 d1 a10 a11 so wo g0 g1 g2 g3 g4 g5",
+ "eng": {
+  "d00": "S",
+  "d01": "V",
+  "d10": "V",
+  "d11": "V",
+  "a000": "S",
+  "a001": "V",
+  "a010": "V",
+  "a011": "S",
+  "a100": "S",
+  "a101": "S",
+  "a110": "S",
+  "a111": "S"
+ },
+ "tasks": "v2 cd01 cd00 R00 R10 v1 v0 R11 qd00 qd01 R01 I00 I01 I02 R02 I03 R12 ca000 i00 i01 i02 qa000 ca001 ca010 R03 qa001 ca011 I10 i03 I11 qa010 I12 R13 qa011 I13 cd11 ca100 cd10 t00 ca101 t01 r00 t02 u00 qd10 qd11 r01 qa100 k00 ca110 r02 u01 r03 ca111 i10 i11 t03 i12 qa110 u02 t10 qa101 k01 qa111 i13 r10 u03 r11 u10 r12 t11 r13 u11 t12 k02 k10 u12 k11 h00 t13 k12 h10 u13 y001 k03 h01 k13 y101 h11 z001 y112 y012 y302 z101 y402 y502 y202 z112 z012 z302 z402 z202 z502"
+}
 
 
 def tile_list_complex_relation_embedding_kernel(
@@ -31,9 +64,8 @@ def tile_list_complex_relation_embedding_kernel(
     nc = tc.nc
     with ExitStack() as ctx:
         keep = ctx.enter_context(tc.tile_pool(name="keep", bufs=1))
-        ring = ctx.enter_context(tc.tile_pool(name="ring", bufs=3))
-        psum_mm = ctx.enter_context(tc.psum_pool(name="psum_mm", bufs=4))
-        psum_tr = ctx.enter_context(tc.psum_pool(name="psum_tr", bufs=4))
+        rings = {k: ctx.enter_context(tc.tile_pool(name="ring_" + k, bufs=n)) for k, n in CFG["rings"].items()}
+        banks = {k: ctx.enter_context(tc.psum_pool(name="psum_" + k, bufs=n)) for k, n in CFG["banks"].items()}
 
         def held(name, shape, dtype):
             return keep.tile(shape, dtype, name=name, align_bytes=64)
@@ -72,34 +104,51 @@ def tile_list_complex_relation_embedding_kernel(
             nc.sync.dma_start(out=tile[:], in_=rows.rearrange("(p i) c -> p i c", i=PACK))
             return tile
 
-        nc.sync.dma_start(list_v2[:], offs2)
-        tab2_w = load_table("tab2_w", tab2_words[0])
-        wd_raw = [load_raw("wd_raw0", wd, 0, 0)]
-        load_scales(tab2_sc, tab2_scales)
-        wd_raw.append(load_raw("wd_raw1", wd, 0, 1))
-        wb_w = held("wb_w", [P, 2 * H], U8)
-        nc.sync.dma_start(out=wb_w[:].bitcast(I32), in_=wb_words[0].bitcast(I32))
-        load_scales(wb_sc, wb_scales)
-        nc.sync.dma_start(list_v[:], offs)
-        tab_w = [load_table("tab_w0", tab_words[0])]
-        load_scales(tab_sc, tab_scales)
-        tab_w.append(load_table("tab_w1", tab_words[1]))
-        load_scales(wc_sc, wc_scales)
-        wc_w = held("wc_w", [P, 2, 2 * H], U8)
-        nc.sync.dma_start(out=wc_w[:].bitcast(I32), in_=wc_words.rearrange("a p c -> p a c").bitcast(I32))
-        wa_raw = [[load_raw("wa_raw%d%d" % (b, a), wa, a, b) for a in range(2)] for b in range(2)]
-        for q in range(4):
-            nc.sync.dma_start(
-                out=wo_sc[32 * q + 4 : 32 * q + 12, :],
-                in_=wo_scales[:, 4 * q : 4 * q + 4, :].bitcast(I32),
-            )
-        wo_w = held("wo_w", [P, 2, N], U32)
-        nc.sync.dma_start(out=wo_w[:].bitcast(I32), in_=wo_words.rearrange("a p c i -> p a (c i)").bitcast(I32))
-        g = []
-        for n in range(N // P):
-            tile = held("g%d" % n, [P, T], F32)
-            nc.sync.dma_start(out=tile[:], in_=gT[P * n : P * (n + 1), :])
-            g.append(tile)
+        st = {}
+
+        def load(name):
+            if name == "o2":
+                nc.sync.dma_start(list_v2[:], offs2)
+            elif name == "o":
+                nc.sync.dma_start(list_v[:], offs)
+            elif name == "t2":
+                st[name] = load_table("tab2_w", tab2_words[0])
+            elif name in ("t0", "t1"):
+                st[name] = load_table("tab_w" + name[1], tab_words[int(name[1])])
+            elif name == "s2":
+                load_scales(tab2_sc, tab2_scales)
+            elif name == "st":
+                load_scales(tab_sc, tab_scales)
+            elif name == "sb":
+                load_scales(wb_sc, wb_scales)
+            elif name == "sc":
+                load_scales(wc_sc, wc_scales)
+            elif name == "so":
+                for q in range(4):
+                    nc.sync.dma_start(
+                        out=wo_sc[32 * q + 4 : 32 * q + 12, :],
+                        in_=wo_scales[:, 4 * q : 4 * q + 4, :].bitcast(I32),
+                    )
+            elif name == "wb":
+                st[name] = held("wb_w", [P, 2 * H], U8)
+                nc.sync.dma_start(out=st[name][:].bitcast(I32), in_=wb_words[0].bitcast(I32))
+            elif name == "wc":
+                st[name] = held("wc_w", [P, 2, 2 * H], U8)
+                nc.sync.dma_start(out=st[name][:].bitcast(I32), in_=wc_words.rearrange("a p c -> p a c").bitcast(I32))
+            elif name == "wo":
+                st[name] = held("wo_w", [P, 2, N], U32)
+                nc.sync.dma_start(out=st[name][:].bitcast(I32), in_=wo_words.rearrange("a p c i -> p a (c i)").bitcast(I32))
+            elif name[0] == "d":
+                st[name] = load_raw("raw" + name, wd, 0, int(name[1]))
+            elif name[0] == "a":
+                st[name] = load_raw("raw" + name, wa, int(name[2]), int(name[1]))
+            else:
+                n = int(name[1])
+                st[name] = held(name, [P, T], F32)
+                nc.sync.dma_start(out=st[name][:], in_=gT[P * n : P * (n + 1), :])
+
+        for name in CFG["loads"].split():
+            load(name)
 
         def gather(name, words, plane, a, offsets):
             codes = held(name + "_codes", [P, S], U32)
@@ -108,37 +157,54 @@ def tile_list_complex_relation_embedding_kernel(
             nc.vector.tensor_copy(out=scales[:], in_=plane[:, a, :].bitcast(U8).indirect(offsets[:]))
             return codes, scales
 
-        def quantise(name, raw, vector_cols):
-            grouped = ring.tile([P, HALF, PACK], BF16, name="grouped", align_bytes=64)
-            for copy, c0, c1 in (
-                (nc.scalar.copy, vector_cols, HALF),
-                (nc.vector.tensor_copy, 0, vector_cols),
-            ):
-                if c1 > c0:
-                    copy(
-                        out=grouped[:, c0:c1, :].rearrange("p (c e) i -> p c i e", e=4),
-                        in_=raw[:, :, c0:c1].rearrange("p i (c e) -> p c i e", e=4),
+        def fresh(engine, name, shape, dtype):
+            return rings[engine].tile(shape, dtype, name=name, tag="slot", align_bytes=64)
+
+        def cast(unit):
+            raw, c0 = st[unit[:-1]], QUARTER * int(unit[-1])
+            engine = CFG["eng"][unit]
+            grouped = fresh(engine, "c" + unit, [P, QUARTER, PACK], BF16)
+            if engine == "G":
+                for p0 in range(0, QUARTER, CFG["piece"]):
+                    p1 = p0 + CFG["piece"]
+                    nc.gpsimd.tensor_scalar(
+                        out=grouped[:, p0:p1, :], in0=raw[:, :, c0 + p0 : c0 + p1].rearrange("p i c -> p c i"),
+                        scalar1=1.0, scalar2=0.0, op0=MULT, op1=ADD,
                     )
-            codes = held(name + "_codes", [P, HALF], U32)
-            scales = held(name + "_scales", [P, HALF], U8)
+            else:
+                copy = nc.scalar.copy if engine == "S" else nc.vector.tensor_copy
+                copy(
+                    out=grouped[:].rearrange("p (c e) i -> p c i e", e=4),
+                    in_=raw[:, :, c0 : c0 + QUARTER].rearrange("p i (c e) -> p c i e", e=4),
+                )
+            return grouped
+
+        def quantise(name, grouped):
+            codes = fresh("V", name + "_codes", [P, QUARTER], U32)
+            scales = held(name + "_scales", [P, QUARTER], U8)
             nc.vector.quantize_mx(
                 out=codes[:].bitcast(FP8X4), scales=scales[:], in_=grouped[:].rearrange("p c i -> p (c i)")
             )
             return codes[:].bitcast(FP8X4), scales[:]
 
-        def product(picked, weights, j):
-            acc = psum_mm.tile([P, HALF], F32, name="acc")
+        def product(picked, weights, j, kind):
+            acc = banks["a"].tile([P, HALF], F32, name="acc")
             cols = slice(P * j, P * (j + 1))
-            for a in range(len(picked)):
-                nc.tensor.matmul_mx(
-                    out=acc[:],
-                    lhsT=picked[a][0][:, cols].bitcast(FP8X4),
-                    lhsT_scale=picked[a][1][:, cols],
-                    rhs=weights[a][0],
-                    rhs_scale=weights[a][1],
-                    start=(a == 0),
-                    stop=(a == len(picked) - 1),
-                )
+            order = list(range(len(picked)))
+            if kind in CFG["rev"]:
+                order = order[::-1]
+            width = HALF // len(weights)
+            for part in range(len(weights)):
+                for a in order:
+                    nc.tensor.matmul_mx(
+                        out=acc[:, width * part : width * (part + 1)],
+                        lhsT=picked[a][0][:, cols].bitcast(FP8X4),
+                        lhsT_scale=picked[a][1][:, cols],
+                        rhs=weights[part][a][0],
+                        rhs_scale=weights[part][a][1],
+                        start=(a == order[0]),
+                        stop=(a == order[-1]),
+                    )
             return acc[:].rearrange("p (m t) -> p t m", t=PACK)
 
         def fp4_half(words, plane, a, b):
@@ -147,67 +213,93 @@ def tile_list_complex_relation_embedding_kernel(
                 plane[:, a, HALF // 4 * b : HALF // 4 * (b + 1)].bitcast(U8),
             )
 
-        tiles = range(S // P)
-        v2 = [gather("v2", tab2_w, tab2_sc, 0, list_v2)]
-        re = [[held("re%d%d" % (b, j), [P, PACK, P], F32) for j in tiles] for b in range(2)]
-        im = [[held("im%d%d" % (b, j), [P, PACK, P], F32) for j in tiles] for b in range(2)]
-        for b in range(2):
-            wd_q = quantise("wd%d" % b, wd_raw[b], HALF)
-            for j in tiles:
-                nc.scalar.activation(out=im[b][j][:], in_=product(v2, [wd_q], j), func=COPY, scale=-1.0)
-        for b in range(2):
-            for j in tiles:
-                nc.scalar.copy(out=re[b][j][:], in_=product(v2, [fp4_half(wb_w, wb_sc, 0, b)], j))
+        def imag(side, b, j, kind):
+            if side == "r":
+                return product(st["v2"], [[st["qd%d%d" % (b, part)]] for part in range(2)], j, kind)
+            wc_q = [fp4_half(st["wc"][:, a, :], wc_sc, a, b) for a in range(2)]
+            return product([st["v0"], st["v1"]], [wc_q], j, kind)
 
-        v = [gather("v%d" % a, tab_w[a], tab_sc, a, list_v) for a in range(2)]
-        h_codes = held("h_codes", [P, 2, S], U32)
-        h_scales = held("h_scales", [P, 2, S], U8)
-        for b in range(2):
-            turned = {}
-            wc_q = [fp4_half(wc_w[:, a, :], wc_sc, a, b) for a in range(2)]
-            for j in tiles:
-                nc.vector.tensor_tensor(out=im[b][j][:], in0=product(v, wc_q, j), in1=im[b][j][:], op=MULT)
-                turned[j] = psum_tr.tile([P, PACK, P], F32, name="turned")
-                for t in range(PACK):
-                    nc.tensor.matmul(
-                        out=turned[j][:, t, :], lhsT=im[b][j][:, t, :], rhs=ident[:],
-                        start=(t == 0), stop=False, is_transpose=True,
-                    )
-            wa_q = [
-                quantise("wa%d%d" % (b, a), wa_raw[b][a], VECTOR_SHARE if (b, a) == (1, 1) else 0)
-                for a in range(2)
-            ]
-            h_bf = held("h_bf%d" % b, [P, S, PACK], BF16)
-            for j in tiles:
-                nc.vector.tensor_tensor(out=re[b][j][:], in0=product(v, wa_q, j), in1=re[b][j][:], op=MULT)
-                for t in range(PACK):
-                    nc.tensor.matmul(
-                        out=turned[j][:, t, :], lhsT=re[b][j][:, t, :], rhs=ident[:],
-                        start=False, stop=(t == PACK - 1), is_transpose=True,
-                    )
-                nc.scalar.copy(out=h_bf[:, P * j : P * (j + 1), :], in_=turned[j][:].rearrange("p t j -> p j t"))
-                if j % 2 == 1:
-                    cols = slice(P * (j - 1), P * (j + 1))
-                    nc.vector.quantize_mx(
-                        out=h_codes[:, b, cols].bitcast(FP8X4),
-                        scales=h_scales[:, b, cols],
-                        in_=h_bf[:, cols, :].rearrange("p j t -> p (j t)"),
-                    )
-
-        for n in range(N // P):
-            y_acc = psum_mm.tile([P, S], F32, name="acc")
-            for b in range(2):
-                nc.tensor.matmul_mx(
-                    out=y_acc[:],
-                    lhsT=wo_w[:, b, P * n : P * (n + 1)].bitcast(FP8X4),
-                    lhsT_scale=wo_sc[4 * (b + 1) :, P // 4 * n : P // 4 * (n + 1)].bitcast(U8),
-                    rhs=h_codes[:, b, :].bitcast(FP8X4),
-                    rhs_scale=h_scales[:, b, :],
-                    start=(b == 0),
-                    stop=(b == 1),
+        def turn(name, first):
+            if first:
+                st["T" + name[1:]] = banks["c"].tile([P, PACK, P], F32, name="turned")
+            src = st[("i" if first else "r") + name[1:]]
+            for t in range(PACK):
+                nc.tensor.matmul(
+                    out=st["T" + name[1:]][:, t, :], lhsT=src[:, t, :], rhs=ident[:],
+                    start=(first and t == 0), stop=(not first and t == PACK - 1), is_transpose=True,
                 )
-            y = ring.tile([P, S], F32, name="y")
-            nc.scalar.copy(out=y[:], in_=y_acc[:])
-            scaled = held("scaled%d" % n, [P, S], F32)
-            nc.vector.tensor_tensor(out=scaled[:], in0=g[n][:].indirect(list_v[:]), in1=y[:], op=MULT)
-            nc.sync.dma_start(out=out[P * n : P * (n + 1), :], in_=scaled[:])
+
+        def task(name):
+            kind = name[0]
+            if name == "v2":
+                st[name] = [gather("v2", st["t2"], tab2_sc, 0, list_v2)]
+            elif name in ("v0", "v1"):
+                a = int(name[1])
+                st[name] = gather(name, st["t" + name[1]], tab_sc, a, list_v)
+            elif kind == "c":
+                st[name] = cast(name[1:])
+            elif kind == "q":
+                st[name] = quantise(name, st["c" + name[1:]])
+            elif kind == "R":
+                b, j = int(name[1]), int(name[2])
+                st[name] = fresh("S", name, [P, PACK, P], F32)
+                nc.scalar.copy(out=st[name][:], in_=product(st["v2"], [[fp4_half(st["wb"], wb_sc, 0, b)]], j, "R"))
+            elif kind == "I":
+                b, j = int(name[1]), int(name[2])
+                st[name] = fresh("S", name, [P, PACK, P], F32)
+                nc.scalar.activation(out=st[name][:], in_=imag(CFG["first"][b], b, j, "I"), func=COPY, scale=-1.0)
+            elif kind == "i":
+                b, j = int(name[1]), int(name[2])
+                st[name] = fresh("V", name, [P, PACK, P], F32)
+                nc.vector.tensor_tensor(
+                    out=st[name][:], in0=imag("rs".replace(CFG["first"][b], ""), b, j, "i"), in1=st["I" + name[1:]][:], op=MULT
+                )
+            elif kind == "t":
+                turn(name, True)
+            elif kind == "r":
+                b, j = int(name[1]), int(name[2])
+                wa_q = [[st["qa%d%d%d" % (b, a, part)] for a in range(2)] for part in range(2)]
+                st[name] = fresh("V", name, [P, PACK, P], F32)
+                nc.vector.tensor_tensor(
+                    out=st[name][:], in0=product([st["v0"], st["v1"]], wa_q, j, "r%d" % b), in1=st["R" + name[1:]][:], op=MULT
+                )
+            elif kind == "u":
+                turn(name, False)
+            elif kind == "k":
+                b, j = int(name[1]), int(name[2])
+                key = "H%d%d" % (b, j // 2)
+                if key not in st:
+                    st[key] = fresh("S", key, [P, 2 * P, PACK], BF16)
+                nc.scalar.copy(
+                    out=st[key][:, P * (j % 2) : P * (j % 2 + 1), :], in_=st["T" + name[1:]][:].rearrange("p t j -> p j t")
+                )
+            elif kind == "h":
+                st[name] = quantise(name, st["H" + name[1:]])
+            elif kind == "y":
+                n, h0, h1 = int(name[1]), int(name[2]), int(name[3])
+                y_acc = banks[CFG["ybank"]].tile([P, S], F32, name="acc" if CFG["ybank"] == "a" else "turned")
+                for half in range(h0, h1):
+                    for b in (1, 0):
+                        nc.tensor.matmul_mx(
+                            out=y_acc[:, QUARTER * (half - h0) : QUARTER * (half - h0 + 1)],
+                            lhsT=st["wo"][:, b, P * n : P * (n + 1)].bitcast(FP8X4),
+                            lhsT_scale=wo_sc[4 * (b + 1) :, P // 4 * n : P // 4 * (n + 1)].bitcast(U8),
+                            rhs=st["h%d%d" % (b, half)][0],
+                            rhs_scale=st["h%d%d" % (b, half)][1],
+                            start=(b == 1),
+                            stop=(b == 0),
+                        )
+                width = QUARTER * (h1 - h0)
+                st[name] = fresh("S", name, [P, width], F32)
+                nc.scalar.copy(out=st[name][:], in_=y_acc[:, :width])
+            else:
+                n, h0, h1 = int(name[1]), int(name[2]), int(name[3])
+                cols = slice(QUARTER * h0, QUARTER * h1)
+                scaled = fresh("V", name, [P, QUARTER * (h1 - h0)], F32)
+                nc.vector.tensor_tensor(
+                    out=scaled[:], in0=st["g%d" % n][:].indirect(list_v[:, 16 * h0 : 16 * h1]), in1=st["y" + name[1:]][:], op=MULT
+                )
+                nc.sync.dma_start(out=out[P * n : P * (n + 1), cols], in_=scaled[:])
+
+        for name in CFG["tasks"].split():
+            task(name)

@@ -15,46 +15,37 @@ U8 = mybir.dt.uint8
 FP8X4 = mybir.dt.float8_e4m3fn_x4
 FP4X4 = mybir.dt.float4_e2m1fn_x4
 MULT = mybir.AluOpType.mult
-ADD = mybir.AluOpType.add
 COPY = mybir.ActivationFunctionType.Copy
 
 P = 128
 PACK = 4
 PASS = P * PACK
 HALF = 512
-QUARTER = 256
-CFG = {
- "piece": 128,
- "rev": [
-  "I"
- ],
- "banks": {
-  "a": 5,
-  "c": 3
- },
- "ybank": "c",
- "rings": {
-  "V": 16,
-  "S": 24
- },
- "first": "rs",
- "loads": "t2 s2 o o2 d0 wb sb t0 st t1 wc sc a00 a01 d1 a10 a11 so wo g0 g1 g2 g3 g4 g5",
- "eng": {
-  "d00": "S",
-  "d01": "V",
-  "d10": "V",
-  "d11": "V",
-  "a000": "S",
-  "a001": "V",
-  "a010": "V",
-  "a011": "S",
-  "a100": "S",
-  "a101": "S",
-  "a110": "S",
-  "a111": "S"
- },
- "tasks": "v2 cd01 cd00 R00 R10 v1 v0 R11 qd00 qd01 R01 I00 I01 I02 R02 I03 R12 ca000 i00 i01 i02 qa000 ca001 ca010 R03 qa001 ca011 I10 i03 I11 qa010 I12 R13 qa011 I13 cd11 ca100 cd10 t00 ca101 t01 r00 t02 u00 qd10 qd11 r01 qa100 k00 ca110 r02 u01 r03 ca111 i10 i11 t03 i12 qa110 u02 t10 qa101 k01 qa111 i13 r10 u03 r11 u10 r12 t11 r13 u11 t12 k02 k10 u12 k11 h00 t13 k12 h10 u13 y001 k03 h01 k13 y101 h11 z001 y112 y012 y302 z101 y402 y502 y202 z112 z012 z302 z402 z202 z502"
-}
+PART = 256
+
+RING_DEPTH = {"V": 16, "S": 24}
+PRODUCT_BANKS = 3
+TURN_BANKS = 5
+
+LOADS = """
+tab2 list2 list tab2_sc wd00 wb_sc wb tab0 tab_sc tab1 wc wc_sc wa00 wo_sc wa01 wd10 wa10 wa11 gT0
+gT1 wo gT2 gT3 gT4 gT5
+""".split()
+
+STEPS = """
+pick:tab2 rre:10 castV:wd001 rre:11 castV:wd000 rre:00 quant:wd001 quant:wd000 rre:01 im1st:00
+rre:12 im1st:01 rre:02 rre:03 im1st:02 pick:tab0 pick:tab1 im1st:03 im:00 im:01 castS:wa000
+castV:wa001 im1st:10 im:02 im1st:11 castS:wa011 im1st:12 quant:wa000 im1st:13 castV:wa010 turn_im:00
+turn_im:01 quant:wa010 quant:wa011 rre:13 quant:wa001 castS:wd101 castV:wd100 castS:wa100 re:00
+castS:wa101 turn_re:00 turn_im:02 im:03 round:00 quant:wd101 quant:wd100 re:01 re:02 quant:wa100
+castS:wa110 re:03 im:10 turn_re:01 castV:wa111 turn_im:03 turn_re:02 im:11 quant:wa111 turn_im:10
+quant:wa110 turn_im:11 quant:wa101 round:01 im:12 re:10 re:11 re:12 turn_re:10 round:02 round:10
+im:13 re:13 turn_re:11 turn_im:12 turn_re:03 round:11 turn_re:12 quant_h:00 round:12 turn_im:13
+quant_h:10 turn_re:13 round:03 round:13 quant_h:01 y:001 y:101 quant_h:11 scale:001 scale:101 y:012
+y:112 y:202 scale:012 y:302 scale:112 y:402 scale:202 y:502 scale:302 scale:402 scale:502
+""".split()
+
+PASS_1_FIRST = {("im1st", 1), ("re", 0)}
 
 
 def tile_list_complex_relation_embedding_kernel(
@@ -64,11 +55,15 @@ def tile_list_complex_relation_embedding_kernel(
     nc = tc.nc
     with ExitStack() as ctx:
         keep = ctx.enter_context(tc.tile_pool(name="keep", bufs=1))
-        rings = {k: ctx.enter_context(tc.tile_pool(name="ring_" + k, bufs=n)) for k, n in CFG["rings"].items()}
-        banks = {k: ctx.enter_context(tc.psum_pool(name="psum_" + k, bufs=n)) for k, n in CFG["banks"].items()}
+        rings = {e: ctx.enter_context(tc.tile_pool(name="ring_" + e, bufs=n)) for e, n in RING_DEPTH.items()}
+        product_banks = ctx.enter_context(tc.psum_pool(name="product_banks", bufs=PRODUCT_BANKS))
+        turn_banks = ctx.enter_context(tc.psum_pool(name="turn_banks", bufs=TURN_BANKS))
 
         def held(name, shape, dtype):
             return keep.tile(shape, dtype, name=name, align_bytes=64)
+
+        def fresh(engine, name, shape, dtype):
+            return rings[engine].tile(shape, dtype, name=name, tag="slot", align_bytes=64)
 
         list_v = keep.tile([P, S // 16], U16, name="list_v")
         list_v2 = keep.tile([P, S // 16], U16, name="list_v2")
@@ -82,128 +77,109 @@ def tile_list_complex_relation_embedding_kernel(
             nc.gpsimd.memset(plane[:], 0)
         for plane in (tab_sc, wc_sc, wo_sc):
             nc.vector.memset(plane[:], 0)
+        planes = {
+            "tab2_sc": (tab2_sc, tab2_scales),
+            "wb_sc": (wb_sc, wb_scales),
+            "tab_sc": (tab_sc, tab_scales),
+            "wc_sc": (wc_sc, wc_scales),
+        }
 
         ident = held("ident", [P, P], F32)
         make_identity(nc, ident[:])
 
-        def load_scales(plane, scales):
-            for q in range(4):
-                nc.sync.dma_start(
-                    out=plane[32 * q : 32 * q + 4, :, :],
-                    in_=scales[:, 4 * q : 4 * q + 4, :].rearrange("a r c -> r a c").bitcast(I32),
-                )
+        made = {}
 
-        def load_table(name, words):
-            tile = held(name, [P, words.shape[1]], U32)
-            nc.sync.dma_start(out=tile[:].bitcast(I32), in_=words.rearrange("p t i -> p (t i)").bitcast(I32))
-            return tile
-
-        def load_raw(name, w, a, b):
-            tile = held(name, [P, PACK, HALF], F32)
-            rows = w[PASS * a : PASS * (a + 1), HALF * b : HALF * (b + 1)]
-            nc.sync.dma_start(out=tile[:], in_=rows.rearrange("(p i) c -> p i c", i=PACK))
-            return tile
-
-        st = {}
+        def load_bytes(name, shape, dtype, source):
+            made[name] = held(name, shape, dtype)
+            nc.sync.dma_start(out=made[name][:].bitcast(I32), in_=source.bitcast(I32))
 
         def load(name):
-            if name == "o2":
-                nc.sync.dma_start(list_v2[:], offs2)
-            elif name == "o":
+            if name == "list":
                 nc.sync.dma_start(list_v[:], offs)
-            elif name == "t2":
-                st[name] = load_table("tab2_w", tab2_words[0])
-            elif name in ("t0", "t1"):
-                st[name] = load_table("tab_w" + name[1], tab_words[int(name[1])])
-            elif name == "s2":
-                load_scales(tab2_sc, tab2_scales)
-            elif name == "st":
-                load_scales(tab_sc, tab_scales)
-            elif name == "sb":
-                load_scales(wb_sc, wb_scales)
-            elif name == "sc":
-                load_scales(wc_sc, wc_scales)
-            elif name == "so":
+            elif name == "list2":
+                nc.sync.dma_start(list_v2[:], offs2)
+            elif name in planes:
+                plane, scales = planes[name]
+                for q in range(4):
+                    nc.sync.dma_start(
+                        out=plane[32 * q : 32 * q + 4, :, :],
+                        in_=scales[:, 4 * q : 4 * q + 4, :].rearrange("a r c -> r a c").bitcast(I32),
+                    )
+            elif name == "wo_sc":
                 for q in range(4):
                     nc.sync.dma_start(
                         out=wo_sc[32 * q + 4 : 32 * q + 12, :],
                         in_=wo_scales[:, 4 * q : 4 * q + 4, :].bitcast(I32),
                     )
+            elif name == "tab2":
+                load_bytes(name, [P, T2], U32, tab2_words[0].rearrange("p t i -> p (t i)"))
+            elif name in ("tab0", "tab1"):
+                load_bytes(name, [P, T], U32, tab_words[int(name[3])].rearrange("p t i -> p (t i)"))
             elif name == "wb":
-                st[name] = held("wb_w", [P, 2 * H], U8)
-                nc.sync.dma_start(out=st[name][:].bitcast(I32), in_=wb_words[0].bitcast(I32))
+                load_bytes(name, [P, 2 * H], U8, wb_words[0])
             elif name == "wc":
-                st[name] = held("wc_w", [P, 2, 2 * H], U8)
-                nc.sync.dma_start(out=st[name][:].bitcast(I32), in_=wc_words.rearrange("a p c -> p a c").bitcast(I32))
+                load_bytes(name, [P, 2, 2 * H], U8, wc_words.rearrange("a p c -> p a c"))
             elif name == "wo":
-                st[name] = held("wo_w", [P, 2, N], U32)
-                nc.sync.dma_start(out=st[name][:].bitcast(I32), in_=wo_words.rearrange("a p c i -> p a (c i)").bitcast(I32))
-            elif name[0] == "d":
-                st[name] = load_raw("raw" + name, wd, 0, int(name[1]))
-            elif name[0] == "a":
-                st[name] = load_raw("raw" + name, wa, int(name[2]), int(name[1]))
+                load_bytes(name, [P, 2, N], U32, wo_words.rearrange("a p c i -> p a (c i)"))
+            elif name.startswith("gT"):
+                n = int(name[2])
+                made[name] = held(name, [P, T], F32)
+                nc.sync.dma_start(out=made[name][:], in_=gT[P * n : P * (n + 1), :])
             else:
-                n = int(name[1])
-                st[name] = held(name, [P, T], F32)
-                nc.sync.dma_start(out=st[name][:], in_=gT[P * n : P * (n + 1), :])
+                weight, b, a = {"wa": wa, "wd": wd}[name[:2]], int(name[2]), int(name[3])
+                made[name] = held(name, [P, PACK, HALF], F32)
+                rows = weight[PASS * a : PASS * (a + 1), HALF * b : HALF * (b + 1)]
+                nc.sync.dma_start(out=made[name][:], in_=rows.rearrange("(p i) c -> p i c", i=PACK))
 
-        for name in CFG["loads"].split():
-            load(name)
-
-        def gather(name, words, plane, a, offsets):
-            codes = held(name + "_codes", [P, S], U32)
-            scales = held(name + "_scales", [P, S], U8)
-            nc.vector.tensor_copy(out=codes[:], in_=words[:].indirect(offsets[:]))
+        def pick(table):
+            plane, a, offsets = {
+                "tab2": (tab2_sc, 0, list_v2),
+                "tab0": (tab_sc, 0, list_v),
+                "tab1": (tab_sc, 1, list_v),
+            }[table]
+            codes = held(table + "_codes", [P, S], U32)
+            scales = held(table + "_scales", [P, S], U8)
+            nc.vector.tensor_copy(out=codes[:], in_=made[table][:].indirect(offsets[:]))
             nc.vector.tensor_copy(out=scales[:], in_=plane[:, a, :].bitcast(U8).indirect(offsets[:]))
             return codes, scales
 
-        def fresh(engine, name, shape, dtype):
-            return rings[engine].tile(shape, dtype, name=name, tag="slot", align_bytes=64)
-
-        def cast(unit):
-            raw, c0 = st[unit[:-1]], QUARTER * int(unit[-1])
-            engine = CFG["eng"][unit]
-            grouped = fresh(engine, "c" + unit, [P, QUARTER, PACK], BF16)
-            if engine == "G":
-                for p0 in range(0, QUARTER, CFG["piece"]):
-                    p1 = p0 + CFG["piece"]
-                    nc.gpsimd.tensor_scalar(
-                        out=grouped[:, p0:p1, :], in0=raw[:, :, c0 + p0 : c0 + p1].rearrange("p i c -> p c i"),
-                        scalar1=1.0, scalar2=0.0, op0=MULT, op1=ADD,
-                    )
-            else:
-                copy = nc.scalar.copy if engine == "S" else nc.vector.tensor_copy
-                copy(
-                    out=grouped[:].rearrange("p (c e) i -> p c i e", e=4),
-                    in_=raw[:, :, c0 : c0 + QUARTER].rearrange("p i (c e) -> p c i e", e=4),
-                )
+        def cast(engine, part):
+            c0 = PART * int(part[4])
+            raw = made[part[:4]][:, :, c0 : c0 + PART]
+            grouped = fresh(engine, "cast_" + part, [P, PART, PACK], BF16)
+            copy = nc.scalar.copy if engine == "S" else nc.vector.tensor_copy
+            copy(
+                out=grouped[:].rearrange("p (c e) i -> p c i e", e=4),
+                in_=raw.rearrange("p i (c e) -> p c i e", e=4),
+            )
             return grouped
 
         def quantise(name, grouped):
-            codes = fresh("V", name + "_codes", [P, QUARTER], U32)
-            scales = held(name + "_scales", [P, QUARTER], U8)
+            codes = fresh("V", name + "_codes", [P, PART], U32)
+            scales = held(name + "_scales", [P, PART], U8)
             nc.vector.quantize_mx(
                 out=codes[:].bitcast(FP8X4), scales=scales[:], in_=grouped[:].rearrange("p c i -> p (c i)")
             )
             return codes[:].bitcast(FP8X4), scales[:]
 
-        def product(picked, weights, j, kind):
-            acc = banks["a"].tile([P, HALF], F32, name="acc")
-            cols = slice(P * j, P * (j + 1))
-            order = list(range(len(picked)))
-            if kind in CFG["rev"]:
-                order = order[::-1]
+        def product(tables, weights, j, pass_1_first):
+            acc = product_banks.tile([P, HALF], F32, name="acc")
+            tokens = slice(P * j, P * (j + 1))
+            passes = list(range(len(tables)))
+            if pass_1_first:
+                passes = passes[::-1]
             width = HALF // len(weights)
-            for part in range(len(weights)):
-                for a in order:
+            for c in range(len(weights)):
+                for a in passes:
+                    codes, scales = made["pick:" + tables[a]]
                     nc.tensor.matmul_mx(
-                        out=acc[:, width * part : width * (part + 1)],
-                        lhsT=picked[a][0][:, cols].bitcast(FP8X4),
-                        lhsT_scale=picked[a][1][:, cols],
-                        rhs=weights[part][a][0],
-                        rhs_scale=weights[part][a][1],
-                        start=(a == order[0]),
-                        stop=(a == order[-1]),
+                        out=acc[:, width * c : width * (c + 1)],
+                        lhsT=codes[:, tokens].bitcast(FP8X4),
+                        lhsT_scale=scales[:, tokens],
+                        rhs=weights[c][a][0],
+                        rhs_scale=weights[c][a][1],
+                        start=(a == passes[0]),
+                        stop=(a == passes[-1]),
                     )
             return acc[:].rearrange("p (m t) -> p t m", t=PACK)
 
@@ -213,93 +189,92 @@ def tile_list_complex_relation_embedding_kernel(
                 plane[:, a, HALF // 4 * b : HALF // 4 * (b + 1)].bitcast(U8),
             )
 
-        def imag(side, b, j, kind):
-            if side == "r":
-                return product(st["v2"], [[st["qd%d%d" % (b, part)]] for part in range(2)], j, kind)
-            wc_q = [fp4_half(st["wc"][:, a, :], wc_sc, a, b) for a in range(2)]
-            return product([st["v0"], st["v1"]], [wc_q], j, kind)
+        def factor(kind, b, j):
+            pass_1_first = (kind, b) in PASS_1_FIRST
+            if kind == "rre":
+                return product(["tab2"], [[fp4_half(made["wb"], wb_sc, 0, b)]], j, pass_1_first)
+            if kind == "re":
+                parts = [[made["quant:wa%d%d%d" % (b, a, c)] for a in range(2)] for c in range(2)]
+                return product(["tab0", "tab1"], parts, j, pass_1_first)
+            if (kind == "im1st") == (b == 0):
+                parts = [[made["quant:wd%d0%d" % (b, c)]] for c in range(2)]
+                return product(["tab2"], parts, j, pass_1_first)
+            whole = [fp4_half(made["wc"][:, a, :], wc_sc, a, b) for a in range(2)]
+            return product(["tab0", "tab1"], [whole], j, pass_1_first)
 
-        def turn(name, first):
-            if first:
-                st["T" + name[1:]] = banks["c"].tile([P, PACK, P], F32, name="turned")
-            src = st[("i" if first else "r") + name[1:]]
+        def turn(term, bank, first):
             for t in range(PACK):
                 nc.tensor.matmul(
-                    out=st["T" + name[1:]][:, t, :], lhsT=src[:, t, :], rhs=ident[:],
+                    out=bank[:, t, :], lhsT=term[:, t, :], rhs=ident[:],
                     start=(first and t == 0), stop=(not first and t == PACK - 1), is_transpose=True,
                 )
 
-        def task(name):
-            kind = name[0]
-            if name == "v2":
-                st[name] = [gather("v2", st["t2"], tab2_sc, 0, list_v2)]
-            elif name in ("v0", "v1"):
-                a = int(name[1])
-                st[name] = gather(name, st["t" + name[1]], tab_sc, a, list_v)
-            elif kind == "c":
-                st[name] = cast(name[1:])
-            elif kind == "q":
-                st[name] = quantise(name, st["c" + name[1:]])
-            elif kind == "R":
-                b, j = int(name[1]), int(name[2])
-                st[name] = fresh("S", name, [P, PACK, P], F32)
-                nc.scalar.copy(out=st[name][:], in_=product(st["v2"], [[fp4_half(st["wb"], wb_sc, 0, b)]], j, "R"))
-            elif kind == "I":
-                b, j = int(name[1]), int(name[2])
-                st[name] = fresh("S", name, [P, PACK, P], F32)
-                nc.scalar.activation(out=st[name][:], in_=imag(CFG["first"][b], b, j, "I"), func=COPY, scale=-1.0)
-            elif kind == "i":
-                b, j = int(name[1]), int(name[2])
-                st[name] = fresh("V", name, [P, PACK, P], F32)
-                nc.vector.tensor_tensor(
-                    out=st[name][:], in0=imag("rs".replace(CFG["first"][b], ""), b, j, "i"), in1=st["I" + name[1:]][:], op=MULT
+        def step(name):
+            kind, where = name.split(":")
+            if kind == "pick":
+                made[name] = pick(where)
+            elif kind.startswith("cast"):
+                made["cast:" + where] = cast(kind[4], where)
+            elif kind == "quant":
+                made[name] = quantise("quant_" + where, made["cast:" + where])
+            elif kind == "quant_h":
+                made[name] = quantise("quant_h" + where, made["h:" + where])
+            elif kind == "rre":
+                made[name] = fresh("S", kind + where, [P, PACK, P], F32)
+                nc.scalar.copy(out=made[name][:], in_=factor(kind, int(where[0]), int(where[1])))
+            elif kind == "im1st":
+                made[name] = fresh("S", kind + where, [P, PACK, P], F32)
+                nc.scalar.activation(
+                    out=made[name][:], in_=factor(kind, int(where[0]), int(where[1])), func=COPY, scale=-1.0
                 )
-            elif kind == "t":
-                turn(name, True)
-            elif kind == "r":
-                b, j = int(name[1]), int(name[2])
-                wa_q = [[st["qa%d%d%d" % (b, a, part)] for a in range(2)] for part in range(2)]
-                st[name] = fresh("V", name, [P, PACK, P], F32)
+            elif kind in ("re", "im"):
+                earlier = made[{"re": "rre:", "im": "im1st:"}[kind] + where]
+                made[name] = fresh("V", kind + where, [P, PACK, P], F32)
                 nc.vector.tensor_tensor(
-                    out=st[name][:], in0=product([st["v0"], st["v1"]], wa_q, j, "r%d" % b), in1=st["R" + name[1:]][:], op=MULT
+                    out=made[name][:], in0=factor(kind, int(where[0]), int(where[1])), in1=earlier[:], op=MULT
                 )
-            elif kind == "u":
-                turn(name, False)
-            elif kind == "k":
-                b, j = int(name[1]), int(name[2])
-                key = "H%d%d" % (b, j // 2)
-                if key not in st:
-                    st[key] = fresh("S", key, [P, 2 * P, PACK], BF16)
+            elif kind == "turn_im":
+                made["bank:" + where] = turn_banks.tile([P, PACK, P], F32, name="turned")
+                turn(made["im:" + where], made["bank:" + where], True)
+            elif kind == "turn_re":
+                turn(made["re:" + where], made["bank:" + where], False)
+            elif kind == "round":
+                j = int(where[1])
+                key = "h:%s%d" % (where[0], j // 2)
+                if key not in made:
+                    made[key] = fresh("S", "h" + key[2:], [P, PART, PACK], BF16)
                 nc.scalar.copy(
-                    out=st[key][:, P * (j % 2) : P * (j % 2 + 1), :], in_=st["T" + name[1:]][:].rearrange("p t j -> p j t")
+                    out=made[key][:, P * (j % 2) : P * (j % 2 + 1), :],
+                    in_=made["bank:" + where][:].rearrange("p t j -> p j t"),
                 )
-            elif kind == "h":
-                st[name] = quantise(name, st["H" + name[1:]])
             elif kind == "y":
-                n, h0, h1 = int(name[1]), int(name[2]), int(name[3])
-                y_acc = banks[CFG["ybank"]].tile([P, S], F32, name="acc" if CFG["ybank"] == "a" else "turned")
-                for half in range(h0, h1):
+                n, c0, c1 = int(where[0]), int(where[1]), int(where[2])
+                acc = product_banks.tile([P, S], F32, name="acc")
+                for c in range(c0, c1):
                     for b in (1, 0):
+                        codes, scales = made["quant_h:%d%d" % (b, c)]
                         nc.tensor.matmul_mx(
-                            out=y_acc[:, QUARTER * (half - h0) : QUARTER * (half - h0 + 1)],
-                            lhsT=st["wo"][:, b, P * n : P * (n + 1)].bitcast(FP8X4),
+                            out=acc[:, PART * (c - c0) : PART * (c - c0 + 1)],
+                            lhsT=made["wo"][:, b, P * n : P * (n + 1)].bitcast(FP8X4),
                             lhsT_scale=wo_sc[4 * (b + 1) :, P // 4 * n : P // 4 * (n + 1)].bitcast(U8),
-                            rhs=st["h%d%d" % (b, half)][0],
-                            rhs_scale=st["h%d%d" % (b, half)][1],
+                            rhs=codes,
+                            rhs_scale=scales,
                             start=(b == 1),
                             stop=(b == 0),
                         )
-                width = QUARTER * (h1 - h0)
-                st[name] = fresh("S", name, [P, width], F32)
-                nc.scalar.copy(out=st[name][:], in_=y_acc[:, :width])
+                width = PART * (c1 - c0)
+                made[name] = fresh("S", kind + where, [P, width], F32)
+                nc.scalar.copy(out=made[name][:], in_=acc[:, :width])
             else:
-                n, h0, h1 = int(name[1]), int(name[2]), int(name[3])
-                cols = slice(QUARTER * h0, QUARTER * h1)
-                scaled = fresh("V", name, [P, QUARTER * (h1 - h0)], F32)
+                n, c0, c1 = int(where[0]), int(where[1]), int(where[2])
+                offsets = list_v[:, PART // 16 * c0 : PART // 16 * c1]
+                scaled = fresh("V", kind + where, [P, PART * (c1 - c0)], F32)
                 nc.vector.tensor_tensor(
-                    out=scaled[:], in0=st["g%d" % n][:].indirect(list_v[:, 16 * h0 : 16 * h1]), in1=st["y" + name[1:]][:], op=MULT
+                    out=scaled[:], in0=made["gT%d" % n][:].indirect(offsets), in1=made["y:" + where][:], op=MULT
                 )
-                nc.sync.dma_start(out=out[P * n : P * (n + 1), cols], in_=scaled[:])
+                nc.sync.dma_start(out=out[P * n : P * (n + 1), PART * c0 : PART * c1], in_=scaled[:])
 
-        for name in CFG["tasks"].split():
-            task(name)
+        for name in LOADS:
+            load(name)
+        for name in STEPS:
+            step(name)

@@ -24,28 +24,28 @@ HALF = 512
 PART = 256
 
 RING_DEPTH = {"V": 16, "S": 24}
-PRODUCT_BANKS = 3
-TURN_BANKS = 5
+PRODUCT_BANKS = 4
+TURN_BANKS = 4
 
 LOADS = """
-tab2 list2 list tab2_sc wd00 wb_sc wb tab0 tab_sc tab1 wc wc_sc wa00 wo_sc wa01 wd10 wa10 wa11 gT0
-gT1 wo gT2 gT3 gT4 gT5
+list list2 wb tab2_sc tab2 wd00 wb_sc tab0 tab_sc tab1 wc_sc wc wa00 wa01 wd10 wa10 wa11 gT0 gT1
+wo_sc wo gT2 gT3 gT4 gT5
 """.split()
 
 STEPS = """
-pick:tab2 rre:10 castV:wd001 rre:11 castV:wd000 rre:00 quant:wd001 quant:wd000 rre:01 im1st:00
-rre:12 im1st:01 rre:02 rre:03 im1st:02 pick:tab0 pick:tab1 im1st:03 im:00 im:01 castS:wa000
-castV:wa001 im1st:10 im:02 im1st:11 castS:wa011 im1st:12 quant:wa000 im1st:13 castV:wa010 turn_im:00
-turn_im:01 quant:wa010 quant:wa011 rre:13 quant:wa001 castS:wd101 castV:wd100 castS:wa100 re:00
-castS:wa101 turn_re:00 turn_im:02 im:03 round:00 quant:wd101 quant:wd100 re:01 re:02 quant:wa100
-castS:wa110 re:03 im:10 turn_re:01 castV:wa111 turn_im:03 turn_re:02 im:11 quant:wa111 turn_im:10
-quant:wa110 turn_im:11 quant:wa101 round:01 im:12 re:10 re:11 re:12 turn_re:10 round:02 round:10
-im:13 re:13 turn_re:11 turn_im:12 turn_re:03 round:11 turn_re:12 quant_h:00 round:12 turn_im:13
-quant_h:10 turn_re:13 round:03 round:13 quant_h:01 y:001 y:101 quant_h:11 scale:001 scale:101 y:012
-y:112 y:202 scale:012 y:302 scale:112 y:402 scale:202 y:502 scale:302 scale:402 scale:502
+pick:tab2 rre:00 rre:10 pick:tab0 castV:wd001 castV:wd000 rre:11 rre:01 quant:wd001 quant:wd000
+im1st:00 pick:tab1 im1st:01 rre:12 rre:02 im1st:02 im1st:03 rre:13 rre:03 castS:wa000 im:00 im:01
+castV:wa001 im:02 quant:wa000 turn_im:00 castV:wa010 im1st:10 castS:wa011 im1st:11 quant:wa010
+im1st:12 quant:wa001 castS:wd101 im1st:13 castS:wa100 quant:wa011 turn_im:01 castV:wd100 re:00 im:03
+castS:wa110 quant:wd101 turn_re:00 castV:wa101 turn_im:02 re:01 re:02 quant:wd100 castS:wa111 re:03
+turn_im:03 quant:wa100 round:00 quant:wa110 turn_re:01 quant:wa101 round:01 im:10 quant:wa111 im:11
+turn_re:02 re:10 turn_im:10 re:11 turn_im:11 round:02 im:12 im:13 turn_re:10 re:12 re:13 round:10
+turn_re:11 turn_im:12 turn_re:03 turn_re:12 turn_im:13 round:03 quant_h:00 quant_h:01 round:11
+turn_re:13 round:12 quant_h:10 y:001 round:13 y:101 quant_h:11 scale:001 scale:101 y:012 y:112 y:202
+scale:012 y:302 scale:112 y:402 scale:202 y:502 scale:302 scale:402 scale:502
 """.split()
 
-PASS_1_FIRST = {("im1st", 1), ("re", 0)}
+PASS_1_FIRST = {("im1st", 1)}
 
 
 def tile_list_complex_relation_embedding_kernel(
@@ -100,10 +100,10 @@ def tile_list_complex_relation_embedding_kernel(
                 nc.sync.dma_start(list_v2[:], offs2)
             elif name in planes:
                 plane, scales = planes[name]
-                for q in range(4):
+                for r in range(4):
                     nc.sync.dma_start(
-                        out=plane[32 * q : 32 * q + 4, :, :],
-                        in_=scales[:, 4 * q : 4 * q + 4, :].rearrange("a r c -> r a c").bitcast(I32),
+                        out=plane[r:P:32, :, :],
+                        in_=scales[:, r:16:4, :].rearrange("a q c -> q a c").bitcast(I32),
                     )
             elif name == "wo_sc":
                 for q in range(4):

@@ -22,30 +22,10 @@ PACK = 4
 PASS = P * PACK
 HALF = 512
 PART = 256
+TILES = S // P
 
-RING_DEPTH = {"V": 16, "S": 24}
-PRODUCT_BANKS = 4
-TURN_BANKS = 4
-
-LOADS = """
-list list2 wb tab2_sc tab2 wd00 wb_sc tab0 tab_sc tab1 wc_sc wc wa00 wa01 wd10 wa10 wa11 gT0 gT1
-wo_sc wo gT2 gT3 gT4 gT5
-""".split()
-
-STEPS = """
-pick:tab2 rre:00 rre:10 pick:tab0 castV:wd001 castV:wd000 rre:11 rre:01 quant:wd001 quant:wd000
-im1st:00 pick:tab1 im1st:01 rre:12 rre:02 im1st:02 im1st:03 rre:13 rre:03 castS:wa000 im:00 im:01
-castV:wa001 im:02 quant:wa000 turn_im:00 castV:wa010 im1st:10 castS:wa011 im1st:11 quant:wa010
-im1st:12 quant:wa001 castS:wd101 im1st:13 castS:wa100 quant:wa011 turn_im:01 castV:wd100 re:00 im:03
-castS:wa110 quant:wd101 turn_re:00 castV:wa101 turn_im:02 re:01 re:02 quant:wd100 castS:wa111 re:03
-turn_im:03 quant:wa100 round:00 quant:wa110 turn_re:01 quant:wa101 round:01 im:10 quant:wa111 im:11
-turn_re:02 re:10 turn_im:10 re:11 turn_im:11 round:02 im:12 im:13 turn_re:10 re:12 re:13 round:10
-turn_re:11 turn_im:12 turn_re:03 turn_re:12 turn_im:13 round:03 quant_h:00 quant_h:01 round:11
-turn_re:13 round:12 quant_h:10 y:001 round:13 y:101 quant_h:11 scale:001 scale:101 y:012 y:112 y:202
-scale:012 y:302 scale:112 y:402 scale:202 y:502 scale:302 scale:402 scale:502
-""".split()
-
-PASS_1_FIRST = {("im1st", 1)}
+VECTOR_RING = 22
+SCALAR_RING = 24
 
 
 def tile_list_complex_relation_embedding_kernel(
@@ -55,15 +35,15 @@ def tile_list_complex_relation_embedding_kernel(
     nc = tc.nc
     with ExitStack() as ctx:
         keep = ctx.enter_context(tc.tile_pool(name="keep", bufs=1))
-        rings = {e: ctx.enter_context(tc.tile_pool(name="ring_" + e, bufs=n)) for e, n in RING_DEPTH.items()}
-        product_banks = ctx.enter_context(tc.psum_pool(name="product_banks", bufs=PRODUCT_BANKS))
-        turn_banks = ctx.enter_context(tc.psum_pool(name="turn_banks", bufs=TURN_BANKS))
+        vector_ring = ctx.enter_context(tc.tile_pool(name="vector_ring", bufs=VECTOR_RING))
+        scalar_ring = ctx.enter_context(tc.tile_pool(name="scalar_ring", bufs=SCALAR_RING))
+        banks = ctx.enter_context(tc.psum_pool(name="banks", bufs=8))
 
         def held(name, shape, dtype):
             return keep.tile(shape, dtype, name=name, align_bytes=64)
 
-        def fresh(engine, name, shape, dtype):
-            return rings[engine].tile(shape, dtype, name=name, tag="slot", align_bytes=64)
+        def fresh(ring, name, shape, dtype):
+            return ring.tile(shape, dtype, name=name, tag="slot", align_bytes=64)
 
         list_v = keep.tile([P, S // 16], U16, name="list_v")
         list_v2 = keep.tile([P, S // 16], U16, name="list_v2")
@@ -73,113 +53,80 @@ def tile_list_complex_relation_embedding_kernel(
         tab_sc = held("tab_sc", [P, 2, T // 4], I32)
         wc_sc = held("wc_sc", [P, 2, H // 4], I32)
         wo_sc = held("wo_sc", [P, N // 4], I32)
-        for plane in (tab2_sc, wb_sc):
-            nc.gpsimd.memset(plane[:], 0)
-        for plane in (tab_sc, wc_sc, wo_sc):
+        for plane in (tab2_sc, tab_sc, wb_sc, wc_sc, wo_sc):
             nc.vector.memset(plane[:], 0)
-        planes = {
-            "tab2_sc": (tab2_sc, tab2_scales),
-            "wb_sc": (wb_sc, wb_scales),
-            "tab_sc": (tab_sc, tab_scales),
-            "wc_sc": (wc_sc, wc_scales),
-        }
 
         ident = held("ident", [P, P], F32)
-        make_identity(nc, ident[:])
 
-        made = {}
+        def load_words(name, shape, dtype, source):
+            tile = held(name, shape, dtype)
+            nc.sync.dma_start(out=tile[:].bitcast(I32), in_=source.bitcast(I32))
+            return tile
 
-        def load_bytes(name, shape, dtype, source):
-            made[name] = held(name, shape, dtype)
-            nc.sync.dma_start(out=made[name][:].bitcast(I32), in_=source.bitcast(I32))
+        def load_plane(queue, plane, scales):
+            for r in range(4):
+                queue.dma_start(
+                    out=plane[r:P:32, :, :], in_=scales[:, r:16:4, :].rearrange("a q c -> q a c").bitcast(I32)
+                )
 
-        def load(name):
-            if name == "list":
-                nc.sync.dma_start(list_v[:], offs)
-            elif name == "list2":
-                nc.sync.dma_start(list_v2[:], offs2)
-            elif name in planes:
-                plane, scales = planes[name]
-                for r in range(4):
-                    nc.sync.dma_start(
-                        out=plane[r:P:32, :, :],
-                        in_=scales[:, r:16:4, :].rearrange("a q c -> q a c").bitcast(I32),
-                    )
-            elif name == "wo_sc":
-                for q in range(4):
-                    nc.sync.dma_start(
-                        out=wo_sc[32 * q + 4 : 32 * q + 12, :],
-                        in_=wo_scales[:, 4 * q : 4 * q + 4, :].bitcast(I32),
-                    )
-            elif name == "tab2":
-                load_bytes(name, [P, T2], U32, tab2_words[0].rearrange("p t i -> p (t i)"))
-            elif name in ("tab0", "tab1"):
-                load_bytes(name, [P, T], U32, tab_words[int(name[3])].rearrange("p t i -> p (t i)"))
-            elif name == "wb":
-                load_bytes(name, [P, 2 * H], U8, wb_words[0])
-            elif name == "wc":
-                load_bytes(name, [P, 2, 2 * H], U8, wc_words.rearrange("a p c -> p a c"))
-            elif name == "wo":
-                load_bytes(name, [P, 2, N], U32, wo_words.rearrange("a p c i -> p a (c i)"))
-            elif name.startswith("gT"):
-                n = int(name[2])
-                made[name] = held(name, [P, T], F32)
-                nc.sync.dma_start(out=made[name][:], in_=gT[P * n : P * (n + 1), :])
-            else:
-                weight, b, a = {"wa": wa, "wd": wd}[name[:2]], int(name[2]), int(name[3])
-                made[name] = held(name, [P, PACK, HALF], F32)
-                rows = weight[PASS * a : PASS * (a + 1), HALF * b : HALF * (b + 1)]
-                nc.sync.dma_start(out=made[name][:], in_=rows.rearrange("(p i) c -> p i c", i=PACK))
+        def load_wo_planes(queue):
+            for q in range(4):
+                queue.dma_start(
+                    out=wo_sc[32 * q + 4 : 32 * q + 12, :], in_=wo_scales[:, 4 * q : 4 * q + 4, :].bitcast(I32)
+                )
 
-        def pick(table):
-            plane, a, offsets = {
-                "tab2": (tab2_sc, 0, list_v2),
-                "tab0": (tab_sc, 0, list_v),
-                "tab1": (tab_sc, 1, list_v),
-            }[table]
-            codes = held(table + "_codes", [P, S], U32)
-            scales = held(table + "_scales", [P, S], U8)
-            nc.vector.tensor_copy(out=codes[:], in_=made[table][:].indirect(offsets[:]))
+        def load_weight(name, weight, b, a):
+            tile = held(name, [P, PACK, HALF], F32)
+            rows = weight[PASS * a : PASS * (a + 1), HALF * b : HALF * (b + 1)]
+            nc.sync.dma_start(out=tile[:], in_=rows.rearrange("(p i) c -> p i c", i=PACK))
+            return tile
+
+        def load_gains(n):
+            tile = held("gT%d" % n, [P, T], F32)
+            nc.sync.dma_start(out=tile[:], in_=gT[P * n : P * (n + 1), :])
+            return tile
+
+        def pick_words(name, words, offsets):
+            codes = fresh(vector_ring, name, [P, S], U32)
+            nc.vector.tensor_copy(out=codes[:], in_=words[:].indirect(offsets[:]))
+            return codes
+
+        def pick_scales(name, plane, a, offsets):
+            scales = fresh(vector_ring, name, [P, S], U8)
             nc.vector.tensor_copy(out=scales[:], in_=plane[:, a, :].bitcast(U8).indirect(offsets[:]))
-            return codes, scales
+            return scales
 
-        def cast(engine, part):
-            c0 = PART * int(part[4])
-            raw = made[part[:4]][:, :, c0 : c0 + PART]
-            grouped = fresh(engine, "cast_" + part, [P, PART, PACK], BF16)
-            copy = nc.scalar.copy if engine == "S" else nc.vector.tensor_copy
+        def cast(on_vector, name, raw, c):
+            ring, copy = (vector_ring, nc.vector.tensor_copy) if on_vector else (scalar_ring, nc.scalar.copy)
+            grouped = fresh(ring, name, [P, PART, PACK], BF16)
             copy(
                 out=grouped[:].rearrange("p (c e) i -> p c i e", e=4),
-                in_=raw.rearrange("p i (c e) -> p c i e", e=4),
+                in_=raw[:, :, PART * c : PART * (c + 1)].rearrange("p i (c e) -> p c i e", e=4),
             )
             return grouped
 
         def quantise(name, grouped):
-            codes = fresh("V", name + "_codes", [P, PART], U32)
+            codes = fresh(vector_ring, name + "_codes", [P, PART], U32)
             scales = held(name + "_scales", [P, PART], U8)
             nc.vector.quantize_mx(
                 out=codes[:].bitcast(FP8X4), scales=scales[:], in_=grouped[:].rearrange("p c i -> p (c i)")
             )
             return codes[:].bitcast(FP8X4), scales[:]
 
-        def product(tables, weights, j, pass_1_first):
-            acc = product_banks.tile([P, HALF], F32, name="acc")
+        def product(picked, weights, j):
+            acc = banks.tile([P, HALF], F32, name="acc", tag="bank")
             tokens = slice(P * j, P * (j + 1))
-            passes = list(range(len(tables)))
-            if pass_1_first:
-                passes = passes[::-1]
             width = HALF // len(weights)
-            for c in range(len(weights)):
-                for a in passes:
-                    codes, scales = made["pick:" + tables[a]]
+            for c, passes in enumerate(weights):
+                for a, (codes, scales) in enumerate(picked):
                     nc.tensor.matmul_mx(
                         out=acc[:, width * c : width * (c + 1)],
                         lhsT=codes[:, tokens].bitcast(FP8X4),
                         lhsT_scale=scales[:, tokens],
-                        rhs=weights[c][a][0],
-                        rhs_scale=weights[c][a][1],
-                        start=(a == passes[0]),
-                        stop=(a == passes[-1]),
+                        rhs=passes[a][0],
+                        rhs_scale=passes[a][1],
+                        start=(a == 0),
+                        stop=(a == len(picked) - 1),
                     )
             return acc[:].rearrange("p (m t) -> p t m", t=PACK)
 
@@ -189,18 +136,15 @@ def tile_list_complex_relation_embedding_kernel(
                 plane[:, a, HALF // 4 * b : HALF // 4 * (b + 1)].bitcast(U8),
             )
 
-        def factor(kind, b, j):
-            pass_1_first = (kind, b) in PASS_1_FIRST
-            if kind == "rre":
-                return product(["tab2"], [[fp4_half(made["wb"], wb_sc, 0, b)]], j, pass_1_first)
-            if kind == "re":
-                parts = [[made["quant:wa%d%d%d" % (b, a, c)] for a in range(2)] for c in range(2)]
-                return product(["tab0", "tab1"], parts, j, pass_1_first)
-            if (kind == "im1st") == (b == 0):
-                parts = [[made["quant:wd%d0%d" % (b, c)]] for c in range(2)]
-                return product(["tab2"], parts, j, pass_1_first)
-            whole = [fp4_half(made["wc"][:, a, :], wc_sc, a, b) for a in range(2)]
-            return product(["tab0", "tab1"], [whole], j, pass_1_first)
+        def keep_factor(name, sums, sign):
+            factor = fresh(scalar_ring, name, [P, PACK, P], F32)
+            nc.scalar.activation(out=factor[:], in_=sums, func=COPY, scale=sign)
+            return factor
+
+        def multiply(name, sums, factor):
+            term = fresh(vector_ring, name, [P, PACK, P], F32)
+            nc.vector.tensor_tensor(out=term[:], in0=sums, in1=factor[:], op=MULT)
+            return term
 
         def turn(term, bank, first):
             for t in range(PACK):
@@ -209,72 +153,180 @@ def tile_list_complex_relation_embedding_kernel(
                     start=(first and t == 0), stop=(not first and t == PACK - 1), is_transpose=True,
                 )
 
-        def step(name):
-            kind, where = name.split(":")
-            if kind == "pick":
-                made[name] = pick(where)
-            elif kind.startswith("cast"):
-                made["cast:" + where] = cast(kind[4], where)
-            elif kind == "quant":
-                made[name] = quantise("quant_" + where, made["cast:" + where])
-            elif kind == "quant_h":
-                made[name] = quantise("quant_h" + where, made["h:" + where])
-            elif kind == "rre":
-                made[name] = fresh("S", kind + where, [P, PACK, P], F32)
-                nc.scalar.copy(out=made[name][:], in_=factor(kind, int(where[0]), int(where[1])))
-            elif kind == "im1st":
-                made[name] = fresh("S", kind + where, [P, PACK, P], F32)
-                nc.scalar.activation(
-                    out=made[name][:], in_=factor(kind, int(where[0]), int(where[1])), func=COPY, scale=-1.0
-                )
-            elif kind in ("re", "im"):
-                earlier = made[{"re": "rre:", "im": "im1st:"}[kind] + where]
-                made[name] = fresh("V", kind + where, [P, PACK, P], F32)
-                nc.vector.tensor_tensor(
-                    out=made[name][:], in0=factor(kind, int(where[0]), int(where[1])), in1=earlier[:], op=MULT
-                )
-            elif kind == "turn_im":
-                made["bank:" + where] = turn_banks.tile([P, PACK, P], F32, name="turned")
-                turn(made["im:" + where], made["bank:" + where], True)
-            elif kind == "turn_re":
-                turn(made["re:" + where], made["bank:" + where], False)
-            elif kind == "round":
-                j = int(where[1])
-                key = "h:%s%d" % (where[0], j // 2)
-                if key not in made:
-                    made[key] = fresh("S", "h" + key[2:], [P, PART, PACK], BF16)
-                nc.scalar.copy(
-                    out=made[key][:, P * (j % 2) : P * (j % 2 + 1), :],
-                    in_=made["bank:" + where][:].rearrange("p t j -> p j t"),
-                )
-            elif kind == "y":
-                n, c0, c1 = int(where[0]), int(where[1]), int(where[2])
-                acc = product_banks.tile([P, S], F32, name="acc")
-                for c in range(c0, c1):
-                    for b in (1, 0):
-                        codes, scales = made["quant_h:%d%d" % (b, c)]
-                        nc.tensor.matmul_mx(
-                            out=acc[:, PART * (c - c0) : PART * (c - c0 + 1)],
-                            lhsT=made["wo"][:, b, P * n : P * (n + 1)].bitcast(FP8X4),
-                            lhsT_scale=wo_sc[4 * (b + 1) :, P // 4 * n : P // 4 * (n + 1)].bitcast(U8),
-                            rhs=codes,
-                            rhs_scale=scales,
-                            start=(b == 1),
-                            stop=(b == 0),
-                        )
-                width = PART * (c1 - c0)
-                made[name] = fresh("S", kind + where, [P, width], F32)
-                nc.scalar.copy(out=made[name][:], in_=acc[:, :width])
-            else:
-                n, c0, c1 = int(where[0]), int(where[1]), int(where[2])
-                offsets = list_v[:, PART // 16 * c0 : PART // 16 * c1]
-                scaled = fresh("V", kind + where, [P, PART * (c1 - c0)], F32)
-                nc.vector.tensor_tensor(
-                    out=scaled[:], in0=made["gT%d" % n][:].indirect(offsets), in1=made["y:" + where][:], op=MULT
-                )
-                nc.sync.dma_start(out=out[P * n : P * (n + 1), PART * c0 : PART * c1], in_=scaled[:])
+        def project(n, c0, c1):
+            acc = banks.tile([P, S], F32, name="acc", tag="bank")
+            for c in range(c0, c1):
+                for b in (1, 0):
+                    codes, scales = h_codes[b, c]
+                    nc.tensor.matmul_mx(
+                        out=acc[:, PART * c : PART * (c + 1)],
+                        lhsT=wo[:, b, P * n : P * (n + 1)].bitcast(FP8X4),
+                        lhsT_scale=wo_sc[4 * (b + 1) :, P // 4 * n : P // 4 * (n + 1)].bitcast(U8),
+                        rhs=codes,
+                        rhs_scale=scales,
+                        start=(b == 1),
+                        stop=(b == 0),
+                    )
+            y[n, c0] = fresh(scalar_ring, "y%d%d" % (n, c0), [P, PART * (c1 - c0)], F32)
+            nc.scalar.copy(out=y[n, c0][:], in_=acc[:, PART * c0 : PART * c1])
 
-        for name in LOADS:
-            load(name)
-        for name in STEPS:
-            step(name)
+        def scale_and_store(n, c0, c1):
+            scaled = fresh(vector_ring, "scaled%d%d" % (n, c0), [P, PART * (c1 - c0)], F32)
+            offsets = list_v[:, PART // 16 * c0 : PART // 16 * c1]
+            nc.vector.tensor_tensor(out=scaled[:], in0=gains[n][:].indirect(offsets), in1=y[n, c0][:], op=MULT)
+            nc.sync.dma_start(out=out[P * n : P * (n + 1), PART * c0 : PART * c1], in_=scaled[:])
+
+        y = {}
+        raw, grouped, quant, r_re, r_im, im, re, bank, h, h_codes, sums = {}, {}, {}, {}, {}, {}, {}, {}, {}, {}, {}
+
+        def cast_part(on_vector, w, b, a, c):
+            grouped[w, b, a, c] = cast(on_vector, "cast_%s%d%d%d" % (w, b, a, c), raw[w, b, a], c)
+
+        def quant_part(w, b, a, c):
+            quant[w, b, a, c] = quantise("q_%s%d%d%d" % (w, b, a, c), grouped[w, b, a, c])
+
+        def keep_r_im(b, j):
+            sums = product(relations, [[quant["wd", b, 0, c]] for c in range(2)], j)
+            r_im[b, j] = keep_factor("r_im%d%d" % (b, j), sums, -1.0)
+
+        def keep_r_re(b, j):
+            sums = product(relations, [[fp4_half(wb, wb_sc, 0, b)]], j)
+            r_re[b, j] = keep_factor("r_re%d%d" % (b, j), sums, 1.0)
+
+        def s_im(b, j):
+            sums["im", b, j] = product(subjects, [[fp4_half(wc[:, a, :], wc_sc, a, b) for a in range(2)]], j)
+
+        def s_re(b, j):
+            sums["re", b, j] = product(subjects, [[quant["wa", b, a, c] for a in range(2)] for c in range(2)], j)
+
+        def im_term(b, j):
+            im[b, j] = multiply("im%d%d" % (b, j), sums["im", b, j], r_im[b, j])
+
+        def re_term(b, j):
+            re[b, j] = multiply("re%d%d" % (b, j), sums["re", b, j], r_re[b, j])
+
+        def turn_im(b, j):
+            bank[b, j] = banks.tile([P, PACK, P], F32, name="turned", tag="bank")
+            turn(im[b, j], bank[b, j], True)
+
+        def turn_re(b, j):
+            turn(re[b, j], bank[b, j], False)
+
+        def round_h(b, j):
+            if j % 2 == 0:
+                h[b, j // 2] = fresh(scalar_ring, "h%d%d" % (b, j // 2), [P, PART, PACK], BF16)
+            nc.scalar.copy(
+                out=h[b, j // 2][:, P * (j % 2) : P * (j % 2 + 1), :], in_=bank[b, j][:].rearrange("p t j -> p j t")
+            )
+
+        def quant_h(b, c):
+            h_codes[b, c] = quantise("q_h%d%d" % (b, c), h[b, c])
+
+        nc.sync.dma_start(list_v2[:], offs2)
+        tab2 = load_words("tab2", [P, T2], U32, tab2_words[0].rearrange("p t i -> p (t i)"))
+        load_plane(nc.sync, tab2_sc, tab2_scales)
+        nc.sync.dma_start(list_v[:], offs)
+        raw["wd", 0, 0] = load_weight("wd0", wd, 0, 0)
+        load_plane(nc.gpsimd, tab_sc, tab_scales)
+        load_plane(nc.gpsimd, wb_sc, wb_scales)
+        load_plane(nc.gpsimd, wc_sc, wc_scales)
+        load_wo_planes(nc.gpsimd)
+        tab0 = load_words("tab0", [P, T], U32, tab_words[0].rearrange("p t i -> p (t i)"))
+        wb = load_words("wb", [P, 2 * H], U8, wb_words[0])
+        tab1 = load_words("tab1", [P, T], U32, tab_words[1].rearrange("p t i -> p (t i)"))
+        wc = load_words("wc", [P, 2, 2 * H], U8, wc_words.rearrange("a p c -> p a c"))
+        for a in range(2):
+            raw["wa", 0, a] = load_weight("wa0%d" % a, wa, 0, a)
+        raw["wd", 1, 0] = load_weight("wd1", wd, 1, 0)
+        for a in range(2):
+            raw["wa", 1, a] = load_weight("wa1%d" % a, wa, 1, a)
+        wo = load_words("wo", [P, 2, N], U32, wo_words.rearrange("a p c i -> p a (c i)"))
+        gains = [load_gains(n) for n in range(N // P)]
+        make_identity(nc, ident[:])
+
+        def keep_s_im(b, j):
+            s_im(b, j)
+            r_im[b, j] = keep_factor("s_im%d%d" % (b, j), sums["im", b, j], -1.0)
+
+        def late_r_im(b, j):
+            sums["im", b, j] = product(relations, [[quant["wd", b, 0, c]] for c in range(2)], j)
+
+        def turn_both(b, j):
+            bank[b, j] = banks.tile([P, PACK, P], F32, name="turned", tag="bank")
+            turn(re[b, j], bank[b, j], True)
+            turn(im[b, j], bank[b, j], False)
+
+        relations = [(pick_words("v2_codes", tab2, list_v2), pick_scales("v2_scales", tab2_sc, 0, list_v2))]
+        for c in range(2):
+            cast_part(c == 0, "wd", 0, 0, c)
+        scales = [pick_scales("v_scales0", tab_sc, 0, list_v)]
+        for c in range(2):
+            quant_part("wd", 0, 0, c)
+        words = [pick_words("v_codes0", tab0, list_v)]
+        scales.append(pick_scales("v_scales1", tab_sc, 1, list_v))
+        words.append(pick_words("v_codes1", tab1, list_v))
+        subjects = list(zip(words, scales))
+        for j in range(TILES):
+            keep_r_im(0, j)
+        for b in range(2):
+            for j in range(TILES):
+                keep_r_re(b, j)
+        for j in range(TILES):
+            s_im(0, j)
+        for c in range(2):
+            cast_part(False, "wa", 0, 0, c)
+        for j in range(TILES):
+            im_term(0, j)
+        for c in range(2):
+            quant_part("wa", 0, 0, c)
+        for j in range(TILES):
+            keep_s_im(1, j)
+            turn_im(0, j)
+        for c in range(2):
+            cast_part(True, "wa", 0, 1, c)
+        for c in range(2):
+            quant_part("wa", 0, 1, c)
+        for c in range(2):
+            cast_part(False, "wd", 1, 0, c)
+        for j in range(TILES):
+            s_re(0, j)
+        for c in range(2):
+            cast_part(False, "wa", 1, 0, c)
+        for j in range(TILES):
+            re_term(0, j)
+        for c in range(2):
+            quant_part("wd", 1, 0, c)
+        for j in range(TILES):
+            turn_re(0, j)
+            round_h(0, j)
+            late_r_im(1, j)
+        for c in range(2):
+            cast_part(True, "wa", 1, 1, c)
+        for a in range(2):
+            for c in range(2):
+                quant_part("wa", 1, a, c)
+        for c in range(2):
+            for j in (2 * c, 2 * c + 1):
+                s_re(1, j)
+            for j in (2 * c, 2 * c + 1):
+                im_term(1, j)
+            for j in (2 * c, 2 * c + 1):
+                re_term(1, j)
+        for j in range(TILES):
+            turn_both(1, j)
+            round_h(1, j)
+        for c in range(2):
+            quant_h(0, c)
+        quant_h(1, 0)
+        for n in range(2):
+            project(n, 0, 1)
+        quant_h(1, 1)
+        for n in range(2):
+            scale_and_store(n, 0, 1)
+            project(n, 1, 2)
+        for n in range(2, N // P):
+            project(n, 0, 2)
+        for n in range(2):
+            scale_and_store(n, 1, 2)
+        for n in range(2, N // P):
+            scale_and_store(n, 0, 2)

@@ -222,27 +222,27 @@ def tile_list_complex_relation_embedding_kernel(
         def quant_h(b, c):
             h_codes[b, c] = quantise("q_h%d%d" % (b, c), h[b, c])
 
+        make_identity(nc, ident[:])
         nc.sync.dma_start(list_v2[:], offs2)
         tab2 = load_words("tab2", [P, T2], U32, tab2_words[0].rearrange("p t i -> p (t i)"))
         load_plane(nc.sync, tab2_sc, tab2_scales)
         nc.sync.dma_start(list_v[:], offs)
         raw["wd", 0, 0] = load_weight("wd0", wd, 0, 0)
-        load_plane(nc.gpsimd, tab_sc, tab_scales)
-        load_plane(nc.gpsimd, wb_sc, wb_scales)
-        load_plane(nc.gpsimd, wc_sc, wc_scales)
-        load_wo_planes(nc.gpsimd)
+        load_plane(nc.sync, tab_sc, tab_scales)
         tab0 = load_words("tab0", [P, T], U32, tab_words[0].rearrange("p t i -> p (t i)"))
+        load_plane(nc.sync, wb_sc, wb_scales)
         wb = load_words("wb", [P, 2 * H], U8, wb_words[0])
         tab1 = load_words("tab1", [P, T], U32, tab_words[1].rearrange("p t i -> p (t i)"))
+        load_plane(nc.sync, wc_sc, wc_scales)
         wc = load_words("wc", [P, 2, 2 * H], U8, wc_words.rearrange("a p c -> p a c"))
-        for a in range(2):
-            raw["wa", 0, a] = load_weight("wa0%d" % a, wa, 0, a)
+        raw["wa", 0, 0] = load_weight("wa00", wa, 0, 0)
+        raw["wa", 0, 1] = load_weight("wa01", wa, 0, 1)
         raw["wd", 1, 0] = load_weight("wd1", wd, 1, 0)
-        for a in range(2):
-            raw["wa", 1, a] = load_weight("wa1%d" % a, wa, 1, a)
+        raw["wa", 1, 0] = load_weight("wa10", wa, 1, 0)
+        raw["wa", 1, 1] = load_weight("wa11", wa, 1, 1)
+        load_wo_planes(nc.sync)
         wo = load_words("wo", [P, 2, N], U32, wo_words.rearrange("a p c i -> p a (c i)"))
         gains = [load_gains(n) for n in range(N // P)]
-        make_identity(nc, ident[:])
 
         def keep_s_im(b, j):
             s_im(b, j)

@@ -113,6 +113,30 @@ def tile_list_complex_relation_embedding_kernel(
             )
             return codes[:].bitcast(FP8X4), scales[:]
 
+        def quantise_half(name, parts):
+            codes = fresh(vector_ring, name + "_codes", [P, HALF], U32)
+            scales = held(name + "_scales", [P, HALF], U8)
+            for c, grouped in enumerate(parts):
+                cols = slice(PART * c, PART * (c + 1))
+                nc.vector.quantize_mx(
+                    out=codes[:, cols].bitcast(FP8X4),
+                    scales=scales[:, cols],
+                    in_=grouped[:].rearrange("p c i -> p (c i)"),
+                )
+            return codes[:].bitcast(FP8X4), scales[:]
+
+        def one_pass(acc, picked, weight, j, start, stop):
+            tokens = slice(P * j, P * (j + 1))
+            nc.tensor.matmul_mx(
+                out=acc[:],
+                lhsT=picked[0][:, tokens].bitcast(FP8X4),
+                lhsT_scale=picked[1][:, tokens],
+                rhs=weight[0],
+                rhs_scale=weight[1],
+                start=start,
+                stop=stop,
+            )
+
         def product(picked, weights, j):
             acc = banks.tile([P, HALF], F32, name="acc", tag="bank")
             tokens = slice(P * j, P * (j + 1))
@@ -171,12 +195,16 @@ def tile_list_complex_relation_embedding_kernel(
             nc.scalar.copy(out=y[n, c0][:], in_=acc[:, PART * c0 : PART * c1])
 
         def scale_and_store(n, c0, c1):
-            scaled = fresh(vector_ring, "scaled%d%d" % (n, c0), [P, PART * (c1 - c0)], F32)
+            if c0 == 0:
+                scaled[n] = fresh(vector_ring, "scaled%d" % n, [P, S], F32)
             offsets = list_v[:, PART // 16 * c0 : PART // 16 * c1]
-            nc.vector.tensor_tensor(out=scaled[:], in0=gains[n][:].indirect(offsets), in1=y[n, c0][:], op=MULT)
-            nc.sync.dma_start(out=out[P * n : P * (n + 1), PART * c0 : PART * c1], in_=scaled[:])
+            nc.vector.tensor_tensor(
+                out=scaled[n][:, PART * c0 : PART * c1], in0=gains[n][:].indirect(offsets), in1=y[n, c0][:], op=MULT
+            )
+            if c1 == 2:
+                nc.sync.dma_start(out=out[P * n : P * (n + 1), :], in_=scaled[n][:])
 
-        y = {}
+        y, scaled, opened = {}, {}, {}
         raw, grouped, quant, r_re, r_im, im, re, bank, h, h_codes, sums = {}, {}, {}, {}, {}, {}, {}, {}, {}, {}, {}
 
         def cast_part(on_vector, w, b, a, c):
@@ -186,7 +214,7 @@ def tile_list_complex_relation_embedding_kernel(
             quant[w, b, a, c] = quantise("q_%s%d%d%d" % (w, b, a, c), grouped[w, b, a, c])
 
         def keep_r_im(b, j):
-            sums = product(relations, [[quant["wd", b, 0, c]] for c in range(2)], j)
+            sums = product(relations, [[quant["wd", b, 0]]], j)
             r_im[b, j] = keep_factor("r_im%d%d" % (b, j), sums, -1.0)
 
         def keep_r_re(b, j):
@@ -197,7 +225,15 @@ def tile_list_complex_relation_embedding_kernel(
             sums["im", b, j] = product(subjects, [[fp4_half(wc[:, a, :], wc_sc, a, b) for a in range(2)]], j)
 
         def s_re(b, j):
-            sums["re", b, j] = product(subjects, [[quant["wa", b, a, c] for a in range(2)] for c in range(2)], j)
+            sums["re", b, j] = product(subjects, [[quant["wa", b, a] for a in range(2)]], j)
+
+        def s_re_open(b, j):
+            opened[b, j] = banks.tile([P, HALF], F32, name="acc", tag="bank")
+            one_pass(opened[b, j], subjects[0], quant["wa", b, 0], j, True, False)
+
+        def s_re_close(b, j):
+            one_pass(opened[b, j], subjects[1], quant["wa", b, 1], j, False, True)
+            sums["re", b, j] = opened[b, j][:].rearrange("p (m t) -> p t m", t=PACK)
 
         def im_term(b, j):
             im[b, j] = multiply("im%d%d" % (b, j), sums["im", b, j], r_im[b, j])
@@ -249,19 +285,24 @@ def tile_list_complex_relation_embedding_kernel(
             r_im[b, j] = keep_factor("s_im%d%d" % (b, j), sums["im", b, j], -1.0)
 
         def late_r_im(b, j):
-            sums["im", b, j] = product(relations, [[quant["wd", b, 0, c]] for c in range(2)], j)
+            sums["im", b, j] = product(relations, [[quant["wd", b, 0]]], j)
 
         def turn_both(b, j):
             bank[b, j] = banks.tile([P, PACK, P], F32, name="turned", tag="bank")
             turn(re[b, j], bank[b, j], True)
             turn(im[b, j], bank[b, j], False)
 
+        def quant_both(w, b, a):
+            quant[w, b, a] = quantise_half("q_%s%d%d" % (w, b, a), [grouped[w, b, a, c] for c in range(2)])
+
+        def cast_both(on_vector, w, b, a):
+            for c in range(2):
+                cast_part(on_vector[c], w, b, a, c)
+
         relations = [(pick_words("v2_codes", tab2, list_v2), pick_scales("v2_scales", tab2_sc, 0, list_v2))]
-        for c in range(2):
-            cast_part(c == 0, "wd", 0, 0, c)
+        cast_both((True, False), "wd", 0, 0)
         scales = [pick_scales("v_scales0", tab_sc, 0, list_v)]
-        for c in range(2):
-            quant_part("wd", 0, 0, c)
+        quant_both("wd", 0, 0)
         words = [pick_words("v_codes0", tab0, list_v)]
         scales.append(pick_scales("v_scales1", tab_sc, 1, list_v))
         words.append(pick_words("v_codes1", tab1, list_v))
@@ -273,60 +314,51 @@ def tile_list_complex_relation_embedding_kernel(
                 keep_r_re(b, j)
         for j in range(TILES):
             s_im(0, j)
-        for c in range(2):
-            cast_part(False, "wa", 0, 0, c)
+        cast_both((False, False), "wa", 0, 0)
         for j in range(TILES):
             im_term(0, j)
-        for c in range(2):
-            quant_part("wa", 0, 0, c)
+        quant_both("wa", 0, 0)
         for j in range(TILES):
             keep_s_im(1, j)
             turn_im(0, j)
-        for c in range(2):
-            cast_part(True, "wa", 0, 1, c)
-        for c in range(2):
-            quant_part("wa", 0, 1, c)
-        for c in range(2):
-            cast_part(False, "wd", 1, 0, c)
+        cast_both((True, True), "wa", 0, 1)
+        quant_both("wa", 0, 1)
+        cast_both((False, False), "wd", 1, 0)
         for j in range(TILES):
             s_re(0, j)
-        for c in range(2):
-            cast_part(False, "wa", 1, 0, c)
+        cast_both((False, False), "wa", 1, 0)
         for j in range(TILES):
             re_term(0, j)
-        for c in range(2):
-            quant_part("wd", 1, 0, c)
+        quant_both("wd", 1, 0)
         for j in range(TILES):
             turn_re(0, j)
-            round_h(0, j)
             late_r_im(1, j)
-        for c in range(2):
-            cast_part(True, "wa", 1, 1, c)
-        for a in range(2):
-            for c in range(2):
-                quant_part("wa", 1, a, c)
-        for c in range(2):
-            for j in (2 * c, 2 * c + 1):
-                s_re(1, j)
-            for j in (2 * c, 2 * c + 1):
-                im_term(1, j)
-            for j in (2 * c, 2 * c + 1):
-                re_term(1, j)
+        cast_both((True, False), "wa", 1, 1)
+        quant_both("wa", 1, 0)
         for j in range(TILES):
+            round_h(0, j)
+            im_term(1, j)
+            s_re_open(1, j)
+            if j == 1:
+                quant_both("wa", 1, 1)
+        for j in range(TILES):
+            s_re_close(1, j)
+        for j in range(TILES):
+            re_term(1, j)
             turn_both(1, j)
             round_h(1, j)
         for c in range(2):
             quant_h(0, c)
         quant_h(1, 0)
-        for n in range(2):
+        for n in range(3):
             project(n, 0, 1)
         quant_h(1, 1)
-        for n in range(2):
+        for n in range(3):
             scale_and_store(n, 0, 1)
             project(n, 1, 2)
-        for n in range(2, N // P):
+        for n in range(3, N // P):
             project(n, 0, 2)
-        for n in range(2):
+        for n in range(3):
             scale_and_store(n, 1, 2)
-        for n in range(2, N // P):
+        for n in range(3, N // P):
             scale_and_store(n, 0, 2)

@@ -191,8 +191,25 @@ def tile_list_complex_relation_embedding_kernel(
                         start=(b == 1),
                         stop=(b == 0),
                     )
-            y[n, c0] = fresh(scalar_ring, "y%d%d" % (n, c0), [P, PART * (c1 - c0)], F32)
-            nc.scalar.copy(out=y[n, c0][:], in_=acc[:, PART * c0 : PART * c1])
+            if n in picked_gains:
+                y[n, c0] = acc
+            else:
+                y[n, c0] = fresh(scalar_ring, "y%d%d" % (n, c0), [P, PART * (c1 - c0)], F32)
+                nc.scalar.copy(out=y[n, c0][:], in_=acc[:, PART * c0 : PART * c1])
+
+        def pick_gains(n):
+            picked_gains[n] = fresh(vector_ring, "picked_gains%d" % n, [P, S], F32)
+            nc.vector.tensor_copy(out=picked_gains[n][:], in_=gains[n][:].indirect(list_v[:]))
+
+        def scale_from_psum(n, c0, c1):
+            if c0 == 0:
+                scaled[n] = fresh(vector_ring, "scaled%d" % n, [P, S], F32)
+            cols = slice(PART * c0, PART * c1)
+            nc.vector.tensor_tensor(
+                out=scaled[n][:, cols], in0=y_bank[n, c0][:, cols], in1=picked_gains[n][:, cols], op=MULT
+            )
+            if c1 == 2:
+                nc.sync.dma_start(out=out[P * n : P * (n + 1), :], in_=scaled[n][:])
 
         def scale_and_store(n, c0, c1):
             if c0 == 0:
@@ -204,6 +221,7 @@ def tile_list_complex_relation_embedding_kernel(
             if c1 == 2:
                 nc.sync.dma_start(out=out[P * n : P * (n + 1), :], in_=scaled[n][:])
 
+        picked_gains, h_scales, y_bank = {}, {}, {}
         y, scaled, opened = {}, {}, {}
         raw, grouped, quant, r_re, r_im, im, re, bank, h, h_codes, sums = {}, {}, {}, {}, {}, {}, {}, {}, {}, {}, {}
 
@@ -256,7 +274,33 @@ def tile_list_complex_relation_embedding_kernel(
             )
 
         def quant_h(b, c):
-            h_codes[b, c] = quantise("q_h%d%d" % (b, c), h[b, c])
+            if c == 0:
+                h_codes[b] = fresh(vector_ring, "h_codes%d" % b, [P, S], U32)
+                h_scales[b] = held("h_scales%d" % b, [P, S], U8)
+            cols = slice(PART * c, PART * (c + 1))
+            nc.vector.quantize_mx(
+                out=h_codes[b][:, cols].bitcast(FP8X4),
+                scales=h_scales[b][:, cols],
+                in_=h[b, c][:].rearrange("p c i -> p (c i)"),
+            )
+
+        def y_pass(n, b, c0=0, c1=2):
+            if b == 0:
+                y_bank[n, c0] = banks.tile([P, S], F32, name="acc", tag="bank")
+            cols = slice(PART * c0, PART * c1)
+            nc.tensor.matmul_mx(
+                out=y_bank[n, c0][:, cols],
+                lhsT=wo[:, b, P * n : P * (n + 1)].bitcast(FP8X4),
+                lhsT_scale=wo_sc[4 * (b + 1) :, P // 4 * n : P // 4 * (n + 1)].bitcast(U8),
+                rhs=h_codes[b][:, cols].bitcast(FP8X4),
+                rhs_scale=h_scales[b][:, cols],
+                start=(b == 0),
+                stop=(b == 1),
+            )
+
+        def keep_y(n):
+            y[n, 0] = fresh(scalar_ring, "y%d" % n, [P, S], F32)
+            nc.scalar.copy(out=y[n, 0][:], in_=y_bank[n, 0][:])
 
         make_identity(nc, ident[:])
         nc.sync.dma_start(list_v2[:], offs2)
@@ -314,51 +358,74 @@ def tile_list_complex_relation_embedding_kernel(
                 keep_r_re(b, j)
         for j in range(TILES):
             s_im(0, j)
-        cast_both((False, False), "wa", 0, 0)
+        cast_part(False, "wa", 0, 0, 1)
         for j in range(TILES):
             im_term(0, j)
+        cast_part(True, "wa", 0, 0, 0)
         quant_both("wa", 0, 0)
-        for j in range(TILES):
-            keep_s_im(1, j)
-            turn_im(0, j)
+        for pair in ((0, 1), (2, 3)):
+            for j in pair:
+                keep_s_im(1, j)
+            for j in pair:
+                turn_im(0, j)
         cast_both((True, True), "wa", 0, 1)
         quant_both("wa", 0, 1)
-        cast_both((False, False), "wd", 1, 0)
+        cast_both((True, False), "wd", 1, 0)
         for j in range(TILES):
             s_re(0, j)
         cast_both((False, False), "wa", 1, 0)
         for j in range(TILES):
             re_term(0, j)
-        quant_both("wd", 1, 0)
-        for j in range(TILES):
-            turn_re(0, j)
-            late_r_im(1, j)
+            if j == 1:
+                quant_both("wd", 1, 0)
+        for pair in ((0, 1), (2, 3)):
+            for j in pair:
+                late_r_im(1, j)
+            for j in pair:
+                turn_re(0, j)
+        im_term(1, 0)
         cast_both((True, False), "wa", 1, 1)
         quant_both("wa", 1, 0)
+        im_term(1, 1)
+        quant_both("wa", 1, 1)
         for j in range(TILES):
             round_h(0, j)
+        for j in (2, 3):
             im_term(1, j)
+        for j in range(TILES):
             s_re_open(1, j)
-            if j == 1:
-                quant_both("wa", 1, 1)
         for j in range(TILES):
             s_re_close(1, j)
-        for j in range(TILES):
-            re_term(1, j)
-            turn_both(1, j)
-            round_h(1, j)
+        for pair in ((0, 1), (2, 3)):
+            for j in pair:
+                turn_im(1, j)
+            for j in pair:
+                re_term(1, j)
+                turn_re(1, j)
+                round_h(1, j)
         for c in range(2):
             quant_h(0, c)
+        for n in (2, 3):
+            y_pass(n, 0)
+        pick_gains(0)
         quant_h(1, 0)
-        for n in range(3):
-            project(n, 0, 1)
+        pick_gains(1)
+        for n in (0, 1):
+            for b in range(2):
+                y_pass(n, b, 0, 1)
         quant_h(1, 1)
-        for n in range(3):
-            scale_and_store(n, 0, 1)
-            project(n, 1, 2)
-        for n in range(3, N // P):
-            project(n, 0, 2)
-        for n in range(3):
-            scale_and_store(n, 1, 2)
-        for n in range(3, N // P):
+        for n in (0, 1):
+            scale_from_psum(n, 0, 1)
+        for n in (0, 1):
+            y_pass(n + 2, 1)
+            keep_y(n + 2)
+            for b in range(2):
+                y_pass(n, b, 1, 2)
+        for n in (4, 5):
+            for b in range(2):
+                y_pass(n, b)
+            keep_y(n)
+        for n in (0, 1):
+            scale_from_psum(n, 1, 2)
+        for n in range(2, N // P):
             scale_and_store(n, 0, 2)

@@ -23,9 +23,14 @@ PASS = P * PACK
 HALF = 512
 PART = 256
 TILES = S // P
+PAIRS = ((0, 1), (2, 3))
+OUT_TILES = N // P
+WHOLE_LIST = slice(0, S)
+LIST_PARTS = (slice(0, PART), slice(PART, S))
 
 VECTOR_RING = 22
 SCALAR_RING = 24
+PSUM_BANKS = 8
 
 
 def tile_list_complex_relation_embedding_kernel(
@@ -37,13 +42,16 @@ def tile_list_complex_relation_embedding_kernel(
         keep = ctx.enter_context(tc.tile_pool(name="keep", bufs=1))
         vector_ring = ctx.enter_context(tc.tile_pool(name="vector_ring", bufs=VECTOR_RING))
         scalar_ring = ctx.enter_context(tc.tile_pool(name="scalar_ring", bufs=SCALAR_RING))
-        banks = ctx.enter_context(tc.psum_pool(name="banks", bufs=8))
+        banks = ctx.enter_context(tc.psum_pool(name="banks", bufs=PSUM_BANKS))
 
         def held(name, shape, dtype):
             return keep.tile(shape, dtype, name=name, align_bytes=64)
 
         def fresh(ring, name, shape, dtype):
             return ring.tile(shape, dtype, name=name, tag="slot", align_bytes=64)
+
+        def next_bank(name, shape):
+            return banks.tile(shape, F32, name=name, tag="bank")
 
         list_v = keep.tile([P, S // 16], U16, name="list_v")
         list_v2 = keep.tile([P, S // 16], U16, name="list_v2")
@@ -57,34 +65,59 @@ def tile_list_complex_relation_embedding_kernel(
             nc.vector.memset(plane[:], 0)
 
         ident = held("ident", [P, P], F32)
+        make_identity(nc, ident[:])
 
         def load_words(name, shape, dtype, source):
             tile = held(name, shape, dtype)
             nc.sync.dma_start(out=tile[:].bitcast(I32), in_=source.bitcast(I32))
             return tile
 
-        def load_plane(queue, plane, scales):
+        def load_planes(plane, scales):
             for r in range(4):
-                queue.dma_start(
+                nc.sync.dma_start(
                     out=plane[r:P:32, :, :], in_=scales[:, r:16:4, :].rearrange("a q c -> q a c").bitcast(I32)
                 )
 
-        def load_wo_planes(queue):
-            for q in range(4):
-                queue.dma_start(
-                    out=wo_sc[32 * q + 4 : 32 * q + 12, :], in_=wo_scales[:, 4 * q : 4 * q + 4, :].bitcast(I32)
-                )
-
         def load_weight(name, weight, b, a):
-            tile = held(name, [P, PACK, HALF], F32)
+            tile = held("%s%d%d" % (name, b, a), [P, PACK, HALF], F32)
             rows = weight[PASS * a : PASS * (a + 1), HALF * b : HALF * (b + 1)]
             nc.sync.dma_start(out=tile[:], in_=rows.rearrange("(p i) c -> p i c", i=PACK))
-            return tile
+            raw[name, b, a] = tile
 
         def load_gains(n):
             tile = held("gT%d" % n, [P, T], F32)
             nc.sync.dma_start(out=tile[:], in_=gT[P * n : P * (n + 1), :])
             return tile
+
+        raw = {}
+        tab2 = load_words("tab2", [P, T2], U32, tab2_words[0].rearrange("p t i -> p (t i)"))
+        nc.sync.dma_start(list_v2[:], offs2)
+        load_planes(tab2_sc, tab2_scales)
+        nc.sync.dma_start(list_v[:], offs)
+        load_weight("wd", wd, 0, 0)
+        load_planes(tab_sc, tab_scales)
+        tab0 = load_words("tab0", [P, T], U32, tab_words[0].rearrange("p t i -> p (t i)"))
+        load_planes(wb_sc, wb_scales)
+        wb = load_words("wb", [P, 2 * H], U8, wb_words[0])
+        tab1 = load_words("tab1", [P, T], U32, tab_words[1].rearrange("p t i -> p (t i)"))
+        load_planes(wc_sc, wc_scales)
+        wc = load_words("wc", [P, 2, 2 * H], U8, wc_words.rearrange("a p c -> p a c"))
+        for a in range(2):
+            load_weight("wa", wa, 0, a)
+        load_weight("wd", wd, 1, 0)
+        for a in range(2):
+            load_weight("wa", wa, 1, a)
+        for q in range(4):
+            nc.sync.dma_start(
+                out=wo_sc[32 * q + 4 : 32 * q + 12, :], in_=wo_scales[:, 4 * q : 4 * q + 4, :].bitcast(I32)
+            )
+        wo = load_words("wo", [P, 2, N], U32, wo_words.rearrange("a p c i -> p a (c i)"))
+        gains = [load_gains(n) for n in range(OUT_TILES)]
+
+        grouped, quantised = {}, {}
+        sums, factor, term, turned = {}, {}, {}, {}
+        h, h_codes, h_scales = {}, {}, {}
+        y_bank, y, picked_gains, scaled = {}, {}, {}, {}
 
         def pick_words(name, words, offsets):
             codes = fresh(vector_ring, name, [P, S], U32)
@@ -96,63 +129,31 @@ def tile_list_complex_relation_embedding_kernel(
             nc.vector.tensor_copy(out=scales[:], in_=plane[:, a, :].bitcast(U8).indirect(offsets[:]))
             return scales
 
-        def cast(on_vector, name, raw, c):
+        def cast(w, b, a, c, on_vector):
             ring, copy = (vector_ring, nc.vector.tensor_copy) if on_vector else (scalar_ring, nc.scalar.copy)
-            grouped = fresh(ring, name, [P, PART, PACK], BF16)
+            tile = fresh(ring, "cast_%s%d%d%d" % (w, b, a, c), [P, PART, PACK], BF16)
             copy(
-                out=grouped[:].rearrange("p (c e) i -> p c i e", e=4),
-                in_=raw[:, :, PART * c : PART * (c + 1)].rearrange("p i (c e) -> p c i e", e=4),
+                out=tile[:].rearrange("p (c e) i -> p c i e", e=4),
+                in_=raw[w, b, a][:, :, PART * c : PART * (c + 1)].rearrange("p i (c e) -> p c i e", e=4),
             )
-            return grouped
+            grouped[w, b, a, c] = tile
 
-        def quantise(name, grouped):
-            codes = fresh(vector_ring, name + "_codes", [P, PART], U32)
-            scales = held(name + "_scales", [P, PART], U8)
+        def cast_shared(w, b, a):
+            for c in range(2):
+                cast(w, b, a, c, on_vector=(c == 0))
+
+        def quantise_part(codes, scales, c, source):
+            cols = slice(PART * c, PART * (c + 1))
             nc.vector.quantize_mx(
-                out=codes[:].bitcast(FP8X4), scales=scales[:], in_=grouped[:].rearrange("p c i -> p (c i)")
-            )
-            return codes[:].bitcast(FP8X4), scales[:]
-
-        def quantise_half(name, parts):
-            codes = fresh(vector_ring, name + "_codes", [P, HALF], U32)
-            scales = held(name + "_scales", [P, HALF], U8)
-            for c, grouped in enumerate(parts):
-                cols = slice(PART * c, PART * (c + 1))
-                nc.vector.quantize_mx(
-                    out=codes[:, cols].bitcast(FP8X4),
-                    scales=scales[:, cols],
-                    in_=grouped[:].rearrange("p c i -> p (c i)"),
-                )
-            return codes[:].bitcast(FP8X4), scales[:]
-
-        def one_pass(acc, picked, weight, j, start, stop):
-            tokens = slice(P * j, P * (j + 1))
-            nc.tensor.matmul_mx(
-                out=acc[:],
-                lhsT=picked[0][:, tokens].bitcast(FP8X4),
-                lhsT_scale=picked[1][:, tokens],
-                rhs=weight[0],
-                rhs_scale=weight[1],
-                start=start,
-                stop=stop,
+                out=codes[:, cols].bitcast(FP8X4), scales=scales[:, cols], in_=source[:].rearrange("p c i -> p (c i)")
             )
 
-        def product(picked, weights, j):
-            acc = banks.tile([P, HALF], F32, name="acc", tag="bank")
-            tokens = slice(P * j, P * (j + 1))
-            width = HALF // len(weights)
-            for c, passes in enumerate(weights):
-                for a, (codes, scales) in enumerate(picked):
-                    nc.tensor.matmul_mx(
-                        out=acc[:, width * c : width * (c + 1)],
-                        lhsT=codes[:, tokens].bitcast(FP8X4),
-                        lhsT_scale=scales[:, tokens],
-                        rhs=passes[a][0],
-                        rhs_scale=passes[a][1],
-                        start=(a == 0),
-                        stop=(a == len(picked) - 1),
-                    )
-            return acc[:].rearrange("p (m t) -> p t m", t=PACK)
+        def quantise_weight(w, b, a):
+            codes = fresh(vector_ring, "codes_%s%d%d" % (w, b, a), [P, HALF], U32)
+            scales = held("scales_%s%d%d" % (w, b, a), [P, HALF], U8)
+            for c in range(2):
+                quantise_part(codes, scales, c, grouped[w, b, a, c])
+            quantised[w, b, a] = (codes[:].bitcast(FP8X4), scales[:])
 
         def fp4_half(words, plane, a, b):
             return (
@@ -160,272 +161,207 @@ def tile_list_complex_relation_embedding_kernel(
                 plane[:, a, HALF // 4 * b : HALF // 4 * (b + 1)].bitcast(U8),
             )
 
-        def keep_factor(name, sums, sign):
-            factor = fresh(scalar_ring, name, [P, PACK, P], F32)
-            nc.scalar.activation(out=factor[:], in_=sums, func=COPY, scale=sign)
-            return factor
+        def operands(name, b):
+            if name == "r_re":
+                return [(relations, fp4_half(wb, wb_sc, 0, b))]
+            if name == "r_im":
+                return [(relations, quantised["wd", b, 0])]
+            if name == "s_im":
+                return [(subjects[a], fp4_half(wc[:, a, :], wc_sc, a, b)) for a in range(2)]
+            return [(subjects[a], quantised["wa", b, a]) for a in range(2)]
 
-        def multiply(name, sums, factor):
-            term = fresh(vector_ring, name, [P, PACK, P], F32)
-            nc.vector.tensor_tensor(out=term[:], in0=sums, in1=factor[:], op=MULT)
-            return term
+        def product_pass(name, b, j, a):
+            passes = operands(name, b)
+            if a == 0:
+                sums[name, b, j] = next_bank("acc", [P, HALF])
+            (codes, scales), (weight_codes, weight_scales) = passes[a]
+            tokens = slice(P * j, P * (j + 1))
+            nc.tensor.matmul_mx(
+                out=sums[name, b, j][:],
+                lhsT=codes[:, tokens].bitcast(FP8X4),
+                lhsT_scale=scales[:, tokens],
+                rhs=weight_codes,
+                rhs_scale=weight_scales,
+                start=(a == 0),
+                stop=(a == len(passes) - 1),
+            )
 
-        def turn(term, bank, first):
+        def product(name, b, j):
+            for a in range(len(operands(name, b))):
+                product_pass(name, b, j, a)
+
+        def by_slot(name, b, j):
+            return sums[name, b, j][:].rearrange("p (m t) -> p t m", t=PACK)
+
+        def keep_factor(name, b, j):
+            product(name, b, j)
+            kind = name[2:]
+            factor[kind, b, j] = fresh(scalar_ring, "%s%d%d" % (name, b, j), [P, PACK, P], F32)
+            sign = 1.0 if kind == "re" else -1.0
+            nc.scalar.activation(out=factor[kind, b, j][:], in_=by_slot(name, b, j), func=COPY, scale=sign)
+
+        def multiply(name, b, j):
+            kind = name[2:]
+            term[kind, b, j] = fresh(vector_ring, "%s%d%d" % (kind, b, j), [P, PACK, P], F32)
+            nc.vector.tensor_tensor(
+                out=term[kind, b, j][:], in0=by_slot(name, b, j), in1=factor[kind, b, j][:], op=MULT
+            )
+
+        def turn(kind, b, j):
+            first = kind == "im"
+            if first:
+                turned[b, j] = next_bank("turned", [P, PACK, P])
             for t in range(PACK):
                 nc.tensor.matmul(
-                    out=bank[:, t, :], lhsT=term[:, t, :], rhs=ident[:],
+                    out=turned[b, j][:, t, :], lhsT=term[kind, b, j][:, t, :], rhs=ident[:],
                     start=(first and t == 0), stop=(not first and t == PACK - 1), is_transpose=True,
                 )
 
-        def project(n, c0, c1):
-            acc = banks.tile([P, S], F32, name="acc", tag="bank")
-            for c in range(c0, c1):
-                for b in (1, 0):
-                    codes, scales = h_codes[b, c]
-                    nc.tensor.matmul_mx(
-                        out=acc[:, PART * c : PART * (c + 1)],
-                        lhsT=wo[:, b, P * n : P * (n + 1)].bitcast(FP8X4),
-                        lhsT_scale=wo_sc[4 * (b + 1) :, P // 4 * n : P // 4 * (n + 1)].bitcast(U8),
-                        rhs=codes,
-                        rhs_scale=scales,
-                        start=(b == 1),
-                        stop=(b == 0),
-                    )
-            if n in picked_gains:
-                y[n, c0] = acc
-            else:
-                y[n, c0] = fresh(scalar_ring, "y%d%d" % (n, c0), [P, PART * (c1 - c0)], F32)
-                nc.scalar.copy(out=y[n, c0][:], in_=acc[:, PART * c0 : PART * c1])
-
-        def pick_gains(n):
-            picked_gains[n] = fresh(vector_ring, "picked_gains%d" % n, [P, S], F32)
-            nc.vector.tensor_copy(out=picked_gains[n][:], in_=gains[n][:].indirect(list_v[:]))
-
-        def scale_from_psum(n, c0, c1):
-            if c0 == 0:
-                scaled[n] = fresh(vector_ring, "scaled%d" % n, [P, S], F32)
-            cols = slice(PART * c0, PART * c1)
-            nc.vector.tensor_tensor(
-                out=scaled[n][:, cols], in0=y_bank[n, c0][:, cols], in1=picked_gains[n][:, cols], op=MULT
-            )
-            if c1 == 2:
-                nc.sync.dma_start(out=out[P * n : P * (n + 1), :], in_=scaled[n][:])
-
-        def scale_and_store(n, c0, c1):
-            if c0 == 0:
-                scaled[n] = fresh(vector_ring, "scaled%d" % n, [P, S], F32)
-            offsets = list_v[:, PART // 16 * c0 : PART // 16 * c1]
-            nc.vector.tensor_tensor(
-                out=scaled[n][:, PART * c0 : PART * c1], in0=gains[n][:].indirect(offsets), in1=y[n, c0][:], op=MULT
-            )
-            if c1 == 2:
-                nc.sync.dma_start(out=out[P * n : P * (n + 1), :], in_=scaled[n][:])
-
-        picked_gains, h_scales, y_bank = {}, {}, {}
-        y, scaled, opened = {}, {}, {}
-        raw, grouped, quant, r_re, r_im, im, re, bank, h, h_codes, sums = {}, {}, {}, {}, {}, {}, {}, {}, {}, {}, {}
-
-        def cast_part(on_vector, w, b, a, c):
-            grouped[w, b, a, c] = cast(on_vector, "cast_%s%d%d%d" % (w, b, a, c), raw[w, b, a], c)
-
-        def quant_part(w, b, a, c):
-            quant[w, b, a, c] = quantise("q_%s%d%d%d" % (w, b, a, c), grouped[w, b, a, c])
-
-        def keep_r_im(b, j):
-            sums = product(relations, [[quant["wd", b, 0]]], j)
-            r_im[b, j] = keep_factor("r_im%d%d" % (b, j), sums, -1.0)
-
-        def keep_r_re(b, j):
-            sums = product(relations, [[fp4_half(wb, wb_sc, 0, b)]], j)
-            r_re[b, j] = keep_factor("r_re%d%d" % (b, j), sums, 1.0)
-
-        def s_im(b, j):
-            sums["im", b, j] = product(subjects, [[fp4_half(wc[:, a, :], wc_sc, a, b) for a in range(2)]], j)
-
-        def s_re(b, j):
-            sums["re", b, j] = product(subjects, [[quant["wa", b, a] for a in range(2)]], j)
-
-        def s_re_open(b, j):
-            opened[b, j] = banks.tile([P, HALF], F32, name="acc", tag="bank")
-            one_pass(opened[b, j], subjects[0], quant["wa", b, 0], j, True, False)
-
-        def s_re_close(b, j):
-            one_pass(opened[b, j], subjects[1], quant["wa", b, 1], j, False, True)
-            sums["re", b, j] = opened[b, j][:].rearrange("p (m t) -> p t m", t=PACK)
-
-        def im_term(b, j):
-            im[b, j] = multiply("im%d%d" % (b, j), sums["im", b, j], r_im[b, j])
-
-        def re_term(b, j):
-            re[b, j] = multiply("re%d%d" % (b, j), sums["re", b, j], r_re[b, j])
-
-        def turn_im(b, j):
-            bank[b, j] = banks.tile([P, PACK, P], F32, name="turned", tag="bank")
-            turn(im[b, j], bank[b, j], True)
-
-        def turn_re(b, j):
-            turn(re[b, j], bank[b, j], False)
-
         def round_h(b, j):
-            if j % 2 == 0:
-                h[b, j // 2] = fresh(scalar_ring, "h%d%d" % (b, j // 2), [P, PART, PACK], BF16)
+            c, side = divmod(j, 2)
+            if side == 0:
+                h[b, c] = fresh(scalar_ring, "h%d%d" % (b, c), [P, PART, PACK], BF16)
             nc.scalar.copy(
-                out=h[b, j // 2][:, P * (j % 2) : P * (j % 2 + 1), :], in_=bank[b, j][:].rearrange("p t j -> p j t")
+                out=h[b, c][:, P * side : P * (side + 1), :], in_=turned[b, j][:].rearrange("p t j -> p j t")
             )
 
-        def quant_h(b, c):
+        def quantise_h(b, c):
             if c == 0:
                 h_codes[b] = fresh(vector_ring, "h_codes%d" % b, [P, S], U32)
                 h_scales[b] = held("h_scales%d" % b, [P, S], U8)
-            cols = slice(PART * c, PART * (c + 1))
-            nc.vector.quantize_mx(
-                out=h_codes[b][:, cols].bitcast(FP8X4),
-                scales=h_scales[b][:, cols],
-                in_=h[b, c][:].rearrange("p c i -> p (c i)"),
-            )
+            quantise_part(h_codes[b], h_scales[b], c, h[b, c])
 
-        def y_pass(n, b, c0=0, c1=2):
+        def y_pass(n, b, entries):
             if b == 0:
-                y_bank[n, c0] = banks.tile([P, S], F32, name="acc", tag="bank")
-            cols = slice(PART * c0, PART * c1)
+                y_bank[n, entries.start] = next_bank("acc", [P, S])
             nc.tensor.matmul_mx(
-                out=y_bank[n, c0][:, cols],
+                out=y_bank[n, entries.start][:, entries],
                 lhsT=wo[:, b, P * n : P * (n + 1)].bitcast(FP8X4),
                 lhsT_scale=wo_sc[4 * (b + 1) :, P // 4 * n : P // 4 * (n + 1)].bitcast(U8),
-                rhs=h_codes[b][:, cols].bitcast(FP8X4),
-                rhs_scale=h_scales[b][:, cols],
+                rhs=h_codes[b][:, entries].bitcast(FP8X4),
+                rhs_scale=h_scales[b][:, entries],
                 start=(b == 0),
                 stop=(b == 1),
             )
 
         def keep_y(n):
-            y[n, 0] = fresh(scalar_ring, "y%d" % n, [P, S], F32)
-            nc.scalar.copy(out=y[n, 0][:], in_=y_bank[n, 0][:])
+            y[n] = fresh(scalar_ring, "y%d" % n, [P, S], F32)
+            nc.scalar.copy(out=y[n][:], in_=y_bank[n, 0][:])
 
-        make_identity(nc, ident[:])
-        nc.sync.dma_start(list_v2[:], offs2)
-        tab2 = load_words("tab2", [P, T2], U32, tab2_words[0].rearrange("p t i -> p (t i)"))
-        load_plane(nc.sync, tab2_sc, tab2_scales)
-        nc.sync.dma_start(list_v[:], offs)
-        raw["wd", 0, 0] = load_weight("wd0", wd, 0, 0)
-        load_plane(nc.sync, tab_sc, tab_scales)
-        tab0 = load_words("tab0", [P, T], U32, tab_words[0].rearrange("p t i -> p (t i)"))
-        load_plane(nc.sync, wb_sc, wb_scales)
-        wb = load_words("wb", [P, 2 * H], U8, wb_words[0])
-        tab1 = load_words("tab1", [P, T], U32, tab_words[1].rearrange("p t i -> p (t i)"))
-        load_plane(nc.sync, wc_sc, wc_scales)
-        wc = load_words("wc", [P, 2, 2 * H], U8, wc_words.rearrange("a p c -> p a c"))
-        raw["wa", 0, 0] = load_weight("wa00", wa, 0, 0)
-        raw["wa", 0, 1] = load_weight("wa01", wa, 0, 1)
-        raw["wd", 1, 0] = load_weight("wd1", wd, 1, 0)
-        raw["wa", 1, 0] = load_weight("wa10", wa, 1, 0)
-        raw["wa", 1, 1] = load_weight("wa11", wa, 1, 1)
-        load_wo_planes(nc.sync)
-        wo = load_words("wo", [P, 2, N], U32, wo_words.rearrange("a p c i -> p a (c i)"))
-        gains = [load_gains(n) for n in range(N // P)]
+        def pick_gains(n):
+            picked_gains[n] = fresh(vector_ring, "picked_gains%d" % n, [P, S], F32)
+            nc.vector.tensor_copy(out=picked_gains[n][:], in_=gains[n][:].indirect(list_v[:]))
 
-        def keep_s_im(b, j):
-            s_im(b, j)
-            r_im[b, j] = keep_factor("s_im%d%d" % (b, j), sums["im", b, j], -1.0)
+        def scale_from_psum(n, entries):
+            if entries.start == 0:
+                scaled[n] = fresh(vector_ring, "scaled%d" % n, [P, S], F32)
+            nc.vector.tensor_tensor(
+                out=scaled[n][:, entries],
+                in0=y_bank[n, entries.start][:, entries],
+                in1=picked_gains[n][:, entries],
+                op=MULT,
+            )
+            if entries.stop == S:
+                nc.sync.dma_start(out=out[P * n : P * (n + 1), :], in_=scaled[n][:])
 
-        def late_r_im(b, j):
-            sums["im", b, j] = product(relations, [[quant["wd", b, 0]]], j)
+        def gather_scale_store(n, entries):
+            piece = fresh(vector_ring, "scaled%d_%d" % (n, entries.start), [P, entries.stop - entries.start], F32)
+            offsets = list_v[:, entries.start // 16 : entries.stop // 16]
+            nc.vector.tensor_tensor(out=piece[:], in0=gains[n][:].indirect(offsets), in1=y[n][:, entries], op=MULT)
+            nc.sync.dma_start(out=out[P * n : P * (n + 1), entries], in_=piece[:])
 
-        def turn_both(b, j):
-            bank[b, j] = banks.tile([P, PACK, P], F32, name="turned", tag="bank")
-            turn(re[b, j], bank[b, j], True)
-            turn(im[b, j], bank[b, j], False)
-
-        def quant_both(w, b, a):
-            quant[w, b, a] = quantise_half("q_%s%d%d" % (w, b, a), [grouped[w, b, a, c] for c in range(2)])
-
-        def cast_both(on_vector, w, b, a):
-            for c in range(2):
-                cast_part(on_vector[c], w, b, a, c)
-
-        relations = [(pick_words("v2_codes", tab2, list_v2), pick_scales("v2_scales", tab2_sc, 0, list_v2))]
-        cast_both((True, False), "wd", 0, 0)
-        scales = [pick_scales("v_scales0", tab_sc, 0, list_v)]
-        quant_both("wd", 0, 0)
-        words = [pick_words("v_codes0", tab0, list_v)]
-        scales.append(pick_scales("v_scales1", tab_sc, 1, list_v))
-        words.append(pick_words("v_codes1", tab1, list_v))
-        subjects = list(zip(words, scales))
+        relations = (pick_words("v2_codes", tab2, list_v2), pick_scales("v2_scales", tab2_sc, 0, list_v2))
+        cast_shared("wd", 0, 0)
+        quantise_weight("wd", 0, 0)
+        scales0 = pick_scales("v_scales0", tab_sc, 0, list_v)
+        words0 = pick_words("v_codes0", tab0, list_v)
+        scales1 = pick_scales("v_scales1", tab_sc, 1, list_v)
+        words1 = pick_words("v_codes1", tab1, list_v)
+        subjects = ((words0, scales0), (words1, scales1))
         for j in range(TILES):
-            keep_r_im(0, j)
+            keep_factor("r_im", 0, j)
         for b in range(2):
             for j in range(TILES):
-                keep_r_re(b, j)
+                keep_factor("r_re", b, j)
+
         for j in range(TILES):
-            s_im(0, j)
-        cast_part(False, "wa", 0, 0, 1)
+            product("s_im", 0, j)
+        cast("wa", 0, 0, 1, on_vector=False)
         for j in range(TILES):
-            im_term(0, j)
-        cast_part(True, "wa", 0, 0, 0)
-        quant_both("wa", 0, 0)
-        for pair in ((0, 1), (2, 3)):
+            multiply("s_im", 0, j)
+        cast("wa", 0, 0, 0, on_vector=True)
+        quantise_weight("wa", 0, 0)
+        for pair in PAIRS:
             for j in pair:
-                keep_s_im(1, j)
+                keep_factor("s_im", 1, j)
             for j in pair:
-                turn_im(0, j)
-        cast_both((True, True), "wa", 0, 1)
-        quant_both("wa", 0, 1)
-        cast_both((True, False), "wd", 1, 0)
+                turn("im", 0, j)
+
+        for c in range(2):
+            cast("wa", 0, 1, c, on_vector=True)
+        quantise_weight("wa", 0, 1)
+        cast_shared("wd", 1, 0)
         for j in range(TILES):
-            s_re(0, j)
-        cast_both((False, False), "wa", 1, 0)
-        for j in range(TILES):
-            re_term(0, j)
-            if j == 1:
-                quant_both("wd", 1, 0)
-        for pair in ((0, 1), (2, 3)):
+            product("s_re", 0, j)
+        for c in range(2):
+            cast("wa", 1, 0, c, on_vector=False)
+        for j in PAIRS[0]:
+            multiply("s_re", 0, j)
+        quantise_weight("wd", 1, 0)
+        for j in PAIRS[1]:
+            multiply("s_re", 0, j)
+        for pair in PAIRS:
             for j in pair:
-                late_r_im(1, j)
+                product("r_im", 1, j)
             for j in pair:
-                turn_re(0, j)
-        im_term(1, 0)
-        cast_both((True, False), "wa", 1, 1)
-        quant_both("wa", 1, 0)
-        im_term(1, 1)
-        quant_both("wa", 1, 1)
+                turn("re", 0, j)
+
+        multiply("r_im", 1, 0)
+        cast_shared("wa", 1, 1)
+        quantise_weight("wa", 1, 0)
+        multiply("r_im", 1, 1)
+        quantise_weight("wa", 1, 1)
         for j in range(TILES):
             round_h(0, j)
-        for j in (2, 3):
-            im_term(1, j)
-        for j in range(TILES):
-            s_re_open(1, j)
-        for j in range(TILES):
-            s_re_close(1, j)
-        for pair in ((0, 1), (2, 3)):
+        for j in PAIRS[1]:
+            multiply("r_im", 1, j)
+        for a in range(2):
+            for j in range(TILES):
+                product_pass("s_re", 1, j, a)
+        for pair in PAIRS:
             for j in pair:
-                turn_im(1, j)
+                turn("im", 1, j)
             for j in pair:
-                re_term(1, j)
-                turn_re(1, j)
+                multiply("s_re", 1, j)
+                turn("re", 1, j)
                 round_h(1, j)
         for c in range(2):
-            quant_h(0, c)
-        for n in (2, 3):
-            y_pass(n, 0)
-        pick_gains(0)
-        quant_h(1, 0)
-        pick_gains(1)
-        for n in (0, 1):
+            quantise_h(0, c)
+
+        ahead, opened, rest = (0, 1), (2, 3), range(4, OUT_TILES)
+        for n in opened:
+            y_pass(n, 0, WHOLE_LIST)
+        pick_gains(ahead[0])
+        quantise_h(1, 0)
+        pick_gains(ahead[1])
+        for n in ahead:
             for b in range(2):
-                y_pass(n, b, 0, 1)
-        quant_h(1, 1)
-        for n in (0, 1):
-            scale_from_psum(n, 0, 1)
-        for n in (0, 1):
-            y_pass(n + 2, 1)
-            keep_y(n + 2)
+                y_pass(n, b, LIST_PARTS[0])
+        quantise_h(1, 1)
+        for n in ahead:
+            scale_from_psum(n, LIST_PARTS[0])
+        for n, later in zip(ahead, opened):
             for b in range(2):
-                y_pass(n, b, 1, 2)
-        for n in (4, 5):
+                y_pass(n, b, LIST_PARTS[1])
+            y_pass(later, 1, WHOLE_LIST)
+            keep_y(later)
+        for n in rest:
             for b in range(2):
-                y_pass(n, b)
+                y_pass(n, b, WHOLE_LIST)
             keep_y(n)
-        for n in (0, 1):
-            scale_from_psum(n, 1, 2)
-        for n in range(2, N // P):
-            scale_and_store(n, 0, 2)
+        for n in ahead:
+            scale_from_psum(n, LIST_PARTS[1])
+        for n in range(len(ahead), OUT_TILES - 1):
+            gather_scale_store(n, WHOLE_LIST)
+        gather_scale_store(OUT_TILES - 1, slice(0, S - P))
+        gather_scale_store(OUT_TILES - 1, slice(S - P, S))

@@ -26,7 +26,7 @@ TILES = S // P
 PAIRS = ((0, 1), (2, 3))
 OUT_TILES = N // P
 WHOLE_LIST = slice(0, S)
-LIST_PARTS = (slice(0, PART), slice(PART, S))
+PASSES = {"s_re": K // PASS, "s_im": K // PASS, "r_re": L // PASS, "r_im": L // PASS}
 
 VECTOR_RING = 22
 SCALAR_RING = 24
@@ -78,11 +78,12 @@ def tile_list_complex_relation_embedding_kernel(
                     out=plane[r:P:32, :, :], in_=scales[:, r:16:4, :].rearrange("a q c -> q a c").bitcast(I32)
                 )
 
-        def load_weight(name, weight, b, a):
-            tile = held("%s%d%d" % (name, b, a), [P, PACK, HALF], F32)
-            rows = weight[PASS * a : PASS * (a + 1), HALF * b : HALF * (b + 1)]
+        def load_weight(name, weight, a, halves):
+            tile = held("%s%d%d" % (name, a, halves.start), [P, PACK, HALF * len(halves)], F32)
+            rows = weight[PASS * a : PASS * (a + 1), HALF * halves.start : HALF * halves.stop]
             nc.sync.dma_start(out=tile[:], in_=rows.rearrange("(p i) c -> p i c", i=PACK))
-            raw[name, b, a] = tile
+            for b in halves:
+                raw[name, b, a] = tile[:, :, HALF * (b - halves.start) : HALF * (b - halves.start + 1)]
 
         def load_gains(n):
             tile = held("gT%d" % n, [P, T], F32)
@@ -94,7 +95,7 @@ def tile_list_complex_relation_embedding_kernel(
         nc.sync.dma_start(list_v2[:], offs2)
         load_planes(tab2_sc, tab2_scales)
         nc.sync.dma_start(list_v[:], offs)
-        load_weight("wd", wd, 0, 0)
+        load_weight("wd", wd, 0, range(2))
         load_planes(tab_sc, tab_scales)
         tab0 = load_words("tab0", [P, T], U32, tab_words[0].rearrange("p t i -> p (t i)"))
         load_planes(wb_sc, wb_scales)
@@ -102,17 +103,16 @@ def tile_list_complex_relation_embedding_kernel(
         tab1 = load_words("tab1", [P, T], U32, tab_words[1].rearrange("p t i -> p (t i)"))
         load_planes(wc_sc, wc_scales)
         wc = load_words("wc", [P, 2, 2 * H], U8, wc_words.rearrange("a p c -> p a c"))
-        for a in range(2):
-            load_weight("wa", wa, 0, a)
-        load_weight("wd", wd, 1, 0)
-        for a in range(2):
-            load_weight("wa", wa, 1, a)
+        load_weight("wa", wa, 0, range(2))
+        load_weight("wa", wa, 1, range(0, 1))
+        load_weight("wa", wa, 1, range(1, 2))
+        gains = [load_gains(n) for n in range(2)]
         for q in range(4):
             nc.sync.dma_start(
                 out=wo_sc[32 * q + 4 : 32 * q + 12, :], in_=wo_scales[:, 4 * q : 4 * q + 4, :].bitcast(I32)
             )
         wo = load_words("wo", [P, 2, N], U32, wo_words.rearrange("a p c i -> p a (c i)"))
-        gains = [load_gains(n) for n in range(OUT_TILES)]
+        gains.extend(load_gains(n) for n in range(2, OUT_TILES))
 
         grouped, quantised = {}, {}
         sums, factor, term, turned = {}, {}, {}, {}
@@ -161,20 +161,19 @@ def tile_list_complex_relation_embedding_kernel(
                 plane[:, a, HALF // 4 * b : HALF // 4 * (b + 1)].bitcast(U8),
             )
 
-        def operands(name, b):
+        def operands(name, b, a):
             if name == "r_re":
-                return [(relations, fp4_half(wb, wb_sc, 0, b))]
+                return relations, fp4_half(wb, wb_sc, 0, b)
             if name == "r_im":
-                return [(relations, quantised["wd", b, 0])]
+                return relations, quantised["wd", b, 0]
             if name == "s_im":
-                return [(subjects[a], fp4_half(wc[:, a, :], wc_sc, a, b)) for a in range(2)]
-            return [(subjects[a], quantised["wa", b, a]) for a in range(2)]
+                return subjects[a], fp4_half(wc[:, a, :], wc_sc, a, b)
+            return subjects[a], quantised["wa", b, a]
 
         def product_pass(name, b, j, a):
-            passes = operands(name, b)
             if a == 0:
                 sums[name, b, j] = next_bank("acc", [P, HALF])
-            (codes, scales), (weight_codes, weight_scales) = passes[a]
+            (codes, scales), (weight_codes, weight_scales) = operands(name, b, a)
             tokens = slice(P * j, P * (j + 1))
             nc.tensor.matmul_mx(
                 out=sums[name, b, j][:],
@@ -183,11 +182,11 @@ def tile_list_complex_relation_embedding_kernel(
                 rhs=weight_codes,
                 rhs_scale=weight_scales,
                 start=(a == 0),
-                stop=(a == len(passes) - 1),
+                stop=(a == PASSES[name] - 1),
             )
 
         def product(name, b, j):
-            for a in range(len(operands(name, b))):
+            for a in range(PASSES[name]):
                 product_pass(name, b, j, a)
 
         def by_slot(name, b, j):
@@ -271,96 +270,78 @@ def tile_list_complex_relation_embedding_kernel(
             nc.sync.dma_start(out=out[P * n : P * (n + 1), entries], in_=piece[:])
 
         relations = (pick_words("v2_codes", tab2, list_v2), pick_scales("v2_scales", tab2_sc, 0, list_v2))
-        cast_shared("wd", 0, 0)
-        quantise_weight("wd", 0, 0)
+        for b in range(2):
+            cast_shared("wd", b, 0)
+        for b in range(2):
+            quantise_weight("wd", b, 0)
         scales0 = pick_scales("v_scales0", tab_sc, 0, list_v)
-        words0 = pick_words("v_codes0", tab0, list_v)
         scales1 = pick_scales("v_scales1", tab_sc, 1, list_v)
+        words0 = pick_words("v_codes0", tab0, list_v)
         words1 = pick_words("v_codes1", tab1, list_v)
         subjects = ((words0, scales0), (words1, scales1))
-        for j in range(TILES):
-            keep_factor("r_im", 0, j)
+        for name in ("r_im", "r_re"):
+            for b in range(2):
+                for j in range(TILES):
+                    keep_factor(name, b, j)
+
         for b in range(2):
             for j in range(TILES):
-                keep_factor("r_re", b, j)
+                product("s_im", b, j)
+                multiply("s_im", b, j)
 
         for j in range(TILES):
-            product("s_im", 0, j)
-        cast("wa", 0, 0, 1, on_vector=False)
-        for j in range(TILES):
-            multiply("s_im", 0, j)
-        cast("wa", 0, 0, 0, on_vector=True)
+            turn("im", 0, j)
+        cast_shared("wa", 0, 0)
         quantise_weight("wa", 0, 0)
-        for pair in PAIRS:
-            for j in pair:
-                keep_factor("s_im", 1, j)
-            for j in pair:
-                turn("im", 0, j)
-
-        for c in range(2):
-            cast("wa", 0, 1, c, on_vector=True)
+        for j in range(TILES):
+            product_pass("s_re", 0, j, 0)
+        cast("wa", 1, 0, 1, on_vector=False)
+        cast_shared("wa", 0, 1)
+        cast("wa", 1, 0, 0, on_vector=True)
         quantise_weight("wa", 0, 1)
-        cast_shared("wd", 1, 0)
         for j in range(TILES):
-            product("s_re", 0, j)
-        for c in range(2):
-            cast("wa", 1, 0, c, on_vector=False)
-        for j in PAIRS[0]:
-            multiply("s_re", 0, j)
-        quantise_weight("wd", 1, 0)
-        for j in PAIRS[1]:
-            multiply("s_re", 0, j)
-        for pair in PAIRS:
-            for j in pair:
-                product("r_im", 1, j)
-            for j in pair:
-                turn("re", 0, j)
-
-        multiply("r_im", 1, 0)
-        cast_shared("wa", 1, 1)
+            product_pass("s_re", 0, j, 1)
         quantise_weight("wa", 1, 0)
-        multiply("r_im", 1, 1)
-        quantise_weight("wa", 1, 1)
-        for j in range(TILES):
-            round_h(0, j)
-        for j in PAIRS[1]:
-            multiply("r_im", 1, j)
-        for a in range(2):
-            for j in range(TILES):
-                product_pass("s_re", 1, j, a)
         for pair in PAIRS:
             for j in pair:
+                multiply("s_re", 0, j)
+                turn("re", 0, j)
                 turn("im", 1, j)
+            if pair == PAIRS[0]:
+                cast_shared("wa", 1, 1)
             for j in pair:
-                multiply("s_re", 1, j)
-                turn("re", 1, j)
-                round_h(1, j)
+                round_h(0, j)
+            if pair == PAIRS[0]:
+                for j in pair:
+                    product_pass("s_re", 1, j, 0)
+        quantise_weight("wa", 1, 1)
+        for j in PAIRS[0]:
+            product_pass("s_re", 1, j, 1)
+        for j in PAIRS[1]:
+            product("s_re", 1, j)
+        pick_gains(0)
+        for j in range(TILES):
+            multiply("s_re", 1, j)
+            turn("re", 1, j)
+            round_h(1, j)
         for c in range(2):
             quantise_h(0, c)
 
-        ahead, opened, rest = (0, 1), (2, 3), range(4, OUT_TILES)
+        ahead, opened = range(3), range(TILES)
         for n in opened:
             y_pass(n, 0, WHOLE_LIST)
-        pick_gains(ahead[0])
-        quantise_h(1, 0)
-        pick_gains(ahead[1])
-        for n in ahead:
-            for b in range(2):
-                y_pass(n, b, LIST_PARTS[0])
-        quantise_h(1, 1)
-        for n in ahead:
-            scale_from_psum(n, LIST_PARTS[0])
-        for n, later in zip(ahead, opened):
-            for b in range(2):
-                y_pass(n, b, LIST_PARTS[1])
-            y_pass(later, 1, WHOLE_LIST)
-            keep_y(later)
-        for n in rest:
-            for b in range(2):
-                y_pass(n, b, WHOLE_LIST)
-            keep_y(n)
-        for n in ahead:
-            scale_from_psum(n, LIST_PARTS[1])
+        pick_gains(1)
+        for c in range(2):
+            quantise_h(1, c)
+        pick_gains(2)
+        for n in range(OUT_TILES):
+            if n not in opened:
+                y_pass(n, 0, WHOLE_LIST)
+            y_pass(n, 1, WHOLE_LIST)
+            if n in ahead:
+                scale_from_psum(n, WHOLE_LIST)
+            else:
+                keep_y(n)
         for n in range(len(ahead), OUT_TILES - 1):
             gather_scale_store(n, WHOLE_LIST)
         gather_scale_store(OUT_TILES - 1, slice(0, S - P))

@@ -15,6 +15,7 @@ U8 = mybir.dt.uint8
 FP8X4 = mybir.dt.float8_e4m3fn_x4
 FP4X4 = mybir.dt.float4_e2m1fn_x4
 MULT = mybir.AluOpType.mult
+ADD = mybir.AluOpType.add
 COPY = mybir.ActivationFunctionType.Copy
 
 P = 128
@@ -28,8 +29,8 @@ OUT_TILES = N // P
 WHOLE_LIST = slice(0, S)
 PASSES = {"s_re": K // PASS, "s_im": K // PASS, "r_re": L // PASS, "r_im": L // PASS}
 
-VECTOR_RING = 22
-SCALAR_RING = 24
+VECTOR_RING = 21
+SCALAR_RING = 23
 PSUM_BANKS = 8
 
 
@@ -129,18 +130,24 @@ def tile_list_complex_relation_embedding_kernel(
             nc.vector.tensor_copy(out=scales[:], in_=plane[:, a, :].bitcast(U8).indirect(offsets[:]))
             return scales
 
-        def cast(w, b, a, c, on_vector):
-            ring, copy = (vector_ring, nc.vector.tensor_copy) if on_vector else (scalar_ring, nc.scalar.copy)
-            tile = fresh(ring, "cast_%s%d%d%d" % (w, b, a, c), [P, PART, PACK], BF16)
-            copy(
-                out=tile[:].rearrange("p (c e) i -> p c i e", e=4),
-                in_=raw[w, b, a][:, :, PART * c : PART * (c + 1)].rearrange("p i (c e) -> p c i e", e=4),
-            )
+        def cast(w, b, a, c, engine):
+            name, shape = "cast_%s%d%d%d" % (w, b, a, c), [P, PART, PACK]
+            ring = {"vector": vector_ring, "scalar": scalar_ring}.get(engine)
+            tile = fresh(ring, name, shape, BF16) if ring else held(name, shape, BF16)
+            laid = tile[:].rearrange("p (c e) i -> p c i e", e=4)
+            rows = raw[w, b, a][:, :, PART * c : PART * (c + 1)].rearrange("p i (c e) -> p c i e", e=4)
+            if engine == "vector":
+                nc.vector.tensor_copy(out=laid, in_=rows)
+            elif engine == "scalar":
+                nc.scalar.copy(out=laid, in_=rows)
+            else:
+                rows = raw[w, b, a][:, :, PART * c : PART * (c + 1)].rearrange("p i c -> p c i")
+                nc.gpsimd.tensor_scalar(out=tile[:], in0=rows, scalar1=1.0, scalar2=0.0, op0=MULT, op1=ADD)
             grouped[w, b, a, c] = tile
 
         def cast_shared(w, b, a):
-            for c in range(2):
-                cast(w, b, a, c, on_vector=(c == 0))
+            for c, engine in enumerate(("vector", "scalar")):
+                cast(w, b, a, c, engine)
 
         def quantise_part(codes, scales, c, source):
             cols = slice(PART * c, PART * (c + 1))
@@ -291,49 +298,55 @@ def tile_list_complex_relation_embedding_kernel(
 
         for j in range(TILES):
             turn("im", 0, j)
-        cast_shared("wa", 0, 0)
+        cast("wa", 0, 0, 0, "gpsimd")
+        cast("wa", 0, 0, 1, "scalar")
         quantise_weight("wa", 0, 0)
         for j in range(TILES):
             product_pass("s_re", 0, j, 0)
-        cast("wa", 1, 0, 1, on_vector=False)
+        cast("wa", 1, 0, 0, "scalar")
         cast_shared("wa", 0, 1)
-        cast("wa", 1, 0, 0, on_vector=True)
+        cast("wa", 1, 0, 1, "scalar")
         quantise_weight("wa", 0, 1)
         for j in range(TILES):
             product_pass("s_re", 0, j, 1)
-        quantise_weight("wa", 1, 0)
-        for pair in PAIRS:
-            for j in pair:
-                multiply("s_re", 0, j)
-                turn("re", 0, j)
-                turn("im", 1, j)
-            if pair == PAIRS[0]:
-                cast_shared("wa", 1, 1)
-            for j in pair:
-                round_h(0, j)
-            if pair == PAIRS[0]:
-                for j in pair:
-                    product_pass("s_re", 1, j, 0)
-        quantise_weight("wa", 1, 1)
         for j in PAIRS[0]:
-            product_pass("s_re", 1, j, 1)
+            multiply("s_re", 0, j)
+            turn("re", 0, j)
+        cast("wa", 1, 1, 0, "gpsimd")
+        cast("wa", 1, 1, 1, "scalar")
+        for a in range(2):
+            quantise_weight("wa", 1, a)
+            for j in PAIRS[0]:
+                product_pass("s_re", 1, j, a)
+        for j in PAIRS[0]:
+            round_h(0, j)
+        for j, early in zip(PAIRS[1], PAIRS[0]):
+            multiply("s_re", 0, j)
+            turn("re", 0, j)
+            turn("im", 1, early)
+            round_h(0, j)
         for j in PAIRS[1]:
             product("s_re", 1, j)
-        pick_gains(0)
-        for j in range(TILES):
+        for j in PAIRS[0]:
             multiply("s_re", 1, j)
             turn("re", 1, j)
             round_h(1, j)
+        for j in PAIRS[1]:
+            turn("im", 1, j)
         for c in range(2):
             quantise_h(0, c)
+        for j in PAIRS[1]:
+            multiply("s_re", 1, j)
+            turn("re", 1, j)
+            round_h(1, j)
 
-        ahead, opened = range(3), range(TILES)
+        ahead, opened = range(2), range(TILES)
         for n in opened:
             y_pass(n, 0, WHOLE_LIST)
-        pick_gains(1)
+        pick_gains(0)
         for c in range(2):
             quantise_h(1, c)
-        pick_gains(2)
+        pick_gains(1)
         for n in range(OUT_TILES):
             if n not in opened:
                 y_pass(n, 0, WHOLE_LIST)

@@ -29,8 +29,8 @@ OUT_TILES = N // P
 WHOLE_LIST = slice(0, S)
 PASSES = {"s_re": K // PASS, "s_im": K // PASS, "r_re": L // PASS, "r_im": L // PASS}
 
-VECTOR_RING = 21
-SCALAR_RING = 23
+VECTOR_RING = 25
+SCALAR_RING = 20
 PSUM_BANKS = 8
 
 
@@ -59,10 +59,11 @@ def tile_list_complex_relation_embedding_kernel(
 
         tab2_sc = held("tab2_sc", [P, 1, T2 // 4], I32)
         wb_sc = held("wb_sc", [P, 1, H // 4], I32)
-        tab_sc = held("tab_sc", [P, 2, T // 4], I32)
+        tab_sc = held("tab_sc", [P, 1, T // 4], I32)
+        v_sc = held("v_sc", [P, 2, S // 4], I32)
         wc_sc = held("wc_sc", [P, 2, H // 4], I32)
         wo_sc = held("wo_sc", [P, N // 4], I32)
-        for plane in (tab2_sc, tab_sc, wb_sc, wc_sc, wo_sc):
+        for plane in (tab2_sc, tab_sc, v_sc, wb_sc, wc_sc, wo_sc):
             nc.vector.memset(plane[:], 0)
 
         ident = held("ident", [P, P], F32)
@@ -92,21 +93,35 @@ def tile_list_complex_relation_embedding_kernel(
             return tile
 
         raw = {}
-        tab2 = load_words("tab2", [P, T2], U32, tab2_words[0].rearrange("p t i -> p (t i)"))
         nc.sync.dma_start(list_v2[:], offs2)
-        load_planes(tab2_sc, tab2_scales)
+        tab2 = load_words("tab2", [P, T2], U32, tab2_words[0].rearrange("p t i -> p (t i)"))
         nc.sync.dma_start(list_v[:], offs)
+        nc.sync.dma_start(out=tab_sc[0:P:4, 0, :], in_=tab_scales.rearrange("a q c -> (a q) c").bitcast(I32))
+        load_planes(tab2_sc, tab2_scales)
         load_weight("wd", wd, 0, range(2))
-        load_planes(tab_sc, tab_scales)
+        v2_codes = fresh(vector_ring, "v2_codes", [P, S], U32)
+        nc.vector.tensor_copy(out=v2_codes[:], in_=tab2[:].indirect(list_v2[:]))
+        v_rows = fresh(vector_ring, "v_rows", [P, S], U8)
+        nc.vector.tensor_copy(out=v_rows[:], in_=tab_sc[:, 0, :].bitcast(U8).indirect(list_v[:]))
+
+        def place_rows(a, rows):
+            for r in rows:
+                nc.sync.dma_start(
+                    out=v_sc[r:P:32, a, :], in_=v_rows[64 * a + 4 * r : 64 * (a + 1) : 16, :].bitcast(I32)
+                )
+
+        place_rows(0, range(4))
+        place_rows(1, range(2))
         tab0 = load_words("tab0", [P, T], U32, tab_words[0].rearrange("p t i -> p (t i)"))
+        place_rows(1, range(2, 4))
         load_planes(wb_sc, wb_scales)
-        wb = load_words("wb", [P, 2 * H], U8, wb_words[0])
         tab1 = load_words("tab1", [P, T], U32, tab_words[1].rearrange("p t i -> p (t i)"))
+        wb = load_words("wb", [P, 2 * H], U8, wb_words[0])
         load_planes(wc_sc, wc_scales)
         wc = load_words("wc", [P, 2, 2 * H], U8, wc_words.rearrange("a p c -> p a c"))
-        load_weight("wa", wa, 0, range(2))
-        load_weight("wa", wa, 1, range(0, 1))
-        load_weight("wa", wa, 1, range(1, 2))
+        for b in range(2):
+            for a in range(2):
+                load_weight("wa", wa, a, range(b, b + 1))
         gains = [load_gains(n) for n in range(2)]
         for q in range(4):
             nc.sync.dma_start(
@@ -206,6 +221,11 @@ def tile_list_complex_relation_embedding_kernel(
             sign = 1.0 if kind == "re" else -1.0
             nc.scalar.activation(out=factor[kind, b, j][:], in_=by_slot(name, b, j), func=COPY, scale=sign)
 
+        def keep_on_vector(name, b, j):
+            product(name, b, j)
+            factor["re", b, j] = fresh(vector_ring, "%s%d%d" % (name, b, j), [P, PACK, P], F32)
+            nc.vector.tensor_copy(out=factor["re", b, j][:], in_=by_slot(name, b, j))
+
         def multiply(name, b, j):
             kind = name[2:]
             term[kind, b, j] = fresh(vector_ring, "%s%d%d" % (kind, b, j), [P, PACK, P], F32)
@@ -276,74 +296,75 @@ def tile_list_complex_relation_embedding_kernel(
             nc.vector.tensor_tensor(out=piece[:], in0=gains[n][:].indirect(offsets), in1=y[n][:, entries], op=MULT)
             nc.sync.dma_start(out=out[P * n : P * (n + 1), entries], in_=piece[:])
 
-        relations = (pick_words("v2_codes", tab2, list_v2), pick_scales("v2_scales", tab2_sc, 0, list_v2))
+        relations = (v2_codes, pick_scales("v2_scales", tab2_sc, 0, list_v2))
         for b in range(2):
             cast_shared("wd", b, 0)
         for b in range(2):
             quantise_weight("wd", b, 0)
-        scales0 = pick_scales("v_scales0", tab_sc, 0, list_v)
-        scales1 = pick_scales("v_scales1", tab_sc, 1, list_v)
         words0 = pick_words("v_codes0", tab0, list_v)
         words1 = pick_words("v_codes1", tab1, list_v)
-        subjects = ((words0, scales0), (words1, scales1))
-        for name in ("r_im", "r_re"):
-            for b in range(2):
-                for j in range(TILES):
-                    keep_factor(name, b, j)
+        subjects = ((words0, v_sc[:, 0, :].bitcast(U8)), (words1, v_sc[:, 1, :].bitcast(U8)))
+        for b in range(2):
+            for j in range(TILES):
+                keep_factor("r_im", b, j)
+        for b in range(2):
+            for j in range(TILES):
+                if b == 0:
+                    keep_on_vector("r_re", b, j)
+                else:
+                    keep_factor("r_re", b, j)
 
         for b in range(2):
             for j in range(TILES):
                 product("s_im", b, j)
-                multiply("s_im", b, j)
-
+        for c in range(2):
+            cast("wa", 0, 0, c, "scalar")
+        for b, j in [(0, j) for j in range(TILES)] + [(1, j) for j in PAIRS[0]]:
+            multiply("s_im", b, j)
         for j in range(TILES):
             turn("im", 0, j)
-        cast("wa", 0, 0, 0, "gpsimd")
-        cast("wa", 0, 0, 1, "scalar")
-        quantise_weight("wa", 0, 0)
-        for j in range(TILES):
-            product_pass("s_re", 0, j, 0)
-        cast("wa", 1, 0, 0, "scalar")
         cast_shared("wa", 0, 1)
-        cast("wa", 1, 0, 1, "scalar")
-        quantise_weight("wa", 0, 1)
-        for j in range(TILES):
-            product_pass("s_re", 0, j, 1)
-        for j in PAIRS[0]:
-            multiply("s_re", 0, j)
-            turn("re", 0, j)
-        cast("wa", 1, 1, 0, "gpsimd")
-        cast("wa", 1, 1, 1, "scalar")
         for a in range(2):
-            quantise_weight("wa", 1, a)
+            quantise_weight("wa", 0, a)
+            multiply("s_im", 1, PAIRS[1][a])
             for j in PAIRS[0]:
-                product_pass("s_re", 1, j, a)
-        for j in PAIRS[0]:
-            round_h(0, j)
-        for j, early in zip(PAIRS[1], PAIRS[0]):
+                product_pass("s_re", 0, j, a)
+        for j in PAIRS[1]:
+            product("s_re", 0, j)
+
+        for c in range(2):
+            cast("wa", 1, 0, c, "scalar")
+        for j in range(3):
             multiply("s_re", 0, j)
             turn("re", 0, j)
-            turn("im", 1, early)
+        quantise_weight("wa", 1, 0)
+        for j in range(3):
+            product_pass("s_re", 1, j, 0)
+        cast_shared("wa", 1, 1)
+        for j in range(3):
             round_h(0, j)
-        for j in PAIRS[1]:
-            product("s_re", 1, j)
-        for j in PAIRS[0]:
-            multiply("s_re", 1, j)
-            turn("re", 1, j)
-            round_h(1, j)
-        for j in PAIRS[1]:
-            turn("im", 1, j)
+        turn("im", 1, 0)
+        multiply("s_re", 0, 3)
+        turn("re", 0, 3)
+        round_h(0, 3)
+        turn("im", 1, 1)
+        quantise_weight("wa", 1, 1)
+        for j in range(3):
+            product_pass("s_re", 1, j, 1)
+        product("s_re", 1, 3)
+        pick_gains(0)
+        for pair, later in zip(PAIRS, PAIRS[1]):
+            turn("im", 1, later)
+            for j in pair:
+                multiply("s_re", 1, j)
+                turn("re", 1, j)
+                round_h(1, j)
         for c in range(2):
             quantise_h(0, c)
-        for j in PAIRS[1]:
-            multiply("s_re", 1, j)
-            turn("re", 1, j)
-            round_h(1, j)
 
         ahead, opened = range(2), range(TILES)
         for n in opened:
             y_pass(n, 0, WHOLE_LIST)
-        pick_gains(0)
         for c in range(2):
             quantise_h(1, c)
         pick_gains(1)

@@ -29,8 +29,8 @@ OUT_TILES = N // P
 WHOLE_LIST = slice(0, S)
 PASSES = {"s_re": K // PASS, "s_im": K // PASS, "r_re": L // PASS, "r_im": L // PASS}
 
-VECTOR_RING = 25
-SCALAR_RING = 20
+VECTOR_RING = 27
+SCALAR_RING = 19
 PSUM_BANKS = 8
 
 
@@ -362,12 +362,13 @@ def tile_list_complex_relation_embedding_kernel(
         for c in range(2):
             quantise_h(0, c)
 
-        ahead, opened = range(2), range(TILES)
+        ahead, opened = range(3), range(TILES)
         for n in opened:
             y_pass(n, 0, WHOLE_LIST)
-        for c in range(2):
-            quantise_h(1, c)
         pick_gains(1)
+        quantise_h(1, 0)
+        quantise_h(1, 1)
+        pick_gains(2)
         for n in range(OUT_TILES):
             if n not in opened:
                 y_pass(n, 0, WHOLE_LIST)

@@ -74,8 +74,8 @@ def tile_list_complex_relation_embedding_kernel(
             nc.sync.dma_start(out=tile[:].bitcast(I32), in_=source.bitcast(I32))
             return tile
 
-        def load_planes(plane, scales):
-            for r in range(4):
+        def load_planes(plane, scales, rows):
+            for r in rows:
                 nc.sync.dma_start(
                     out=plane[r:P:32, :, :], in_=scales[:, r:16:4, :].rearrange("a q c -> q a c").bitcast(I32)
                 )
@@ -93,31 +93,31 @@ def tile_list_complex_relation_embedding_kernel(
             return tile
 
         raw = {}
-        nc.sync.dma_start(list_v2[:], offs2)
         tab2 = load_words("tab2", [P, T2], U32, tab2_words[0].rearrange("p t i -> p (t i)"))
+        nc.sync.dma_start(list_v2[:], offs2)
         nc.sync.dma_start(list_v[:], offs)
+        load_planes(tab2_sc, tab2_scales, range(3))
         nc.sync.dma_start(out=tab_sc[0:P:4, 0, :], in_=tab_scales.rearrange("a q c -> (a q) c").bitcast(I32))
-        load_planes(tab2_sc, tab2_scales)
         load_weight("wd", wd, 0, range(2))
-        v2_codes = fresh(vector_ring, "v2_codes", [P, S], U32)
-        nc.vector.tensor_copy(out=v2_codes[:], in_=tab2[:].indirect(list_v2[:]))
+        load_planes(tab2_sc, tab2_scales, range(3, 4))
         v_rows = fresh(vector_ring, "v_rows", [P, S], U8)
         nc.vector.tensor_copy(out=v_rows[:], in_=tab_sc[:, 0, :].bitcast(U8).indirect(list_v[:]))
 
-        def place_rows(a, rows):
-            for r in rows:
+        def place_rows(rows):
+            for a, r in rows:
                 nc.sync.dma_start(
                     out=v_sc[r:P:32, a, :], in_=v_rows[64 * a + 4 * r : 64 * (a + 1) : 16, :].bitcast(I32)
                 )
 
-        place_rows(0, range(4))
-        place_rows(1, range(2))
+        moves = [(a, r) for a in range(2) for r in range(4)]
+        place_rows(moves[:5])
         tab0 = load_words("tab0", [P, T], U32, tab_words[0].rearrange("p t i -> p (t i)"))
-        place_rows(1, range(2, 4))
-        load_planes(wb_sc, wb_scales)
+        place_rows(moves[5:])
+        load_planes(wb_sc, wb_scales, range(3))
         tab1 = load_words("tab1", [P, T], U32, tab_words[1].rearrange("p t i -> p (t i)"))
+        load_planes(wb_sc, wb_scales, range(3, 4))
         wb = load_words("wb", [P, 2 * H], U8, wb_words[0])
-        load_planes(wc_sc, wc_scales)
+        load_planes(wc_sc, wc_scales, range(4))
         wc = load_words("wc", [P, 2, 2 * H], U8, wc_words.rearrange("a p c -> p a c"))
         for b in range(2):
             for a in range(2):
@@ -296,11 +296,12 @@ def tile_list_complex_relation_embedding_kernel(
             nc.vector.tensor_tensor(out=piece[:], in0=gains[n][:].indirect(offsets), in1=y[n][:, entries], op=MULT)
             nc.sync.dma_start(out=out[P * n : P * (n + 1), entries], in_=piece[:])
 
+        v2_codes = pick_words("v2_codes", tab2, list_v2)
+        cast_shared("wd", 0, 0)
         relations = (v2_codes, pick_scales("v2_scales", tab2_sc, 0, list_v2))
-        for b in range(2):
-            cast_shared("wd", b, 0)
-        for b in range(2):
-            quantise_weight("wd", b, 0)
+        quantise_weight("wd", 0, 0)
+        cast_shared("wd", 1, 0)
+        quantise_weight("wd", 1, 0)
         words0 = pick_words("v_codes0", tab0, list_v)
         words1 = pick_words("v_codes1", tab1, list_v)
         subjects = ((words0, v_sc[:, 0, :].bitcast(U8)), (words1, v_sc[:, 1, :].bitcast(U8)))
@@ -366,8 +367,8 @@ def tile_list_complex_relation_embedding_kernel(
         for n in opened:
             y_pass(n, 0, WHOLE_LIST)
         pick_gains(1)
-        quantise_h(1, 0)
-        quantise_h(1, 1)
+        for c in range(2):
+            quantise_h(1, c)
         pick_gains(2)
         for n in range(OUT_TILES):
             if n not in opened:

@@ -15,7 +15,6 @@ U8 = mybir.dt.uint8
 FP8X4 = mybir.dt.float8_e4m3fn_x4
 FP4X4 = mybir.dt.float4_e2m1fn_x4
 MULT = mybir.AluOpType.mult
-ADD = mybir.AluOpType.add
 COPY = mybir.ActivationFunctionType.Copy
 
 P = 128
@@ -24,9 +23,8 @@ PASS = P * PACK
 HALF = 512
 PART = 256
 TILES = S // P
-PAIRS = ((0, 1), (2, 3))
 OUT_TILES = N // P
-WHOLE_LIST = slice(0, S)
+WO_PLANE = 4
 PASSES = {"s_re": K // PASS, "s_im": K // PASS, "r_re": L // PASS, "r_im": L // PASS}
 
 VECTOR_RING = 27
@@ -41,15 +39,17 @@ def tile_list_complex_relation_embedding_kernel(
     nc = tc.nc
     with ExitStack() as ctx:
         keep = ctx.enter_context(tc.tile_pool(name="keep", bufs=1))
-        vector_ring = ctx.enter_context(tc.tile_pool(name="vector_ring", bufs=VECTOR_RING))
-        scalar_ring = ctx.enter_context(tc.tile_pool(name="scalar_ring", bufs=SCALAR_RING))
+        rings = {
+            "vector": ctx.enter_context(tc.tile_pool(name="vector_ring", bufs=VECTOR_RING)),
+            "scalar": ctx.enter_context(tc.tile_pool(name="scalar_ring", bufs=SCALAR_RING)),
+        }
         banks = ctx.enter_context(tc.psum_pool(name="banks", bufs=PSUM_BANKS))
 
         def held(name, shape, dtype):
             return keep.tile(shape, dtype, name=name, align_bytes=64)
 
-        def fresh(ring, name, shape, dtype):
-            return ring.tile(shape, dtype, name=name, tag="slot", align_bytes=64)
+        def fresh(engine, name, shape, dtype):
+            return rings[engine].tile(shape, dtype, name=name, tag="slot", align_bytes=64)
 
         def next_bank(name, shape):
             return banks.tile(shape, F32, name=name, tag="bank")
@@ -59,25 +59,23 @@ def tile_list_complex_relation_embedding_kernel(
 
         tab2_sc = held("tab2_sc", [P, 1, T2 // 4], I32)
         wb_sc = held("wb_sc", [P, 1, H // 4], I32)
-        tab_sc = held("tab_sc", [P, 1, T // 4], I32)
-        v_sc = held("v_sc", [P, 2, S // 4], I32)
         wc_sc = held("wc_sc", [P, 2, H // 4], I32)
-        wo_sc = held("wo_sc", [P, N // 4], I32)
-        for plane in (tab2_sc, tab_sc, v_sc, wb_sc, wc_sc, wo_sc):
+        tab_sc = held("tab_sc", [P, T // 4], I32)
+        v_sc = held("v_sc", [P, 2, S // 4], I32)
+        wo_sc = held("wo_sc", [P, 2, N // 4], I32)
+        for plane in (tab2_sc, tab_sc, wb_sc, v_sc, wc_sc, wo_sc):
             nc.vector.memset(plane[:], 0)
-
-        ident = held("ident", [P, P], F32)
-        make_identity(nc, ident[:])
 
         def load_words(name, shape, dtype, source):
             tile = held(name, shape, dtype)
             nc.sync.dma_start(out=tile[:].bitcast(I32), in_=source.bitcast(I32))
             return tile
 
-        def load_planes(plane, scales, rows):
+        def load_planes(queue, plane, scales, first, rows):
             for r in rows:
-                nc.sync.dma_start(
-                    out=plane[r:P:32, :, :], in_=scales[:, r:16:4, :].rearrange("a q c -> q a c").bitcast(I32)
+                queue.dma_start(
+                    out=plane[first + r : P : 32, :, :],
+                    in_=scales[:, r:16:4, :].rearrange("a q c -> q a c").bitcast(I32),
                 )
 
         def load_weight(name, weight, a, halves):
@@ -92,77 +90,26 @@ def tile_list_complex_relation_embedding_kernel(
             nc.sync.dma_start(out=tile[:], in_=gT[P * n : P * (n + 1), :])
             return tile
 
-        raw = {}
-        tab2 = load_words("tab2", [P, T2], U32, tab2_words[0].rearrange("p t i -> p (t i)"))
-        nc.sync.dma_start(list_v2[:], offs2)
-        nc.sync.dma_start(list_v[:], offs)
-        load_planes(tab2_sc, tab2_scales, range(3))
-        nc.sync.dma_start(out=tab_sc[0:P:4, 0, :], in_=tab_scales.rearrange("a q c -> (a q) c").bitcast(I32))
-        load_weight("wd", wd, 0, range(2))
-        load_planes(tab2_sc, tab2_scales, range(3, 4))
-        v_rows = fresh(vector_ring, "v_rows", [P, S], U8)
-        nc.vector.tensor_copy(out=v_rows[:], in_=tab_sc[:, 0, :].bitcast(U8).indirect(list_v[:]))
-
-        def place_rows(rows):
-            for a, r in rows:
-                nc.sync.dma_start(
-                    out=v_sc[r:P:32, a, :], in_=v_rows[64 * a + 4 * r : 64 * (a + 1) : 16, :].bitcast(I32)
-                )
-
-        moves = [(a, r) for a in range(2) for r in range(4)]
-        place_rows(moves[:5])
-        tab0 = load_words("tab0", [P, T], U32, tab_words[0].rearrange("p t i -> p (t i)"))
-        place_rows(moves[5:])
-        load_planes(wb_sc, wb_scales, range(3))
-        tab1 = load_words("tab1", [P, T], U32, tab_words[1].rearrange("p t i -> p (t i)"))
-        load_planes(wb_sc, wb_scales, range(3, 4))
-        wb = load_words("wb", [P, 2 * H], U8, wb_words[0])
-        load_planes(wc_sc, wc_scales, range(4))
-        wc = load_words("wc", [P, 2, 2 * H], U8, wc_words.rearrange("a p c -> p a c"))
-        for b in range(2):
-            for a in range(2):
-                load_weight("wa", wa, a, range(b, b + 1))
-        gains = [load_gains(n) for n in range(2)]
-        for q in range(4):
-            nc.sync.dma_start(
-                out=wo_sc[32 * q + 4 : 32 * q + 12, :], in_=wo_scales[:, 4 * q : 4 * q + 4, :].bitcast(I32)
-            )
-        wo = load_words("wo", [P, 2, N], U32, wo_words.rearrange("a p c i -> p a (c i)"))
-        gains.extend(load_gains(n) for n in range(2, OUT_TILES))
-
-        grouped, quantised = {}, {}
+        raw, grouped, quantised = {}, {}, {}
         sums, factor, term, turned = {}, {}, {}, {}
         h, h_codes, h_scales = {}, {}, {}
-        y_bank, y, picked_gains, scaled = {}, {}, {}, {}
+        y_bank, y, picked_gains = {}, {}, {}
+        tables = {}
 
-        def pick_words(name, words, offsets):
-            codes = fresh(vector_ring, name, [P, S], U32)
-            nc.vector.tensor_copy(out=codes[:], in_=words[:].indirect(offsets[:]))
-            return codes
-
-        def pick_scales(name, plane, a, offsets):
-            scales = fresh(vector_ring, name, [P, S], U8)
-            nc.vector.tensor_copy(out=scales[:], in_=plane[:, a, :].bitcast(U8).indirect(offsets[:]))
-            return scales
+        def pick(name, dtype, window, offsets):
+            picked = fresh("vector", name, [P, S], dtype)
+            nc.vector.tensor_copy(out=picked[:], in_=window.indirect(offsets[:]))
+            return picked
 
         def cast(w, b, a, c, engine):
-            name, shape = "cast_%s%d%d%d" % (w, b, a, c), [P, PART, PACK]
-            ring = {"vector": vector_ring, "scalar": scalar_ring}.get(engine)
-            tile = fresh(ring, name, shape, BF16) if ring else held(name, shape, BF16)
+            tile = fresh(engine, "cast_%s%d%d%d" % (w, b, a, c), [P, PART, PACK], BF16)
             laid = tile[:].rearrange("p (c e) i -> p c i e", e=4)
             rows = raw[w, b, a][:, :, PART * c : PART * (c + 1)].rearrange("p i (c e) -> p c i e", e=4)
             if engine == "vector":
                 nc.vector.tensor_copy(out=laid, in_=rows)
-            elif engine == "scalar":
-                nc.scalar.copy(out=laid, in_=rows)
             else:
-                rows = raw[w, b, a][:, :, PART * c : PART * (c + 1)].rearrange("p i c -> p c i")
-                nc.gpsimd.tensor_scalar(out=tile[:], in0=rows, scalar1=1.0, scalar2=0.0, op0=MULT, op1=ADD)
+                nc.scalar.copy(out=laid, in_=rows)
             grouped[w, b, a, c] = tile
-
-        def cast_shared(w, b, a):
-            for c, engine in enumerate(("vector", "scalar")):
-                cast(w, b, a, c, engine)
 
         def quantise_part(codes, scales, c, source):
             cols = slice(PART * c, PART * (c + 1))
@@ -171,7 +118,7 @@ def tile_list_complex_relation_embedding_kernel(
             )
 
         def quantise_weight(w, b, a):
-            codes = fresh(vector_ring, "codes_%s%d%d" % (w, b, a), [P, HALF], U32)
+            codes = fresh("vector", "codes_%s%d%d" % (w, b, a), [P, HALF], U32)
             scales = held("scales_%s%d%d" % (w, b, a), [P, HALF], U8)
             for c in range(2):
                 quantise_part(codes, scales, c, grouped[w, b, a, c])
@@ -185,12 +132,12 @@ def tile_list_complex_relation_embedding_kernel(
 
         def operands(name, b, a):
             if name == "r_re":
-                return relations, fp4_half(wb, wb_sc, 0, b)
+                return tables["v2", 0], fp4_half(wb, wb_sc, 0, b)
             if name == "r_im":
-                return relations, quantised["wd", b, 0]
+                return tables["v2", 0], quantised["wd", b, 0]
             if name == "s_im":
-                return subjects[a], fp4_half(wc[:, a, :], wc_sc, a, b)
-            return subjects[a], quantised["wa", b, a]
+                return tables["v", a], fp4_half(wc[:, a, :], wc_sc, a, b)
+            return tables["v", a], quantised["wa", b, a]
 
         def product_pass(name, b, j, a):
             if a == 0:
@@ -214,21 +161,18 @@ def tile_list_complex_relation_embedding_kernel(
         def by_slot(name, b, j):
             return sums[name, b, j][:].rearrange("p (m t) -> p t m", t=PACK)
 
-        def keep_factor(name, b, j):
-            product(name, b, j)
+        def keep_factor(name, b, j, engine):
             kind = name[2:]
-            factor[kind, b, j] = fresh(scalar_ring, "%s%d%d" % (name, b, j), [P, PACK, P], F32)
-            sign = 1.0 if kind == "re" else -1.0
-            nc.scalar.activation(out=factor[kind, b, j][:], in_=by_slot(name, b, j), func=COPY, scale=sign)
-
-        def keep_on_vector(name, b, j):
-            product(name, b, j)
-            factor["re", b, j] = fresh(vector_ring, "%s%d%d" % (name, b, j), [P, PACK, P], F32)
-            nc.vector.tensor_copy(out=factor["re", b, j][:], in_=by_slot(name, b, j))
+            factor[kind, b, j] = fresh(engine, "%s%d%d" % (name, b, j), [P, PACK, P], F32)
+            if engine == "vector":
+                nc.vector.tensor_copy(out=factor[kind, b, j][:], in_=by_slot(name, b, j))
+            else:
+                sign = 1.0 if kind == "re" else -1.0
+                nc.scalar.activation(out=factor[kind, b, j][:], in_=by_slot(name, b, j), func=COPY, scale=sign)
 
         def multiply(name, b, j):
             kind = name[2:]
-            term[kind, b, j] = fresh(vector_ring, "%s%d%d" % (kind, b, j), [P, PACK, P], F32)
+            term[kind, b, j] = fresh("vector", "%s%d%d" % (kind, b, j), [P, PACK, P], F32)
             nc.vector.tensor_tensor(
                 out=term[kind, b, j][:], in0=by_slot(name, b, j), in1=factor[kind, b, j][:], op=MULT
             )
@@ -246,139 +190,175 @@ def tile_list_complex_relation_embedding_kernel(
         def round_h(b, j):
             c, side = divmod(j, 2)
             if side == 0:
-                h[b, c] = fresh(scalar_ring, "h%d%d" % (b, c), [P, PART, PACK], BF16)
+                h[b, c] = fresh("scalar", "h%d%d" % (b, c), [P, PART, PACK], BF16)
             nc.scalar.copy(
                 out=h[b, c][:, P * side : P * (side + 1), :], in_=turned[b, j][:].rearrange("p t j -> p j t")
             )
 
         def quantise_h(b, c):
             if c == 0:
-                h_codes[b] = fresh(vector_ring, "h_codes%d" % b, [P, S], U32)
+                h_codes[b] = fresh("vector", "h_codes%d" % b, [P, S], U32)
                 h_scales[b] = held("h_scales%d" % b, [P, S], U8)
             quantise_part(h_codes[b], h_scales[b], c, h[b, c])
 
-        def y_pass(n, b, entries):
+        def y_pass(n, b):
             if b == 0:
-                y_bank[n, entries.start] = next_bank("acc", [P, S])
+                y_bank[n] = next_bank("acc", [P, S])
             nc.tensor.matmul_mx(
-                out=y_bank[n, entries.start][:, entries],
+                out=y_bank[n][:],
                 lhsT=wo[:, b, P * n : P * (n + 1)].bitcast(FP8X4),
-                lhsT_scale=wo_sc[4 * (b + 1) :, P // 4 * n : P // 4 * (n + 1)].bitcast(U8),
-                rhs=h_codes[b][:, entries].bitcast(FP8X4),
-                rhs_scale=h_scales[b][:, entries],
+                lhsT_scale=wo_sc[WO_PLANE:, b, P // 4 * n : P // 4 * (n + 1)].bitcast(U8),
+                rhs=h_codes[b][:].bitcast(FP8X4),
+                rhs_scale=h_scales[b][:],
                 start=(b == 0),
                 stop=(b == 1),
             )
 
         def keep_y(n):
-            y[n] = fresh(scalar_ring, "y%d" % n, [P, S], F32)
-            nc.scalar.copy(out=y[n][:], in_=y_bank[n, 0][:])
+            y[n] = fresh("scalar", "y%d" % n, [P, S], F32)
+            nc.scalar.copy(out=y[n][:], in_=y_bank[n][:])
 
         def pick_gains(n):
-            picked_gains[n] = fresh(vector_ring, "picked_gains%d" % n, [P, S], F32)
-            nc.vector.tensor_copy(out=picked_gains[n][:], in_=gains[n][:].indirect(list_v[:]))
+            picked_gains[n] = pick("picked_gains%d" % n, F32, gains[n][:], list_v)
 
-        def scale_from_psum(n, entries):
-            if entries.start == 0:
-                scaled[n] = fresh(vector_ring, "scaled%d" % n, [P, S], F32)
-            nc.vector.tensor_tensor(
-                out=scaled[n][:, entries],
-                in0=y_bank[n, entries.start][:, entries],
-                in1=picked_gains[n][:, entries],
-                op=MULT,
-            )
-            if entries.stop == S:
-                nc.sync.dma_start(out=out[P * n : P * (n + 1), :], in_=scaled[n][:])
+        def scale_from_psum(n):
+            scaled = fresh("vector", "scaled%d" % n, [P, S], F32)
+            nc.vector.tensor_tensor(out=scaled[:], in0=y_bank[n][:], in1=picked_gains[n][:], op=MULT)
+            nc.sync.dma_start(out=out[P * n : P * (n + 1), :], in_=scaled[:])
 
         def gather_scale_store(n, entries):
-            piece = fresh(vector_ring, "scaled%d_%d" % (n, entries.start), [P, entries.stop - entries.start], F32)
+            piece = fresh("vector", "scaled%d_%d" % (n, entries.start), [P, entries.stop - entries.start], F32)
             offsets = list_v[:, entries.start // 16 : entries.stop // 16]
             nc.vector.tensor_tensor(out=piece[:], in0=gains[n][:].indirect(offsets), in1=y[n][:, entries], op=MULT)
             nc.sync.dma_start(out=out[P * n : P * (n + 1), entries], in_=piece[:])
 
-        v2_codes = pick_words("v2_codes", tab2, list_v2)
-        cast_shared("wd", 0, 0)
-        relations = (v2_codes, pick_scales("v2_scales", tab2_sc, 0, list_v2))
-        quantise_weight("wd", 0, 0)
-        cast_shared("wd", 1, 0)
-        quantise_weight("wd", 1, 0)
-        words0 = pick_words("v_codes0", tab0, list_v)
-        words1 = pick_words("v_codes1", tab1, list_v)
-        subjects = ((words0, v_sc[:, 0, :].bitcast(U8)), (words1, v_sc[:, 1, :].bitcast(U8)))
+        tab2 = load_words("tab2", [P, T2], U32, tab2_words[0].rearrange("p t i -> p (t i)"))
+        nc.sync.dma_start(list_v2[:], offs2)
+        nc.sync.dma_start(list_v[:], offs)
+        nc.sync.dma_start(out=tab_sc[0:P:4, :], in_=tab_scales.rearrange("a m c -> m a c").bitcast(I32))
+        load_planes(nc.sync, tab2_sc, tab2_scales, 0, range(2))
+        load_planes(nc.gpsimd, tab2_sc, tab2_scales, 0, range(2, 4))
+        load_planes(nc.gpsimd, wb_sc, wb_scales, 0, range(4))
+        ident = held("ident", [P, P], F32)
+        make_identity(nc, ident[:])
+        wb = load_words("wb", [P, 2 * H], U8, wb_words[0])
+        load_weight("wd", wd, 0, range(2))
+        v_rows = pick("v_rows", U8, tab_sc[:].bitcast(U8), list_v)
+        for q in range(4):
+            nc.sync.dma_start(out=v_sc[32 * q : 32 * q + 4, :, :], in_=v_rows[32 * q : 32 * (q + 1) : 4, :].bitcast(I32))
+        tab = [load_words("tab%d" % a, [P, T], U32, tab_words[a].rearrange("p t i -> p (t i)")) for a in range(2)]
+        wc = load_words("wc", [P, 2, 2 * H], U8, wc_words.rearrange("a p c -> p a c"))
+        load_planes(nc.sync, wc_sc, wc_scales, 0, range(4))
         for b in range(2):
-            for j in range(TILES):
-                keep_factor("r_im", b, j)
-        for b in range(2):
-            for j in range(TILES):
-                if b == 0:
-                    keep_on_vector("r_re", b, j)
-                else:
-                    keep_factor("r_re", b, j)
+            for a in range(2):
+                load_weight("wa", wa, a, range(b, b + 1))
+        gains = [load_gains(0)]
+        load_planes(nc.sync, wo_sc, wo_scales, WO_PLANE, range(4))
+        wo = load_words("wo", [P, 2, N], U32, wo_words.rearrange("a p c i -> p a (c i)"))
+        gains.extend(load_gains(n) for n in range(1, OUT_TILES))
 
+        tables["v2", 0] = (
+            pick("v2_codes", U32, tab2[:], list_v2),
+            pick("v2_scales", U8, tab2_sc[:, 0, :].bitcast(U8), list_v2),
+        )
         for b in range(2):
             for j in range(TILES):
-                product("s_im", b, j)
+                product("r_re", b, j)
+        keep_factor("r_re", 0, 0, "vector")
+        keep_factor("r_re", 0, 1, "vector")
+        for b in range(2):
+            cast("wd", b, 0, 1, "scalar")
+        for b in range(2):
+            cast("wd", b, 0, 0, "vector")
+        quantise_weight("wd", 0, 0)
+        keep_factor("r_re", 0, 2, "vector")
+        quantise_weight("wd", 1, 0)
+        tables["v", 0] = (pick("v_codes0", U32, tab[0][:], list_v), v_sc[:, 0, :].bitcast(U8))
+        keep_factor("r_re", 0, 3, "vector")
+        tables["v", 1] = (pick("v_codes1", U32, tab[1][:], list_v), v_sc[:, 1, :].bitcast(U8))
+        for j in range(TILES):
+            keep_factor("r_re", 1, j, "scalar")
+        for b in range(2):
+            for j in range(TILES):
+                product("r_im", b, j)
+                keep_factor("r_im", b, j, "scalar")
+
+        units = [(b, j) for b in range(2) for j in range(TILES)]
+        for b, j in units[:7]:
+            product("s_im", b, j)
+            multiply("s_im", b, j)
+        for j in range(2):
+            turn("im", 0, j)
+        product("s_im", 1, 3)
+        for j in range(2, 4):
+            turn("im", 0, j)
         for c in range(2):
             cast("wa", 0, 0, c, "scalar")
-        for b, j in [(0, j) for j in range(TILES)] + [(1, j) for j in PAIRS[0]]:
-            multiply("s_im", b, j)
-        for j in range(TILES):
-            turn("im", 0, j)
-        cast_shared("wa", 0, 1)
-        for a in range(2):
-            quantise_weight("wa", 0, a)
-            multiply("s_im", 1, PAIRS[1][a])
-            for j in PAIRS[0]:
-                product_pass("s_re", 0, j, a)
-        for j in PAIRS[1]:
-            product("s_re", 0, j)
-
-        for c in range(2):
-            cast("wa", 1, 0, c, "scalar")
+        cast("wa", 0, 1, 0, "scalar")
+        cast("wa", 0, 1, 1, "vector")
+        quantise_weight("wa", 0, 0)
+        multiply("s_im", 1, 3)
         for j in range(3):
+            product_pass("s_re", 0, j, 0)
+        quantise_weight("wa", 0, 1)
+        for j in range(3):
+            product_pass("s_re", 0, j, 1)
+        product("s_re", 0, 3)
+        cast("wa", 1, 0, 0, "scalar")
+        cast("wa", 1, 0, 1, "vector")
+
+        for j in range(2):
             multiply("s_re", 0, j)
             turn("re", 0, j)
+        round_h(0, 0)
         quantise_weight("wa", 1, 0)
-        for j in range(3):
+        for j in range(2):
             product_pass("s_re", 1, j, 0)
-        cast_shared("wa", 1, 1)
-        for j in range(3):
-            round_h(0, j)
+        cast("wa", 1, 1, 0, "scalar")
+        cast("wa", 1, 1, 1, "vector")
+        round_h(0, 1)
         turn("im", 1, 0)
+        multiply("s_re", 0, 2)
+        turn("re", 0, 2)
+        round_h(0, 2)
+        product_pass("s_re", 1, 2, 0)
         multiply("s_re", 0, 3)
         turn("re", 0, 3)
         round_h(0, 3)
-        turn("im", 1, 1)
         quantise_weight("wa", 1, 1)
         for j in range(3):
             product_pass("s_re", 1, j, 1)
-        product("s_re", 1, 3)
         pick_gains(0)
-        for pair, later in zip(PAIRS, PAIRS[1]):
-            turn("im", 1, later)
-            for j in pair:
-                multiply("s_re", 1, j)
-                turn("re", 1, j)
-                round_h(1, j)
+        for j in range(1, 3):
+            turn("im", 1, j)
+        multiply("s_re", 1, 0)
+        turn("re", 1, 0)
+        round_h(1, 0)
+        product("s_re", 1, 3)
+        multiply("s_re", 1, 1)
+        turn("re", 1, 1)
+        round_h(1, 1)
+        turn("im", 1, 3)
+        for j in range(2, 4):
+            multiply("s_re", 1, j)
+            turn("re", 1, j)
+            round_h(1, j)
         for c in range(2):
             quantise_h(0, c)
 
-        ahead, opened = range(3), range(TILES)
+        ahead, opened = range(2), range(OUT_TILES)
         for n in opened:
-            y_pass(n, 0, WHOLE_LIST)
+            y_pass(n, 0)
         pick_gains(1)
-        for c in range(2):
-            quantise_h(1, c)
-        pick_gains(2)
+        quantise_h(1, 0)
+        quantise_h(1, 1)
         for n in range(OUT_TILES):
-            if n not in opened:
-                y_pass(n, 0, WHOLE_LIST)
-            y_pass(n, 1, WHOLE_LIST)
+            y_pass(n, 1)
             if n in ahead:
-                scale_from_psum(n, WHOLE_LIST)
+                scale_from_psum(n)
             else:
                 keep_y(n)
         for n in range(len(ahead), OUT_TILES - 1):
-            gather_scale_store(n, WHOLE_LIST)
+            gather_scale_store(n, slice(0, S))
         gather_scale_store(OUT_TILES - 1, slice(0, S - P))
         gather_scale_store(OUT_TILES - 1, slice(S - P, S))

@@ -63,7 +63,7 @@ def tile_list_complex_relation_embedding_kernel(
         tab_sc = held("tab_sc", [P, T // 4], I32)
         v_sc = held("v_sc", [P, 2, S // 4], I32)
         wo_sc = held("wo_sc", [P, 2, N // 4], I32)
-        for plane in (tab2_sc, tab_sc, wb_sc, v_sc, wc_sc, wo_sc):
+        for plane in (tab2_sc, tab_sc, v_sc, wb_sc, wc_sc, wo_sc):
             nc.vector.memset(plane[:], 0)
 
         def load_words(name, shape, dtype, source):
@@ -232,21 +232,22 @@ def tile_list_complex_relation_embedding_kernel(
             nc.vector.tensor_tensor(out=piece[:], in0=gains[n][:].indirect(offsets), in1=y[n][:, entries], op=MULT)
             nc.sync.dma_start(out=out[P * n : P * (n + 1), entries], in_=piece[:])
 
+        ident = held("ident", [P, P], F32)
+        make_identity(nc, ident[:])
         tab2 = load_words("tab2", [P, T2], U32, tab2_words[0].rearrange("p t i -> p (t i)"))
         nc.sync.dma_start(list_v2[:], offs2)
         nc.sync.dma_start(list_v[:], offs)
+        load_planes(nc.sync, tab2_sc, tab2_scales, 0, range(3))
         nc.sync.dma_start(out=tab_sc[0:P:4, :], in_=tab_scales.rearrange("a m c -> m a c").bitcast(I32))
-        load_planes(nc.sync, tab2_sc, tab2_scales, 0, range(2))
-        load_planes(nc.gpsimd, tab2_sc, tab2_scales, 0, range(2, 4))
-        load_planes(nc.gpsimd, wb_sc, wb_scales, 0, range(4))
-        ident = held("ident", [P, P], F32)
-        make_identity(nc, ident[:])
-        wb = load_words("wb", [P, 2 * H], U8, wb_words[0])
         load_weight("wd", wd, 0, range(2))
+        load_planes(nc.sync, tab2_sc, tab2_scales, 0, range(3, 4))
         v_rows = pick("v_rows", U8, tab_sc[:].bitcast(U8), list_v)
         for q in range(4):
             nc.sync.dma_start(out=v_sc[32 * q : 32 * q + 4, :, :], in_=v_rows[32 * q : 32 * (q + 1) : 4, :].bitcast(I32))
-        tab = [load_words("tab%d" % a, [P, T], U32, tab_words[a].rearrange("p t i -> p (t i)")) for a in range(2)]
+        tab = [load_words("tab0", [P, T], U32, tab_words[0].rearrange("p t i -> p (t i)"))]
+        wb = load_words("wb", [P, 2 * H], U8, wb_words[0])
+        load_planes(nc.sync, wb_sc, wb_scales, 0, range(4))
+        tab.append(load_words("tab1", [P, T], U32, tab_words[1].rearrange("p t i -> p (t i)")))
         wc = load_words("wc", [P, 2, 2 * H], U8, wc_words.rearrange("a p c -> p a c"))
         load_planes(nc.sync, wc_sc, wc_scales, 0, range(4))
         for b in range(2):
@@ -257,31 +258,31 @@ def tile_list_complex_relation_embedding_kernel(
         wo = load_words("wo", [P, 2, N], U32, wo_words.rearrange("a p c i -> p a (c i)"))
         gains.extend(load_gains(n) for n in range(1, OUT_TILES))
 
-        tables["v2", 0] = (
-            pick("v2_codes", U32, tab2[:], list_v2),
-            pick("v2_scales", U8, tab2_sc[:, 0, :].bitcast(U8), list_v2),
-        )
-        for b in range(2):
-            for j in range(TILES):
-                product("r_re", b, j)
-        keep_factor("r_re", 0, 0, "vector")
-        keep_factor("r_re", 0, 1, "vector")
+        v2_codes = pick("v2_codes", U32, tab2[:], list_v2)
         for b in range(2):
             cast("wd", b, 0, 1, "scalar")
-        for b in range(2):
-            cast("wd", b, 0, 0, "vector")
+        cast("wd", 0, 0, 0, "vector")
+        tables["v2", 0] = (v2_codes, pick("v2_scales", U8, tab2_sc[:, 0, :].bitcast(U8), list_v2))
         quantise_weight("wd", 0, 0)
-        keep_factor("r_re", 0, 2, "vector")
-        quantise_weight("wd", 1, 0)
+        cast("wd", 1, 0, 0, "vector")
         tables["v", 0] = (pick("v_codes0", U32, tab[0][:], list_v), v_sc[:, 0, :].bitcast(U8))
-        keep_factor("r_re", 0, 3, "vector")
-        tables["v", 1] = (pick("v_codes1", U32, tab[1][:], list_v), v_sc[:, 1, :].bitcast(U8))
+        quantise_weight("wd", 1, 0)
         for j in range(TILES):
+            product("r_im", 0, j)
+            keep_factor("r_im", 0, j, "scalar")
+        for j in range(2):
+            product("r_re", 0, j)
+            keep_factor("r_re", 0, j, "vector")
+        for j in range(TILES):
+            product("r_im", 1, j)
+            keep_factor("r_im", 1, j, "scalar")
+        tables["v", 1] = (pick("v_codes1", U32, tab[1][:], list_v), v_sc[:, 1, :].bitcast(U8))
+        for j in range(2, 4):
+            product("r_re", 0, j)
+            keep_factor("r_re", 0, j, "vector")
+        for j in range(TILES):
+            product("r_re", 1, j)
             keep_factor("r_re", 1, j, "scalar")
-        for b in range(2):
-            for j in range(TILES):
-                product("r_im", b, j)
-                keep_factor("r_im", b, j, "scalar")
 
         units = [(b, j) for b in range(2) for j in range(TILES)]
         for b, j in units[:7]:

@@ -27,8 +27,8 @@ OUT_TILES = N // P
 WO_PLANE = 4
 PASSES = {"s_re": K // PASS, "s_im": K // PASS, "r_re": L // PASS, "r_im": L // PASS}
 
-VECTOR_RING = 27
-SCALAR_RING = 19
+VECTOR_RING = 25
+SCALAR_RING = 17
 PSUM_BANKS = 8
 
 
@@ -63,7 +63,7 @@ def tile_list_complex_relation_embedding_kernel(
         tab_sc = held("tab_sc", [P, T // 4], I32)
         v_sc = held("v_sc", [P, 2, S // 4], I32)
         wo_sc = held("wo_sc", [P, 2, N // 4], I32)
-        for plane in (tab2_sc, tab_sc, v_sc, wb_sc, wc_sc, wo_sc):
+        for plane in (wo_sc, tab2_sc, tab_sc, v_sc, wb_sc, wc_sc):
             nc.vector.memset(plane[:], 0)
 
         def load_words(name, shape, dtype, source):
@@ -85,16 +85,18 @@ def tile_list_complex_relation_embedding_kernel(
             for b in halves:
                 raw[name, b, a] = tile[:, :, HALF * (b - halves.start) : HALF * (b - halves.start + 1)]
 
-        def load_gains(n):
-            tile = held("gT%d" % n, [P, T], F32)
-            nc.sync.dma_start(out=tile[:], in_=gT[P * n : P * (n + 1), :])
-            return tile
+        def load_gains(tiles):
+            tile = held("gT%d" % tiles.start, [P, T * len(tiles)], F32)
+            rows = gT[P * tiles.start : P * tiles.stop, :].rearrange("(i p) t -> p i t", p=P)
+            nc.sync.dma_start(out=tile[:].rearrange("p (i t) -> p i t", t=T), in_=rows)
+            for i, n in enumerate(tiles):
+                gains[n] = tile[:, T * i : T * (i + 1)] if i else tile[:]
 
         raw, grouped, quantised = {}, {}, {}
         sums, factor, term, turned = {}, {}, {}, {}
         h, h_codes, h_scales = {}, {}, {}
         y_bank, y, picked_gains = {}, {}, {}
-        tables = {}
+        tables, gains, scaled = {}, {}, {}
 
         def pick(name, dtype, window, offsets):
             picked = fresh("vector", name, [P, S], dtype)
@@ -219,19 +221,31 @@ def tile_list_complex_relation_embedding_kernel(
             nc.scalar.copy(out=y[n][:], in_=y_bank[n][:])
 
         def pick_gains(n):
-            picked_gains[n] = pick("picked_gains%d" % n, F32, gains[n][:], list_v)
+            picked_gains[n] = pick("picked_gains%d" % n, F32, gains[n], list_v)
+
+        def open_store(tiles):
+            tile = held("scaled%d" % tiles.start, [P, len(tiles), S], F32)
+            for i, n in enumerate(tiles):
+                scaled[n] = tile[:, i, :]
+            return tile
+
+        def store(tiles, tile):
+            rows = out[P * tiles.start : P * tiles.stop, :].rearrange("(i p) j -> p i j", p=P)
+            nc.sync.dma_start(out=rows, in_=tile[:])
 
         def scale_from_psum(n):
-            scaled = fresh("vector", "scaled%d" % n, [P, S], F32)
-            nc.vector.tensor_tensor(out=scaled[:], in0=y_bank[n][:], in1=picked_gains[n][:], op=MULT)
-            nc.sync.dma_start(out=out[P * n : P * (n + 1), :], in_=scaled[:])
+            nc.vector.tensor_tensor(out=scaled[n], in0=y_bank[n][:], in1=picked_gains[n][:], op=MULT)
+
+        def gather_scale(n):
+            nc.vector.tensor_tensor(out=scaled[n], in0=gains[n].indirect(list_v[:]), in1=y[n][:], op=MULT)
 
         def gather_scale_store(n, entries):
             piece = fresh("vector", "scaled%d_%d" % (n, entries.start), [P, entries.stop - entries.start], F32)
             offsets = list_v[:, entries.start // 16 : entries.stop // 16]
-            nc.vector.tensor_tensor(out=piece[:], in0=gains[n][:].indirect(offsets), in1=y[n][:, entries], op=MULT)
+            nc.vector.tensor_tensor(out=piece[:], in0=gains[n].indirect(offsets), in1=y[n][:, entries], op=MULT)
             nc.sync.dma_start(out=out[P * n : P * (n + 1), entries], in_=piece[:])
 
+        load_planes(nc.gpsimd, wo_sc, wo_scales, WO_PLANE, range(4))
         ident = held("ident", [P, P], F32)
         make_identity(nc, ident[:])
         tab2 = load_words("tab2", [P, T2], U32, tab2_words[0].rearrange("p t i -> p (t i)"))
@@ -253,10 +267,10 @@ def tile_list_complex_relation_embedding_kernel(
         for b in range(2):
             for a in range(2):
                 load_weight("wa", wa, a, range(b, b + 1))
-        gains = [load_gains(0)]
-        load_planes(nc.sync, wo_sc, wo_scales, WO_PLANE, range(4))
+        load_gains(range(1))
         wo = load_words("wo", [P, 2, N], U32, wo_words.rearrange("a p c i -> p a (c i)"))
-        gains.extend(load_gains(n) for n in range(1, OUT_TILES))
+        for n in range(1, OUT_TILES):
+            load_gains(range(n, n + 1))
 
         v2_codes = pick("v2_codes", U32, tab2[:], list_v2)
         for b in range(2):
@@ -347,19 +361,24 @@ def tile_list_complex_relation_embedding_kernel(
         for c in range(2):
             quantise_h(0, c)
 
-        ahead, opened = range(2), range(OUT_TILES)
-        for n in opened:
+        for n in range(OUT_TILES):
             y_pass(n, 0)
         pick_gains(1)
         quantise_h(1, 0)
         quantise_h(1, 1)
+        pick_gains(2)
+        joined = [range(0, 2), range(2, 4), range(4, 5)]
+        opened = [open_store(tiles) for tiles in joined]
         for n in range(OUT_TILES):
             y_pass(n, 1)
-            if n in ahead:
+            if n < 3:
                 scale_from_psum(n)
             else:
                 keep_y(n)
-        for n in range(len(ahead), OUT_TILES - 1):
-            gather_scale_store(n, slice(0, S))
-        gather_scale_store(OUT_TILES - 1, slice(0, S - P))
-        gather_scale_store(OUT_TILES - 1, slice(S - P, S))
+        for tiles, tile in zip(joined, opened):
+            for n in tiles:
+                if n >= 3:
+                    gather_scale(n)
+            store(tiles, tile)
+        for entries in (slice(0, 256), slice(256, 512)):
+            gather_scale_store(OUT_TILES - 1, entries)

@@ -23,12 +23,13 @@ PASS = P * PACK
 HALF = 512
 PART = 256
 TILES = S // P
+PAIRS = ((0, 1), (2, 3))
 OUT_TILES = N // P
 WO_PLANE = 4
 PASSES = {"s_re": K // PASS, "s_im": K // PASS, "r_re": L // PASS, "r_im": L // PASS}
 
-VECTOR_RING = 25
-SCALAR_RING = 17
+VECTOR_RING = 27
+SCALAR_RING = 19
 PSUM_BANKS = 8
 
 
@@ -85,18 +86,16 @@ def tile_list_complex_relation_embedding_kernel(
             for b in halves:
                 raw[name, b, a] = tile[:, :, HALF * (b - halves.start) : HALF * (b - halves.start + 1)]
 
-        def load_gains(tiles):
-            tile = held("gT%d" % tiles.start, [P, T * len(tiles)], F32)
-            rows = gT[P * tiles.start : P * tiles.stop, :].rearrange("(i p) t -> p i t", p=P)
-            nc.sync.dma_start(out=tile[:].rearrange("p (i t) -> p i t", t=T), in_=rows)
-            for i, n in enumerate(tiles):
-                gains[n] = tile[:, T * i : T * (i + 1)] if i else tile[:]
+        def load_gains(n):
+            tile = held("gT%d" % n, [P, T], F32)
+            nc.sync.dma_start(out=tile[:], in_=gT[P * n : P * (n + 1), :])
+            return tile
 
         raw, grouped, quantised = {}, {}, {}
         sums, factor, term, turned = {}, {}, {}, {}
         h, h_codes, h_scales = {}, {}, {}
         y_bank, y, picked_gains = {}, {}, {}
-        tables, gains, scaled = {}, {}, {}
+        tables = {}
 
         def pick(name, dtype, window, offsets):
             picked = fresh("vector", name, [P, S], dtype)
@@ -221,28 +220,17 @@ def tile_list_complex_relation_embedding_kernel(
             nc.scalar.copy(out=y[n][:], in_=y_bank[n][:])
 
         def pick_gains(n):
-            picked_gains[n] = pick("picked_gains%d" % n, F32, gains[n], list_v)
-
-        def open_store(tiles):
-            tile = held("scaled%d" % tiles.start, [P, len(tiles), S], F32)
-            for i, n in enumerate(tiles):
-                scaled[n] = tile[:, i, :]
-            return tile
-
-        def store(tiles, tile):
-            rows = out[P * tiles.start : P * tiles.stop, :].rearrange("(i p) j -> p i j", p=P)
-            nc.sync.dma_start(out=rows, in_=tile[:])
+            picked_gains[n] = pick("picked_gains%d" % n, F32, gains[n][:], list_v)
 
         def scale_from_psum(n):
-            nc.vector.tensor_tensor(out=scaled[n], in0=y_bank[n][:], in1=picked_gains[n][:], op=MULT)
-
-        def gather_scale(n):
-            nc.vector.tensor_tensor(out=scaled[n], in0=gains[n].indirect(list_v[:]), in1=y[n][:], op=MULT)
+            scaled = fresh("vector", "scaled%d" % n, [P, S], F32)
+            nc.vector.tensor_tensor(out=scaled[:], in0=y_bank[n][:], in1=picked_gains[n][:], op=MULT)
+            nc.sync.dma_start(out=out[P * n : P * (n + 1), :], in_=scaled[:])
 
         def gather_scale_store(n, entries):
             piece = fresh("vector", "scaled%d_%d" % (n, entries.start), [P, entries.stop - entries.start], F32)
             offsets = list_v[:, entries.start // 16 : entries.stop // 16]
-            nc.vector.tensor_tensor(out=piece[:], in0=gains[n].indirect(offsets), in1=y[n][:, entries], op=MULT)
+            nc.vector.tensor_tensor(out=piece[:], in0=gains[n][:].indirect(offsets), in1=y[n][:, entries], op=MULT)
             nc.sync.dma_start(out=out[P * n : P * (n + 1), entries], in_=piece[:])
 
         load_planes(nc.gpsimd, wo_sc, wo_scales, WO_PLANE, range(4))
@@ -267,10 +255,9 @@ def tile_list_complex_relation_embedding_kernel(
         for b in range(2):
             for a in range(2):
                 load_weight("wa", wa, a, range(b, b + 1))
-        load_gains(range(1))
+        gains = [load_gains(0)]
         wo = load_words("wo", [P, 2, N], U32, wo_words.rearrange("a p c i -> p a (c i)"))
-        for n in range(1, OUT_TILES):
-            load_gains(range(n, n + 1))
+        gains.extend(load_gains(n) for n in range(1, OUT_TILES))
 
         v2_codes = pick("v2_codes", U32, tab2[:], list_v2)
         for b in range(2):
@@ -298,87 +285,72 @@ def tile_list_complex_relation_embedding_kernel(
             product("r_re", 1, j)
             keep_factor("r_re", 1, j, "scalar")
 
-        units = [(b, j) for b in range(2) for j in range(TILES)]
-        for b, j in units[:7]:
-            product("s_im", b, j)
-            multiply("s_im", b, j)
-        for j in range(2):
-            turn("im", 0, j)
-        product("s_im", 1, 3)
-        for j in range(2, 4):
-            turn("im", 0, j)
+        for b in range(2):
+            for j in range(TILES):
+                product("s_im", b, j)
         for c in range(2):
             cast("wa", 0, 0, c, "scalar")
-        cast("wa", 0, 1, 0, "scalar")
-        cast("wa", 0, 1, 1, "vector")
-        quantise_weight("wa", 0, 0)
-        multiply("s_im", 1, 3)
-        for j in range(3):
-            product_pass("s_re", 0, j, 0)
-        quantise_weight("wa", 0, 1)
-        for j in range(3):
-            product_pass("s_re", 0, j, 1)
-        product("s_re", 0, 3)
-        cast("wa", 1, 0, 0, "scalar")
-        cast("wa", 1, 0, 1, "vector")
+        for b, j in [(0, j) for j in range(TILES)] + [(1, j) for j in PAIRS[0]]:
+            multiply("s_im", b, j)
+        for j in range(TILES):
+            turn("im", 0, j)
+        cast("wa", 0, 1, 0, "vector")
+        cast("wa", 0, 1, 1, "scalar")
+        for a in range(2):
+            quantise_weight("wa", 0, a)
+            multiply("s_im", 1, PAIRS[1][a])
+            for j in PAIRS[0]:
+                product_pass("s_re", 0, j, a)
+        for j in PAIRS[1]:
+            product("s_re", 0, j)
 
-        for j in range(2):
+        for c in range(2):
+            cast("wa", 1, 0, c, "scalar")
+        for j in range(3):
             multiply("s_re", 0, j)
             turn("re", 0, j)
-        round_h(0, 0)
         quantise_weight("wa", 1, 0)
-        for j in range(2):
+        for j in range(3):
             product_pass("s_re", 1, j, 0)
-        cast("wa", 1, 1, 0, "scalar")
-        cast("wa", 1, 1, 1, "vector")
-        round_h(0, 1)
+        cast("wa", 1, 1, 0, "vector")
+        cast("wa", 1, 1, 1, "scalar")
+        for j in range(3):
+            round_h(0, j)
         turn("im", 1, 0)
-        multiply("s_re", 0, 2)
-        turn("re", 0, 2)
-        round_h(0, 2)
-        product_pass("s_re", 1, 2, 0)
         multiply("s_re", 0, 3)
         turn("re", 0, 3)
         round_h(0, 3)
+        turn("im", 1, 1)
         quantise_weight("wa", 1, 1)
         for j in range(3):
             product_pass("s_re", 1, j, 1)
-        pick_gains(0)
-        for j in range(1, 3):
-            turn("im", 1, j)
-        multiply("s_re", 1, 0)
-        turn("re", 1, 0)
-        round_h(1, 0)
         product("s_re", 1, 3)
-        multiply("s_re", 1, 1)
-        turn("re", 1, 1)
-        round_h(1, 1)
-        turn("im", 1, 3)
-        for j in range(2, 4):
-            multiply("s_re", 1, j)
-            turn("re", 1, j)
-            round_h(1, j)
+        pick_gains(0)
+        for pair, later in zip(PAIRS, PAIRS[1]):
+            turn("im", 1, later)
+            for j in pair:
+                multiply("s_re", 1, j)
+                turn("re", 1, j)
+                round_h(1, j)
         for c in range(2):
             quantise_h(0, c)
 
-        for n in range(OUT_TILES):
+        ahead, opened = range(3), range(TILES)
+        for n in opened:
             y_pass(n, 0)
         pick_gains(1)
-        quantise_h(1, 0)
-        quantise_h(1, 1)
+        for c in range(2):
+            quantise_h(1, c)
         pick_gains(2)
-        joined = [range(0, 2), range(2, 4), range(4, 5)]
-        opened = [open_store(tiles) for tiles in joined]
         for n in range(OUT_TILES):
+            if n not in opened:
+                y_pass(n, 0)
             y_pass(n, 1)
-            if n < 3:
+            if n in ahead:
                 scale_from_psum(n)
             else:
                 keep_y(n)
-        for tiles, tile in zip(joined, opened):
-            for n in tiles:
-                if n >= 3:
-                    gather_scale(n)
-            store(tiles, tile)
-        for entries in (slice(0, 256), slice(256, 512)):
-            gather_scale_store(OUT_TILES - 1, entries)
+        for n in range(len(ahead), OUT_TILES - 1):
+            gather_scale_store(n, slice(0, S))
+        gather_scale_store(OUT_TILES - 1, slice(0, S - P))
+        gather_scale_store(OUT_TILES - 1, slice(S - P, S))

@@ -64,7 +64,7 @@ def tile_list_complex_relation_embedding_kernel(
         tab_sc = held("tab_sc", [P, T // 4], I32)
         v_sc = held("v_sc", [P, 2, S // 4], I32)
         wo_sc = held("wo_sc", [P, 2, N // 4], I32)
-        for plane in (wo_sc, tab2_sc, tab_sc, v_sc, wb_sc, wc_sc):
+        for plane in (tab_sc, tab2_sc, wo_sc, v_sc, wb_sc, wc_sc):
             nc.vector.memset(plane[:], 0)
 
         def load_words(name, shape, dtype, source):
@@ -239,8 +239,8 @@ def tile_list_complex_relation_embedding_kernel(
         tab2 = load_words("tab2", [P, T2], U32, tab2_words[0].rearrange("p t i -> p (t i)"))
         nc.sync.dma_start(list_v2[:], offs2)
         nc.sync.dma_start(list_v[:], offs)
-        load_planes(nc.sync, tab2_sc, tab2_scales, 0, range(3))
         nc.sync.dma_start(out=tab_sc[0:P:4, :], in_=tab_scales.rearrange("a m c -> m a c").bitcast(I32))
+        load_planes(nc.sync, tab2_sc, tab2_scales, 0, range(3))
         load_weight("wd", wd, 0, range(2))
         load_planes(nc.sync, tab2_sc, tab2_scales, 0, range(3, 4))
         v_rows = pick("v_rows", U8, tab_sc[:].bitcast(U8), list_v)
@@ -352,5 +352,5 @@ def tile_list_complex_relation_embedding_kernel(
                 keep_y(n)
         for n in range(len(ahead), OUT_TILES - 1):
             gather_scale_store(n, slice(0, S))
-        gather_scale_store(OUT_TILES - 1, slice(0, S - P))
-        gather_scale_store(OUT_TILES - 1, slice(S - P, S))
+        for entries in (slice(0, 256), slice(256, 448), slice(448, S)):
+            gather_scale_store(OUT_TILES - 1, entries)

@@ -64,7 +64,7 @@ def tile_list_complex_relation_embedding_kernel(
         tab_sc = held("tab_sc", [P, T // 4], I32)
         v_sc = held("v_sc", [P, 2, S // 4], I32)
         wo_sc = held("wo_sc", [P, 2, N // 4], I32)
-        for plane in (tab_sc, tab2_sc, wo_sc, v_sc, wb_sc, wc_sc):
+        for plane in (tab_sc, tab2_sc, v_sc, wb_sc, wc_sc, wo_sc):
             nc.vector.memset(plane[:], 0)
 
         def load_words(name, shape, dtype, source):
@@ -233,7 +233,6 @@ def tile_list_complex_relation_embedding_kernel(
             nc.vector.tensor_tensor(out=piece[:], in0=gains[n][:].indirect(offsets), in1=y[n][:, entries], op=MULT)
             nc.sync.dma_start(out=out[P * n : P * (n + 1), entries], in_=piece[:])
 
-        load_planes(nc.gpsimd, wo_sc, wo_scales, WO_PLANE, range(4))
         ident = held("ident", [P, P], F32)
         make_identity(nc, ident[:])
         tab2 = load_words("tab2", [P, T2], U32, tab2_words[0].rearrange("p t i -> p (t i)"))
@@ -257,6 +256,7 @@ def tile_list_complex_relation_embedding_kernel(
                 load_weight("wa", wa, a, range(b, b + 1))
         gains = [load_gains(0)]
         wo = load_words("wo", [P, 2, N], U32, wo_words.rearrange("a p c i -> p a (c i)"))
+        load_planes(nc.sync, wo_sc, wo_scales, WO_PLANE, range(4))
         gains.extend(load_gains(n) for n in range(1, OUT_TILES))
 
         v2_codes = pick("v2_codes", U32, tab2[:], list_v2)

@@ -28,7 +28,7 @@ OUT_TILES = N // P
 WO_PLANE = 4
 PASSES = {"s_re": K // PASS, "s_im": K // PASS, "r_re": L // PASS, "r_im": L // PASS}
 
-VECTOR_RING = 27
+VECTOR_RING = 28
 SCALAR_RING = 19
 PSUM_BANKS = 8
 
@@ -64,7 +64,7 @@ def tile_list_complex_relation_embedding_kernel(
         tab_sc = held("tab_sc", [P, T // 4], I32)
         v_sc = held("v_sc", [P, 2, S // 4], I32)
         wo_sc = held("wo_sc", [P, 2, N // 4], I32)
-        for plane in (tab_sc, tab2_sc, v_sc, wb_sc, wc_sc, wo_sc):
+        for plane in (tab_sc, tab2_sc, wb_sc, v_sc, wc_sc, wo_sc):
             nc.vector.memset(plane[:], 0)
 
         def load_words(name, shape, dtype, source):
@@ -242,12 +242,12 @@ def tile_list_complex_relation_embedding_kernel(
         load_planes(nc.sync, tab2_sc, tab2_scales, 0, range(3))
         load_weight("wd", wd, 0, range(2))
         load_planes(nc.sync, tab2_sc, tab2_scales, 0, range(3, 4))
+        load_planes(nc.sync, wb_sc, wb_scales, 0, range(4))
+        wb = load_words("wb", [P, 2 * H], U8, wb_words[0])
+        tab = [load_words("tab0", [P, T], U32, tab_words[0].rearrange("p t i -> p (t i)"))]
         v_rows = pick("v_rows", U8, tab_sc[:].bitcast(U8), list_v)
         for q in range(4):
             nc.sync.dma_start(out=v_sc[32 * q : 32 * q + 4, :, :], in_=v_rows[32 * q : 32 * (q + 1) : 4, :].bitcast(I32))
-        tab = [load_words("tab0", [P, T], U32, tab_words[0].rearrange("p t i -> p (t i)"))]
-        wb = load_words("wb", [P, 2 * H], U8, wb_words[0])
-        load_planes(nc.sync, wb_sc, wb_scales, 0, range(4))
         tab.append(load_words("tab1", [P, T], U32, tab_words[1].rearrange("p t i -> p (t i)")))
         wc = load_words("wc", [P, 2, 2 * H], U8, wc_words.rearrange("a p c -> p a c"))
         load_planes(nc.sync, wc_sc, wc_scales, 0, range(4))
@@ -260,30 +260,28 @@ def tile_list_complex_relation_embedding_kernel(
         gains.extend(load_gains(n) for n in range(1, OUT_TILES))
 
         v2_codes = pick("v2_codes", U32, tab2[:], list_v2)
+        tables["v2", 0] = (v2_codes, pick("v2_scales", U8, tab2_sc[:, 0, :].bitcast(U8), list_v2))
         for b in range(2):
             cast("wd", b, 0, 1, "scalar")
         cast("wd", 0, 0, 0, "vector")
-        tables["v2", 0] = (v2_codes, pick("v2_scales", U8, tab2_sc[:, 0, :].bitcast(U8), list_v2))
         quantise_weight("wd", 0, 0)
         cast("wd", 1, 0, 0, "vector")
         tables["v", 0] = (pick("v_codes0", U32, tab[0][:], list_v), v_sc[:, 0, :].bitcast(U8))
         quantise_weight("wd", 1, 0)
-        for j in range(TILES):
-            product("r_im", 0, j)
-            keep_factor("r_im", 0, j, "scalar")
-        for j in range(2):
-            product("r_re", 0, j)
-            keep_factor("r_re", 0, j, "vector")
-        for j in range(TILES):
-            product("r_im", 1, j)
-            keep_factor("r_im", 1, j, "scalar")
+
+        def relation(name, tiles, engine):
+            for b, j in tiles:
+                product(name, b, j)
+                keep_factor(name, b, j, engine)
+
+        every = [(b, j) for b in range(2) for j in range(TILES)]
+        relation("r_re", every[:3], "scalar")
+        relation("r_im", every[:TILES], "scalar")
+        relation("r_re", every[3:5], "vector")
+        relation("r_im", every[TILES:], "scalar")
         tables["v", 1] = (pick("v_codes1", U32, tab[1][:], list_v), v_sc[:, 1, :].bitcast(U8))
-        for j in range(2, 4):
-            product("r_re", 0, j)
-            keep_factor("r_re", 0, j, "vector")
-        for j in range(TILES):
-            product("r_re", 1, j)
-            keep_factor("r_re", 1, j, "scalar")
+        relation("r_re", every[5:7], "vector")
+        relation("r_re", every[7:], "scalar")
 
         for b in range(2):
             for j in range(TILES):

from contextlib import ExitStack

import concourse.mybir as mybir
from concourse.masks import make_identity

K, L, H, N, T, T2, S = 1024, 512, 1024, 768, 2048, 1024, 512
FLOPS = 2 * S * (2 * K * H + 2 * L * H + H * N)

F32 = mybir.dt.float32
BF16 = mybir.dt.bfloat16
I32 = mybir.dt.int32
U32 = mybir.dt.uint32
U16 = mybir.dt.uint16
U8 = mybir.dt.uint8
FP8X4 = mybir.dt.float8_e4m3fn_x4
FP4X4 = mybir.dt.float4_e2m1fn_x4
MULT = mybir.AluOpType.mult
COPY = mybir.ActivationFunctionType.Copy

P = 128
PACK = 4
PASS = P * PACK
HALF = 512
PART = 256
TILES = S // P
PAIRS = ((0, 1), (2, 3))
OUT_TILES = N // P
WO_PLANE = 4
PASSES = {"s_re": K // PASS, "s_im": K // PASS, "r_re": L // PASS, "r_im": L // PASS}

VECTOR_RING = 28
SCALAR_RING = 19
PSUM_BANKS = 8


def tile_list_complex_relation_embedding_kernel(
    tc, tab_words, tab_scales, tab2_words, tab2_scales, offs, offs2, wa, wb_words, wb_scales,
    wc_words, wc_scales, wd, wo_words, wo_scales, gT, out,
):
    nc = tc.nc
    with ExitStack() as ctx:
        keep = ctx.enter_context(tc.tile_pool(name="keep", bufs=1))
        rings = {
            "vector": ctx.enter_context(tc.tile_pool(name="vector_ring", bufs=VECTOR_RING)),
            "scalar": ctx.enter_context(tc.tile_pool(name="scalar_ring", bufs=SCALAR_RING)),
        }
        banks = ctx.enter_context(tc.psum_pool(name="banks", bufs=PSUM_BANKS))

        def held(name, shape, dtype):
            return keep.tile(shape, dtype, name=name, align_bytes=64)

        def fresh(engine, name, shape, dtype):
            return rings[engine].tile(shape, dtype, name=name, tag="slot", align_bytes=64)

        def next_bank(name, shape):
            return banks.tile(shape, F32, name=name, tag="bank")

        list_v = keep.tile([P, S // 16], U16, name="list_v")
        list_v2 = keep.tile([P, S // 16], U16, name="list_v2")

        tab2_sc = held("tab2_sc", [P, 1, T2 // 4], I32)
        wb_sc = held("wb_sc", [P, 1, H // 4], I32)
        wc_sc = held("wc_sc", [P, 2, H // 4], I32)
        tab_sc = held("tab_sc", [P, T // 4], I32)
        v_sc = held("v_sc", [P, 2, S // 4], I32)
        wo_sc = held("wo_sc", [P, 2, N // 4], I32)
        for plane in (tab_sc, tab2_sc, wb_sc, v_sc, wc_sc, wo_sc):
            nc.vector.memset(plane[:], 0)

        def load_words(name, shape, dtype, source):
            tile = held(name, shape, dtype)
            nc.sync.dma_start(out=tile[:].bitcast(I32), in_=source.bitcast(I32))
            return tile

        def load_planes(queue, plane, scales, first, rows):
            for r in rows:
                queue.dma_start(
                    out=plane[first + r : P : 32, :, :],
                    in_=scales[:, r:16:4, :].rearrange("a q c -> q a c").bitcast(I32),
                )

        def load_weight(name, weight, a, halves):
            tile = held("%s%d%d" % (name, a, halves.start), [P, PACK, HALF * len(halves)], F32)
            rows = weight[PASS * a : PASS * (a + 1), HALF * halves.start : HALF * halves.stop]
            nc.sync.dma_start(out=tile[:], in_=rows.rearrange("(p i) c -> p i c", i=PACK))
            for b in halves:
                raw[name, b, a] = tile[:, :, HALF * (b - halves.start) : HALF * (b - halves.start + 1)]

        def load_gains(n):
            tile = held("gT%d" % n, [P, T], F32)
            nc.sync.dma_start(out=tile[:], in_=gT[P * n : P * (n + 1), :])
            return tile

        raw, grouped, quantised = {}, {}, {}
        sums, factor, term, turned = {}, {}, {}, {}
        h, h_codes, h_scales = {}, {}, {}
        y_bank, y, picked_gains = {}, {}, {}
        tables = {}

        def pick(name, dtype, window, offsets):
            picked = fresh("vector", name, [P, S], dtype)
            nc.vector.tensor_copy(out=picked[:], in_=window.indirect(offsets[:]))
            return picked

        def cast(w, b, a, c, engine):
            tile = fresh(engine, "cast_%s%d%d%d" % (w, b, a, c), [P, PART, PACK], BF16)
            laid = tile[:].rearrange("p (c e) i -> p c i e", e=4)
            rows = raw[w, b, a][:, :, PART * c : PART * (c + 1)].rearrange("p i (c e) -> p c i e", e=4)
            if engine == "vector":
                nc.vector.tensor_copy(out=laid, in_=rows)
            else:
                nc.scalar.copy(out=laid, in_=rows)
            grouped[w, b, a, c] = tile

        def quantise_part(codes, scales, c, source):
            cols = slice(PART * c, PART * (c + 1))
            nc.vector.quantize_mx(
                out=codes[:, cols].bitcast(FP8X4), scales=scales[:, cols], in_=source[:].rearrange("p c i -> p (c i)")
            )

        def quantise_weight(w, b, a):
            codes = fresh("vector", "codes_%s%d%d" % (w, b, a), [P, HALF], U32)
            scales = held("scales_%s%d%d" % (w, b, a), [P, HALF], U8)
            for c in range(2):
                quantise_part(codes, scales, c, grouped[w, b, a, c])
            quantised[w, b, a] = (codes[:].bitcast(FP8X4), scales[:])

        def fp4_half(words, plane, a, b):
            return (
                words[:, 2 * HALF * b : 2 * HALF * (b + 1)].bitcast(FP4X4),
                plane[:, a, HALF // 4 * b : HALF // 4 * (b + 1)].bitcast(U8),
            )

        def operands(name, b, a):
            if name == "r_re":
                return tables["v2", 0], fp4_half(wb, wb_sc, 0, b)
            if name == "r_im":
                return tables["v2", 0], quantised["wd", b, 0]
            if name == "s_im":
                return tables["v", a], fp4_half(wc[:, a, :], wc_sc, a, b)
            return tables["v", a], quantised["wa", b, a]

        def product_pass(name, b, j, a):
            if a == 0:
                sums[name, b, j] = next_bank("acc", [P, HALF])
            (codes, scales), (weight_codes, weight_scales) = operands(name, b, a)
            tokens = slice(P * j, P * (j + 1))
            nc.tensor.matmul_mx(
                out=sums[name, b, j][:],
                lhsT=codes[:, tokens].bitcast(FP8X4),
                lhsT_scale=scales[:, tokens],
                rhs=weight_codes,
                rhs_scale=weight_scales,
                start=(a == 0),
                stop=(a == PASSES[name] - 1),
            )

        def product(name, b, j):
            for a in range(PASSES[name]):
                product_pass(name, b, j, a)

        def by_slot(name, b, j):
            return sums[name, b, j][:].rearrange("p (m t) -> p t m", t=PACK)

        def keep_factor(name, b, j, engine):
            kind = name[2:]
            factor[kind, b, j] = fresh(engine, "%s%d%d" % (name, b, j), [P, PACK, P], F32)
            if engine == "vector":
                nc.vector.tensor_copy(out=factor[kind, b, j][:], in_=by_slot(name, b, j))
            else:
                sign = 1.0 if kind == "re" else -1.0
                nc.scalar.activation(out=factor[kind, b, j][:], in_=by_slot(name, b, j), func=COPY, scale=sign)

        def multiply(name, b, j):
            kind = name[2:]
            term[kind, b, j] = fresh("vector", "%s%d%d" % (kind, b, j), [P, PACK, P], F32)
            nc.vector.tensor_tensor(
                out=term[kind, b, j][:], in0=by_slot(name, b, j), in1=factor[kind, b, j][:], op=MULT
            )

        def turn(kind, b, j):
            first = kind == "im"
            if first:
                turned[b, j] = next_bank("turned", [P, PACK, P])
            for t in range(PACK):
                nc.tensor.matmul(
                    out=turned[b, j][:, t, :], lhsT=term[kind, b, j][:, t, :], rhs=ident[:],
                    start=(first and t == 0), stop=(not first and t == PACK - 1), is_transpose=True,
                )

        def round_h(b, j):
            c, side = divmod(j, 2)
            if side == 0:
                h[b, c] = fresh("scalar", "h%d%d" % (b, c), [P, PART, PACK], BF16)
            nc.scalar.copy(
                out=h[b, c][:, P * side : P * (side + 1), :], in_=turned[b, j][:].rearrange("p t j -> p j t")
            )

        def quantise_h(b, c):
            if c == 0:
                h_codes[b] = fresh("vector", "h_codes%d" % b, [P, S], U32)
                h_scales[b] = held("h_scales%d" % b, [P, S], U8)
            quantise_part(h_codes[b], h_scales[b], c, h[b, c])

        def y_pass(n, b):
            if b == 0:
                y_bank[n] = next_bank("acc", [P, S])
            nc.tensor.matmul_mx(
                out=y_bank[n][:],
                lhsT=wo[:, b, P * n : P * (n + 1)].bitcast(FP8X4),
                lhsT_scale=wo_sc[WO_PLANE:, b, P // 4 * n : P // 4 * (n + 1)].bitcast(U8),
                rhs=h_codes[b][:].bitcast(FP8X4),
                rhs_scale=h_scales[b][:],
                start=(b == 0),
                stop=(b == 1),
            )

        def keep_y(n):
            y[n] = fresh("scalar", "y%d" % n, [P, S], F32)
            nc.scalar.copy(out=y[n][:], in_=y_bank[n][:])

        def pick_gains(n):
            picked_gains[n] = pick("picked_gains%d" % n, F32, gains[n][:], list_v)

        def scale_from_psum(n):
            scaled = fresh("vector", "scaled%d" % n, [P, S], F32)
            nc.vector.tensor_tensor(out=scaled[:], in0=y_bank[n][:], in1=picked_gains[n][:], op=MULT)
            nc.sync.dma_start(out=out[P * n : P * (n + 1), :], in_=scaled[:])

        def gather_scale_store(n, entries):
            piece = fresh("vector", "scaled%d_%d" % (n, entries.start), [P, entries.stop - entries.start], F32)
            offsets = list_v[:, entries.start // 16 : entries.stop // 16]
            nc.vector.tensor_tensor(out=piece[:], in0=gains[n][:].indirect(offsets), in1=y[n][:, entries], op=MULT)
            nc.sync.dma_start(out=out[P * n : P * (n + 1), entries], in_=piece[:])

        ident = held("ident", [P, P], F32)
        make_identity(nc, ident[:])
        tab2 = load_words("tab2", [P, T2], U32, tab2_words[0].rearrange("p t i -> p (t i)"))
        nc.sync.dma_start(list_v2[:], offs2)
        nc.sync.dma_start(list_v[:], offs)
        nc.sync.dma_start(out=tab_sc[0:P:4, :], in_=tab_scales.rearrange("a m c -> m a c").bitcast(I32))
        load_planes(nc.sync, tab2_sc, tab2_scales, 0, range(3))
        load_weight("wd", wd, 0, range(2))
        load_planes(nc.sync, tab2_sc, tab2_scales, 0, range(3, 4))
        load_planes(nc.sync, wb_sc, wb_scales, 0, range(4))
        wb = load_words("wb", [P, 2 * H], U8, wb_words[0])
        tab = [load_words("tab0", [P, T], U32, tab_words[0].rearrange("p t i -> p (t i)"))]
        v_rows = pick("v_rows", U8, tab_sc[:].bitcast(U8), list_v)
        for q in range(4):
            nc.sync.dma_start(out=v_sc[32 * q : 32 * q + 4, :, :], in_=v_rows[32 * q : 32 * (q + 1) : 4, :].bitcast(I32))
        tab.append(load_words("tab1", [P, T], U32, tab_words[1].rearrange("p t i -> p (t i)")))
        wc = load_words("wc", [P, 2, 2 * H], U8, wc_words.rearrange("a p c -> p a c"))
        load_planes(nc.sync, wc_sc, wc_scales, 0, range(4))
        for b in range(2):
            for a in range(2):
                load_weight("wa", wa, a, range(b, b + 1))
        gains = [load_gains(0)]
        wo = load_words("wo", [P, 2, N], U32, wo_words.rearrange("a p c i -> p a (c i)"))
        load_planes(nc.sync, wo_sc, wo_scales, WO_PLANE, range(4))
        gains.extend(load_gains(n) for n in range(1, OUT_TILES))

        v2_codes = pick("v2_codes", U32, tab2[:], list_v2)
        tables["v2", 0] = (v2_codes, pick("v2_scales", U8, tab2_sc[:, 0, :].bitcast(U8), list_v2))
        for b in range(2):
            cast("wd", b, 0, 1, "scalar")
        cast("wd", 0, 0, 0, "vector")
        quantise_weight("wd", 0, 0)
        cast("wd", 1, 0, 0, "vector")
        tables["v", 0] = (pick("v_codes0", U32, tab[0][:], list_v), v_sc[:, 0, :].bitcast(U8))
        quantise_weight("wd", 1, 0)

        def relation(name, tiles, engine):
            for b, j in tiles:
                product(name, b, j)
                keep_factor(name, b, j, engine)

        every = [(b, j) for b in range(2) for j in range(TILES)]
        relation("r_re", every[:3], "scalar")
        relation("r_im", every[:TILES], "scalar")
        relation("r_re", every[3:5], "vector")
        relation("r_im", every[TILES:], "scalar")
        tables["v", 1] = (pick("v_codes1", U32, tab[1][:], list_v), v_sc[:, 1, :].bitcast(U8))
        relation("r_re", every[5:7], "vector")
        relation("r_re", every[7:], "scalar")

        for b in range(2):
            for j in range(TILES):
                product("s_im", b, j)
        for c in range(2):
            cast("wa", 0, 0, c, "scalar")
        for b, j in [(0, j) for j in range(TILES)] + [(1, j) for j in PAIRS[0]]:
            multiply("s_im", b, j)
        for j in range(TILES):
            turn("im", 0, j)
        cast("wa", 0, 1, 0, "vector")
        cast("wa", 0, 1, 1, "scalar")
        for a in range(2):
            quantise_weight("wa", 0, a)
            multiply("s_im", 1, PAIRS[1][a])
            for j in PAIRS[0]:
                product_pass("s_re", 0, j, a)
        for j in PAIRS[1]:
            product("s_re", 0, j)

        for c in range(2):
            cast("wa", 1, 0, c, "scalar")
        for j in range(3):
            multiply("s_re", 0, j)
            turn("re", 0, j)
        quantise_weight("wa", 1, 0)
        for j in range(3):
            product_pass("s_re", 1, j, 0)
        cast("wa", 1, 1, 0, "vector")
        cast("wa", 1, 1, 1, "scalar")
        for j in range(3):
            round_h(0, j)
        turn("im", 1, 0)
        multiply("s_re", 0, 3)
        turn("re", 0, 3)
        round_h(0, 3)
        turn("im", 1, 1)
        quantise_weight("wa", 1, 1)
        for j in range(3):
            product_pass("s_re", 1, j, 1)
        product("s_re", 1, 3)
        pick_gains(0)
        for pair, later in zip(PAIRS, PAIRS[1]):
            turn("im", 1, later)
            for j in pair:
                multiply("s_re", 1, j)
                turn("re", 1, j)
                round_h(1, j)
        for c in range(2):
            quantise_h(0, c)

        ahead, opened = range(3), range(TILES)
        for n in opened:
            y_pass(n, 0)
        pick_gains(1)
        for c in range(2):
            quantise_h(1, c)
        pick_gains(2)
        for n in range(OUT_TILES):
            if n not in opened:
                y_pass(n, 0)
            y_pass(n, 1)
            if n in ahead:
                scale_from_psum(n)
            else:
                keep_y(n)
        for n in range(len(ahead), OUT_TILES - 1):
            gather_scale_store(n, slice(0, S))
        for entries in (slice(0, 256), slice(256, 448), slice(448, S)):
            gather_scale_store(OUT_TILES - 1, entries)
